import numpy as np
import ml_dtypes


def mxq(x, axis, fmt="e4m3"):
    dtype, down = {"e4m3": (ml_dtypes.float8_e4m3fn, 7), "e5m2": (ml_dtypes.float8_e5m2, 14)}[fmt]
    v = np.moveaxis(np.asarray(x, np.float32).astype(ml_dtypes.bfloat16).astype(np.float64), axis, -1)
    blocks = v.reshape(v.shape[:-1] + (-1, 32))
    amax = np.abs(blocks).max(-1, keepdims=True)
    byte = np.maximum(np.where(amax > 0, np.frexp(amax)[1] - 1 + 127, 0) - down, 1)
    scale = np.exp2(byte - 127.0)
    codes = (blocks / scale).astype(np.float32).astype(dtype).astype(np.float64)
    return np.moveaxis((codes * scale).reshape(v.shape), -1, axis)


WIDE = False


def mx_kscale(k):
    if not WIDE:
        return np.ones(k)
    levels = np.array([10, -10, 5, -5, 0])
    if k % 512:
        return np.exp2(np.random.permutation(np.resize(levels, k // 32))).repeat(32)
    a = np.empty((k // 512, 16))
    for p in range(k // 512):
        a[p, :8] = np.random.permutation(np.resize(levels, 8))
        for g in range(8):
            far = levels[np.abs(levels - a[p, g]) >= 10]
            a[p, g + 8] = far[np.random.randint(len(far))]
    return np.exp2(a.ravel()).repeat(32)


BF16 = ml_dtypes.bfloat16


def bf(x):
    return np.asarray(x, np.float32).astype(BF16)


def f64(x):
    return np.asarray(x).astype(np.float64)


E2M1 = np.array([0.0, 0.5, 1.0, 1.5, 2.0, 3.0, 4.0, 6.0, -0.0, -0.5, -1.0, -1.5, -2.0, -3.0, -4.0, -6.0])


def pack_weight(w, fmt):
    k, n = w.shape
    w = f64(bf(w)).reshape(k // 32, 32, n)
    amax = np.abs(w).max(1)
    if fmt == "e4m3":
        byte = np.frexp(amax)[1] - 1 + 127 - 7
    else:
        mant, ex = np.frexp(amax / 6.0)
        byte = np.where(mant > 0.5, ex, ex - 1) + 127
    byte = np.clip(np.where(amax > 0, byte, 1), 1, 254)
    scaled = (w * np.exp2(127.0 - byte)[:, None, :]).reshape(k, n).astype(np.float32)
    by_word = np.ascontiguousarray(scaled.reshape(k // 512, 128, 4, n).transpose(0, 1, 3, 2))
    if fmt == "e4m3":
        words = by_word.astype(ml_dtypes.float8_e4m3fn).view(np.uint8)
    else:
        c = by_word.astype(ml_dtypes.float4_e2m1fn).view(np.uint8) & 0xF
        words = c[..., 0::2] | (c[..., 1::2] << 4)
    return np.ascontiguousarray(words), np.ascontiguousarray(byte.astype(np.uint8).reshape(k // 512, 16, n))


def unpack_weight(words, scales, fmt):
    g, p, n, _ = words.shape
    if fmt == "e4m3":
        vals = np.ascontiguousarray(words).view(ml_dtypes.float8_e4m3fn).astype(np.float64)
    else:
        nib = np.empty((g, p, n, 4), np.uint8)
        nib[..., 0::2] = words & 0xF
        nib[..., 1::2] = words >> 4
        vals = E2M1[nib]
    vals = vals * np.repeat(np.exp2(scales.astype(np.float64) - 127.0), 8, axis=1)[..., None]
    return vals.transpose(0, 1, 3, 2).reshape(g * 512, n)
def pack4(w):
    words, scales = pack_weight(w, "e2m1")
    return words.reshape(words.shape[0], 128, -1), scales


def unpack4(words, scales):
    return unpack_weight(words.reshape(words.shape[0], 128, -1, 2), scales, "e2m1")


def planes(Y):
    n, m = Y.shape
    b = f64(bf(Y)).reshape(n // 32, 32, m)
    amax = np.abs(b).max(1)
    byte = np.clip(np.where(amax > 0, np.frexp(amax)[1] - 1 + 127 - 7, 1), 1, 254)
    codes = (b * np.exp2(127.0 - byte)[:, None, :]).reshape(n, m).astype(np.float32).astype(ml_dtypes.float8_e4m3fn).view(np.uint8)
    words = codes.reshape(n // 512, 128, 4, m).transpose(0, 1, 3, 2)
    return np.ascontiguousarray(words), np.ascontiguousarray(byte.astype(np.uint8).reshape(n // 512, 16, m))


T, D, N, Q = 1024, 1024, 1024, 1024


def setup_inputs():
    s, t = mx_kscale(D), mx_kscale(T)
    z = bf(np.random.standard_normal((T, D)) * s)
    wo_words, wo_scales = pack4(np.random.standard_normal((D, N)) / np.sqrt(D) / s[:, None])
    wg_words, wg_scales = pack4(np.random.standard_normal((D, Q)) / np.sqrt(D) / s[:, None])
    return {"z": z,
            "wo_words": wo_words,
            "wo_scales": wo_scales,
            "wg_words": wg_words,
            "wg_scales": wg_scales,
            "bg": bf(np.random.standard_normal(Q) * 0.5),
            "r": bf(np.random.standard_normal((T, N))),
            "v": bf((1.0 + 0.1 * np.random.standard_normal(T)) * t),
            "u": bf((1.0 + 0.1 * np.random.standard_normal(T)) / t)}


def stochastic_discount_factor(zq, wo, r):
    om = zq @ wo
    return 1.0 - (1.0 / np.sqrt(N)) * np.sum(om * r, axis=1)


def weighted_test_functions(zq, wg, bg, u):
    return u[:, None] * np.tanh((zq @ wg) + bg[None, :])


def core(z, wo_words, wo_scales, wg_words, wg_scales, bg, r, v, u):
    rr = f64(r)
    zq = mxq(f64(z), 1, "e4m3")
    sdf = stochastic_discount_factor(zq, unpack4(wo_words, wo_scales), rr)
    f = weighted_test_functions(zq, unpack4(wg_words, wg_scales), f64(bg), f64(u))
    d = (f64(v) * sdf)[:, None] * rr
    return (1.0 / np.sqrt(T)) * (mxq(d, 0, "e4m3").T @ mxq(f, 0, "e4m3"))


def reference(z, wo_words, wo_scales, wg_words, wg_scales, bg, r, v, u):
    R_out = core(z, wo_words, wo_scales, wg_words, wg_scales, bg, r, v, u)
    words, scales = planes(R_out.T)
    return R_out, words, scales

@@ -1,0 +1,496 @@
+from contextlib import ExitStack
+
+import concourse.mybir as mybir
+from concourse.masks import make_identity
+
+F32 = mybir.dt.float32
+BF16 = mybir.dt.bfloat16
+U8 = mybir.dt.uint8
+U32 = mybir.dt.uint32
+I32 = mybir.dt.int32
+E4M3 = mybir.dt.float8_e4m3fn_x4
+E2M1 = mybir.dt.float4_e2m1fn_x4
+ADD = mybir.AluOpType.add
+MULT = mybir.AluOpType.mult
+ACT = mybir.ActivationFunctionType
+
+T, D, N, Q = 1024, 1024, 1024, 1024
+FLOPS = 3 * 2 * 1024 * 1024 * 1024
+
+
+def tile_adversarialsdfconditionalpricingmoments_x2_kernel(
+    tc, z, wo_words, wo_scales, wg_words, wg_scales, bg, r, v, u, out_0, out_1, out_2
+):
+    nc = tc.nc
+    with ExitStack() as ctx:
+        keep = ctx.enter_context(tc.tile_pool(name="keep", bufs=1))
+        work = ctx.enter_context(tc.tile_pool(name="work", bufs=4))
+        psum = ctx.enter_context(tc.psum_pool(name="psum", bufs=4))
+
+        def kt(name, shape, dtype):
+            return keep.tile(shape, dtype, name=name, align_bytes=64)
+
+        ident = kt("ident", [128, 128], F32)
+        z_sb = [kt("z%d" % g, [128, 4, D], BF16) for g in range(2)]
+        r_sb = [kt("r%d" % g, [128, 4, N], BF16) for g in range(2)]
+        w_sb = {k: kt("w" + k, [128, 2, 2 * N], U8) for k in "og"}
+        ws_sb = {k: kt("ws" + k, [128, 2, N], U8) for k in "og"}
+        bg_rows = kt("bg_rows", [128, 128], BF16)
+        bg_t = kt("bg_t", [128, 8], F32)
+        v_sb = kt("v", [128, 2, 4], BF16)
+        u_row = kt("u_row", [128, T], BF16)
+        ones = kt("ones", [128, 128], BF16)
+        u_bc = kt("u_bc", [128, 2, 512], F32)
+        eye = kt("eye", [128, 8], BF16)
+        warm = kt("warm", [128, 1], F32)
+        zero = kt("zero", [128, 512], BF16)
+        zin = [[kt("zin%d%d" % (g, h), [128, 512, 4], BF16) for h in range(2)] for g in range(2)]
+        zc = [[kt("zc%d%d" % (g, h), [128, 512], U32) for h in range(2)] for g in range(2)]
+        zs = [[kt("zs%d%d" % (g, h), [128, 512], U8) for h in range(2)] for g in range(2)]
+        fin = [kt("fin%d" % g, [128, Q, 4], BF16) for g in range(2)]
+        fc = [kt("fc%d" % g, [128, Q], U32) for g in range(2)]
+        fs = [kt("fs%d" % g, [128, Q], U8) for g in range(2)]
+        dsc = [kt("dsc%d" % g, [128, 4, N], BF16) for g in range(2)]
+        din = [kt("din%d" % g, [128, N, 4], BF16) for g in range(2)]
+        dc = [kt("dc%d" % g, [128, N], U32) for g in range(2)]
+        ds = [kt("ds%d" % g, [128, N], U8) for g in range(2)]
+        acc = [kt("acc%d" % g, [128, 4, 2], F32) for g in range(2)]
+        sv = [kt("sv%d" % g, [128, 3, 4], F32) for g in range(2)]
+        pin = [kt("pin%d" % h, [128, N, 4], BF16) for h in range(2)]
+        pc = [kt("pc%d" % h, [128, N], U32) for h in range(2)]
+        ps = [kt("ps%d" % h, [128, N], U8) for h in range(2)]
+
+        nc.vector.memset(zero[:], 0.0)
+        for k in "og":
+            nc.vector.memset(ws_sb[k][:].rearrange("p g n -> p (g n)").bitcast(I32), 0)
+        nc.vector.memset(bg_rows[:], 0.0)
+        nc.vector.memset(warm[:], 0.0)
+        nc.vector.memset(u_row[:], 0.0)
+        nc.vector.memset(ones[:], 1.0)
+        nc.scalar.activation(out=warm[:], in_=warm[:], func=ACT.Tanh)
+
+        def load_z(g, j0, j1):
+            nc.sync.dma_start(
+                out=z_sb[g][:, j0:j1, :],
+                in_=z[512 * g : 512 * (g + 1), :].rearrange("(p j) d -> p j d", j=4)[:, j0:j1, :],
+            )
+
+        def load_scales(eng, k, src):
+            for b in range(4):
+                eng.dma_start(
+                    out=ws_sb[k][32 * b : 32 * b + 4, :, :].bitcast(I32),
+                    in_=src[:, 4 * b : 4 * b + 4, :].rearrange("g q n -> q g n").bitcast(I32),
+                )
+
+        def load_words(k, src, c0, c1):
+            nc.sync.dma_start(
+                out=w_sb[k][:, :, c0:c1].bitcast(I32), in_=src.rearrange("g p n -> p g n")[:, :, c0:c1].bitcast(I32)
+            )
+
+        def load_r(g, j0, j1):
+            nc.sync.dma_start(
+                out=r_sb[g][:, j0:j1, :],
+                in_=r[512 * g : 512 * (g + 1), :].rearrange("(p j) i -> p j i", j=4)[:, j0:j1, :],
+            )
+
+        load_z(0, 0, 2)
+        load_z(0, 2, 4)
+        load_scales(nc.scalar, "o", wo_scales)
+        load_words("o", wo_words, 0, 2 * N)
+        load_r(0, 0, 2)
+        load_r(0, 2, 4)
+        load_words("g", wg_words, 0, 2 * N)
+        load_z(1, 0, 4)
+        load_r(1, 0, 4)
+        make_identity(nc, ident[:])
+        nc.gpsimd.dma_start(out=bg_rows[0:8, :], in_=bg.rearrange("(a p) -> a p", p=128))
+        nc.gpsimd.dma_start(out=v_sb[:], in_=v.rearrange("(g p j) -> p g j", p=128, j=4))
+        nc.gpsimd.dma_start(out=u_row[0:1, :], in_=u.unsqueeze(0))
+        load_scales(nc.gpsimd, "g", wg_scales)
+
+        def bank(tag, shape):
+            return psum.tile(shape, F32, name=tag, tag=tag)
+
+        hold = {}
+
+        def zT(g, h, j0, j1):
+            n = 128 * (j1 - j0)
+            t = bank("tr", [128, 2, n])
+            w = z_sb[g][:].rearrange("p j d -> p (j d)").bitcast(F32).rearrange("p (j w) -> p j w", j=4)
+            for j in range(j0, j1):
+                for e in range(2):
+                    nc.tensor.transpose(
+                        t[:, e, 128 * (j - j0) : 128 * (j - j0 + 1)], w[:, j, 256 * h + e : 256 * (h + 1) : 2], ident[:]
+                    )
+            hold["z", g, h, j0] = t
+
+        def zE(g, h, j0, j1, eng):
+            o = zin[g][h][:, 128 * j0 : 128 * j1, :].rearrange("p c k -> p (c k)").bitcast(F32).rearrange("p (c e) -> p c e", e=2)
+            i = hold["z", g, h, j0][:].rearrange("p e c -> p c e")
+            if eng == "S":
+                nc.scalar.copy(out=o, in_=i)
+            else:
+                nc.vector.tensor_copy(out=o, in_=i)
+
+        def dummy(n):
+            for k in range(n):
+                t = bank("mm", [128, 512])
+                nc.tensor.matmul(t[:], zero[:, 0:128], zero[:], start=True, stop=True)
+
+        def zQ(g, h, c0, c1):
+            nc.vector.quantize_mx(
+                out=zc[g][h][:, c0:c1].bitcast(E4M3),
+                scales=zs[g][h][:, c0:c1],
+                in_=zin[g][h][:, c0:c1, :].rearrange("p c k -> p (c k)"),
+            )
+
+        def bgT():
+            nc.scalar.copy(out=eye[:], in_=ident[:, 0:8])
+            t = bank("tr", [128, 8])
+            nc.tensor.matmul(t[:], bg_rows[:], eye[:], start=True, stop=True)
+            nc.scalar.copy(out=bg_t[:], in_=t[:])
+
+        def wgM(g, qt):
+            t = bank("mm", [128, 512])
+            for h in range(2):
+                nc.tensor.matmul_mx(
+                    out=t[:],
+                    lhsT=w_sb["g"][:, h, 256 * qt : 256 * (qt + 1)].bitcast(E2M1),
+                    lhsT_scale=ws_sb["g"][:, h, 128 * qt : 128 * (qt + 1)],
+                    rhs=zc[g][h][:].bitcast(E4M3),
+                    rhs_scale=zs[g][h][:],
+                    start=h == 0,
+                    stop=h == 1,
+                )
+            hold["x", g, qt] = t
+
+        def tanh(g, qt):
+            t = work.tile([128, 512], F32, name="th", bufs=12)
+            nc.scalar.activation(out=t[:], in_=hold["x", g, qt][:], func=ACT.Tanh, bias=bg_t[:, qt : qt + 1])
+            hold["t", g, qt] = t
+
+        def uB():
+            for g in range(2):
+                t = bank("tr", [128, 512])
+                nc.tensor.matmul(t[:], ones[:], u_row[:, 512 * g : 512 * (g + 1)], start=True, stop=True)
+                nc.scalar.copy(
+                    out=u_bc[:, g, :].rearrange("p (w c e) -> p w c e", w=2, e=2),
+                    in_=t[:].rearrange("p (c w e) -> p w c e", w=2, e=2),
+                )
+
+        def fU(g, qt, eng="V"):
+            t = work.tile([128, 512], BF16, name="fb", bufs=8)
+            (nc.vector if eng == "V" else nc.gpsimd).tensor_tensor(
+                out=t[:].rearrange("p (w c e) -> p w c e", w=2, e=2),
+                in0=hold["t", g, qt][:].rearrange("p (w e c) -> p w c e", w=2, e=2),
+                in1=u_bc[:, g, :].rearrange("p (w c e) -> p w c e", w=2, e=2),
+                op=MULT,
+            )
+            hold["b", g, qt] = t
+
+        def fT(g, qp):
+            t = bank("tr", [128, 2, 256])
+            for k in range(2):
+                w = hold["b", g, 2 * qp + k][:].bitcast(F32)
+                for e in range(2):
+                    nc.tensor.transpose(t[:, e, 128 * k : 128 * (k + 1)], w[:, 128 * e : 128 * (e + 1)], ident[:])
+            hold["f", g, qp] = t
+
+        def fE(g, qp, eng="S"):
+            w = fin[g][:].rearrange("p c k -> p (c k)").bitcast(F32).rearrange("p (h j b a e) -> p h j b a e", h=2, j=4, b=2, a=64)
+            o = w[:, qp // 2, :, qp % 2, :, :]
+            i = hold["f", g, qp][:].rearrange("p e (a j) -> p j a e", j=4)
+            if eng == "S":
+                nc.scalar.copy(out=o, in_=i)
+            else:
+                nc.vector.tensor_copy(out=o, in_=i)
+
+        def fQ(g, h):
+            c = slice(512 * h, 512 * (h + 1))
+            nc.vector.quantize_mx(
+                out=fc[g][:, c].bitcast(E4M3), scales=fs[g][:, c], in_=fin[g][:, c, :].rearrange("p c k -> p (c k)")
+            )
+
+        def omM(g, j, nh):
+            t = bank("mm", [128, 512])
+            for h in range(2):
+                nc.tensor.matmul_mx(
+                    out=t[:],
+                    lhsT=zc[g][h][:, 128 * j : 128 * (j + 1)].bitcast(E4M3),
+                    lhsT_scale=zs[g][h][:, 128 * j : 128 * (j + 1)],
+                    rhs=w_sb["o"][:, h, 1024 * nh : 1024 * (nh + 1)].bitcast(E2M1),
+                    rhs_scale=ws_sb["o"][:, h, 512 * nh : 512 * (nh + 1)],
+                    start=h == 0,
+                    stop=h == 1,
+                )
+            hold["o", g, j, nh] = t
+
+        def omR(g, j, nh):
+            junk = work.tile([128, 512], F32, name="junk", bufs=2)
+            nc.vector.scalar_tensor_tensor(
+                out=junk[:],
+                in0=hold["o", g, j, nh][:],
+                scalar=1.0,
+                in1=r_sb[g][:, j, 512 * nh : 512 * (nh + 1)],
+                op0=MULT,
+                op1=MULT,
+                accum_out=acc[g][:, j, nh : nh + 1],
+            )
+
+        def sd(g):
+            a, b, c = (sv[g][:, k, :] for k in range(3))
+            nc.vector.tensor_tensor(out=a, in0=acc[g][:, :, 0], in1=acc[g][:, :, 1], op=ADD)
+            nc.vector.tensor_scalar(out=b, in0=a, scalar1=-1.0 / 32, scalar2=1.0, op0=MULT, op1=ADD)
+            nc.vector.tensor_tensor(out=c, in0=b, in1=v_sb[:, g, :], op=MULT)
+
+        def dS(g, j, eng="V"):
+            a = dict(out=dsc[g][:, j, :], in0=r_sb[g][:, j, :], scalar1=sv[g][:, 2, j : j + 1], op0=MULT)
+            if eng == "V":
+                nc.vector.tensor_scalar(scalar2=None, **a)
+            else:
+                nc.gpsimd.tensor_scalar(scalar2=0.0, op1=ADD, **a)
+
+        def dI(g, c0, c1, eng="S"):
+            o, i = din[g][:, c0:c1, :], dsc[g][:, :, c0:c1].rearrange("p j c -> p c j")
+            if eng == "S":
+                nc.scalar.copy(out=o, in_=i)
+            else:
+                nc.vector.tensor_copy(out=o, in_=i)
+
+        def dQ(g, c0, c1):
+            nc.vector.quantize_mx(
+                out=dc[g][:, c0:c1].bitcast(E4M3), scales=ds[g][:, c0:c1], in_=din[g][:, c0:c1, :].rearrange("p c k -> p (c k)")
+            )
+
+        def outM(h, it):
+            t = bank("mm", [128, 512])
+            for g in range(2):
+                nc.tensor.matmul_mx(
+                    out=t[:],
+                    lhsT=dc[g][:, 128 * it : 128 * (it + 1)].bitcast(E4M3),
+                    lhsT_scale=ds[g][:, 128 * it : 128 * (it + 1)],
+                    rhs=fc[g][:, 512 * h : 512 * (h + 1)].bitcast(E4M3),
+                    rhs_scale=fs[g][:, 512 * h : 512 * (h + 1)],
+                    start=g == 0,
+                    stop=g == 1,
+                )
+            hold["out", h, it] = t
+
+        def outE(h, it, eng="S"):
+            t = work.tile([128, 512], F32, name="osb", bufs=8)
+            o = t[:].rearrange("p (c j) -> p c j", j=4)
+            i = hold["out", h, it][:].rearrange("p (j c) -> p c j", j=4)
+            if eng == "S":
+                nc.scalar.mul(out=o, in_=i, mul=1.0 / 32)
+            else:
+                nc.vector.tensor_scalar(out=o, in0=i, scalar1=1.0 / 32, scalar2=None, op0=MULT)
+            nc.sync.dma_start(out=out_0[128 * it : 128 * (it + 1), 512 * h : 512 * (h + 1)], in_=t[:])
+            hold["os", h, it] = t
+
+        def pB(h, it, eng="V"):
+            t = work.tile([128, 512], BF16, name="ob", bufs=8)
+            o = t[:].rearrange("p (w c e) -> p w c e", w=2, e=2)
+            i = hold["os", h, it][:].rearrange("p (c w e) -> p w c e", w=2, e=2)
+            if eng == "V":
+                nc.vector.tensor_copy(out=o, in_=i)
+            else:
+                nc.gpsimd.tensor_scalar(out=o, in0=i, scalar1=1.0, scalar2=0.0, op0=MULT, op1=ADD)
+            hold["ob", h, it] = t
+
+        def pT(h, ip):
+            t = bank("tr", [128, 2, 256])
+            for k in range(2):
+                w = hold["ob", h, 2 * ip + k][:].bitcast(F32)
+                for e in range(2):
+                    nc.tensor.transpose(t[:, e, 128 * k : 128 * (k + 1)], w[:, 128 * e : 128 * (e + 1)], ident[:])
+            hold["pt", h, ip] = t
+
+        def pE(h, ip, eng):
+            c = slice(256 * ip, 256 * (ip + 1))
+            o = pin[h][:, c, :].rearrange("p c k -> p (c k)").bitcast(F32).rearrange("p (c e) -> p c e", e=2)
+            i = hold["pt", h, ip][:].rearrange("p e c -> p c e")
+            if eng == "S":
+                nc.scalar.copy(out=o, in_=i)
+            else:
+                nc.vector.tensor_copy(out=o, in_=i)
+
+        def pM(h, it):
+            t = bank("tr", [128, 4, 128])
+            for j in range(4):
+                c = slice(512 * h + 128 * j, 512 * h + 128 * (j + 1))
+                for g in range(2):
+                    nc.tensor.matmul_mx(
+                        out=t[:, j, :],
+                        lhsT=fc[g][:, c].bitcast(E4M3),
+                        lhsT_scale=fs[g][:, c],
+                        rhs=dc[g][:, 128 * it : 128 * (it + 1)].bitcast(E4M3),
+                        rhs_scale=ds[g][:, 128 * it : 128 * (it + 1)],
+                        start=g == 0,
+                        stop=g == 1,
+                    )
+            hold["pm", h, it] = t
+
+        def pD(h, it, eng):
+            o = pin[h][:, 128 * it : 128 * (it + 1), :]
+            i = hold["pm", h, it][:].rearrange("p j c -> p c j")
+            if eng == "S":
+                nc.scalar.mul(out=o, in_=i, mul=1.0 / 32)
+            else:
+                nc.vector.tensor_scalar(out=o, in0=i, scalar1=1.0 / 32, scalar2=None, op0=MULT)
+
+        def pQ(h, c0, c1):
+            nc.vector.quantize_mx(
+                out=pc[h][:, c0:c1].bitcast(E4M3), scales=ps[h][:, c0:c1], in_=pin[h][:, c0:c1, :].rearrange("p c k -> p (c k)")
+            )
+
+        def pW(h, c0, c1):
+            nc.sync.dma_start(
+                out=out_1[h].rearrange("p m t -> p (m t)")[:, 4 * c0 : 4 * c1].bitcast(I32), in_=pc[h][:, c0:c1].bitcast(I32)
+            )
+
+        def pS(h, eng=None):
+            for b in range(4):
+                (eng or nc.sync).dma_start(
+                    out=out_2[h, 4 * b : 4 * b + 4, :].bitcast(I32), in_=ps[h][32 * b : 32 * b + 4, :].bitcast(I32)
+                )
+
+
+        dummy(7)
+        for j in (0, 2):
+            for h in range(2):
+                zT(0, h, j, j + 2)
+                zE(0, h, j, j + 2, "SV"[h])
+            for h in range(2):
+                zQ(0, h, 128 * j, 128 * (j + 2))
+            if j == 2:
+                dummy(2)
+        om = [(j, nh) for j in range(4) for nh in range(2)]
+        for k in range(8):
+            omM(0, *om[k])
+            omR(0, *om[k])
+            if k == 3:
+                bgT()
+                uB()
+        for q in range(4):
+            wgM(0, q)
+            tanh(0, q)
+        sd(0)
+        fU(0, 0)
+        fU(0, 1)
+        for j in range(4):
+            dS(0, j)
+        for j in (0, 2):
+            for h in range(2):
+                zT(1, h, j, j + 2)
+                zE(1, h, j, j + 2, "S")
+            for h in range(2):
+                zQ(1, h, 128 * j, 128 * (j + 2))
+        fU(0, 2)
+        fU(0, 3)
+        for k in range(4):
+            for i in (2 * k, 2 * k + 1):
+                omM(1, *om[i])
+                omR(1, *om[i])
+            wgM(1, k)
+            tanh(1, k)
+            if k:
+                fU(1, k - 1)
+            dI(0, 256 * k, 256 * (k + 1))
+            if k == 1:
+                fT(0, 0)
+                fT(0, 1)
+                fE(0, 0)
+                fE(0, 1)
+        sd(1)
+        fU(1, 3)
+        for j in range(4):
+            dS(1, j)
+        for q in range(4, 6):
+            wgM(0, q)
+            tanh(0, q)
+        dI(1, 0, 256)
+        fT(1, 0)
+        fT(1, 1)
+        dI(1, 256, 512, "V")
+        fE(1, 0, "V")
+        fE(1, 1)
+        fQ(0, 0)
+        dQ(0, 0, 512)
+        dQ(1, 256, 512)
+        dQ(1, 0, 256)
+        fQ(1, 0)
+        for q in range(6, 8):
+            wgM(0, q)
+            tanh(0, q)
+        dI(1, 512, 768)
+        for q in range(4, 6):
+            wgM(1, q)
+            tanh(1, q)
+        for q in range(4, 8):
+            fU(0, q)
+        for it in range(4):
+            outM(0, it)
+            outE(0, it, "S")
+        dQ(0, 512, 1024)
+        dI(1, 768, 1024, "V")
+        dQ(1, 512, 1024)
+        for q in range(6, 8):
+            wgM(1, q)
+            tanh(1, q)
+        fT(0, 2)
+        fT(0, 3)
+        fE(0, 2, "V")
+        fE(0, 3)
+        for q in range(4, 8):
+            fU(1, q)
+        for it in range(4, 8):
+            outM(0, it)
+            outE(0, it, "S")
+        for it in range(4):
+            pB(0, it, "G")
+        fQ(0, 1)
+        fT(1, 2)
+        fT(1, 3)
+        fE(1, 2, "V")
+        fE(1, 3)
+        fQ(1, 1)
+        for ip in range(2):
+            pT(0, ip)
+            pE(0, ip, "S")
+        for it in range(4, 8):
+            pB(0, it, "G")
+        for it in range(4):
+            outM(1, it)
+            outE(1, it, "S")
+        pQ(0, 0, 512)
+        pW(0, 0, 512)
+        for ip in range(2, 4):
+            pT(0, ip)
+            pE(0, ip, "SV"[ip % 2])
+        pQ(0, 512, 1024)
+        pW(0, 512, 1024)
+        pS(0)
+        for it in range(4):
+            pB(1, it, "GV"[it % 2])
+        for it in range(6, 8):
+            pM(1, it)
+            pD(1, it, "SV"[it % 2])
+        for it in range(4, 6):
+            outM(1, it)
+            outE(1, it, "S")
+            pB(1, it, "V")
+        pQ(1, 768, 1024)
+        for ip in range(2):
+            pT(1, ip)
+            pE(1, ip, "VS"[ip])
+        pQ(1, 0, 512)
+        pW(1, 0, 512)
+        for it in range(6, 8):
+            outM(1, it)
+            outE(1, it, "S")
+            if it == 6:
+                pT(1, 2)
+                pE(1, 2, "V")
+        pQ(1, 512, 768)
+        pW(1, 512, 1024)
+        pS(1)

@@ -15,6 +15,8 @@ MULT = mybir.AluOpType.mult
 ACT = mybir.ActivationFunctionType
 
 T, D, N, Q = 1024, 1024, 1024, 1024
+THB, OSB = 12, 12
+DI0, PB = "S", "S"
 FLOPS = 3 * 2 * 1024 * 1024 * 1024
 
 
@@ -25,26 +27,23 @@ def tile_adversarialsdfconditionalpricingmoments_x2_kernel(
     with ExitStack() as ctx:
         keep = ctx.enter_context(tc.tile_pool(name="keep", bufs=1))
         work = ctx.enter_context(tc.tile_pool(name="work", bufs=4))
-        psum = ctx.enter_context(tc.psum_pool(name="psum", bufs=4))
+        psum = ctx.enter_context(tc.psum_pool(name="psum", bufs=8))
+        ctx.enter_context(tc.manual_schedule())
 
         def kt(name, shape, dtype):
             return keep.tile(shape, dtype, name=name, align_bytes=64)
 
         ident = kt("ident", [128, 128], F32)
-        z_sb = [kt("z%d" % g, [128, 4, D], BF16) for g in range(2)]
-        r_sb = [kt("r%d" % g, [128, 4, N], BF16) for g in range(2)]
-        w_sb = {k: kt("w" + k, [128, 2, 2 * N], U8) for k in "og"}
+        z_sb, r_sb = {}, {}
+        w_sb = {(k, a): kt("w%s%d" % (k, a), [128, 2, 1024], U8) for k in "og" for a in range(2)}
         ws_sb = {k: kt("ws" + k, [128, 2, N], U8) for k in "og"}
         bg_rows = kt("bg_rows", [128, 128], BF16)
         bg_t = kt("bg_t", [128, 8], F32)
         v_sb = kt("v", [128, 2, 4], BF16)
-        u_row = kt("u_row", [128, T], BF16)
-        ones = kt("ones", [128, 128], BF16)
-        u_bc = kt("u_bc", [128, 2, 512], F32)
+        nv = kt("nv", [128, 2, 4], F32)
+        u_sb = kt("u", [128, 2, 4], BF16)
         eye = kt("eye", [128, 8], BF16)
-        warm = kt("warm", [128, 1], F32)
-        zero = kt("zero", [128, 512], BF16)
-        zin = [[kt("zin%d%d" % (g, h), [128, 512, 4], BF16) for h in range(2)] for g in range(2)]
+        zin = [[kt("zin%d%d" % (g, a), [128, 2, 256, 4], BF16) for a in range(2)] for g in range(2)]
         zc = [[kt("zc%d%d" % (g, h), [128, 512], U32) for h in range(2)] for g in range(2)]
         zs = [[kt("zs%d%d" % (g, h), [128, 512], U8) for h in range(2)] for g in range(2)]
         fin = [kt("fin%d" % g, [128, Q, 4], BF16) for g in range(2)]
@@ -55,25 +54,32 @@ def tile_adversarialsdfconditionalpricingmoments_x2_kernel(
         dc = [kt("dc%d" % g, [128, N], U32) for g in range(2)]
         ds = [kt("ds%d" % g, [128, N], U8) for g in range(2)]
         acc = [kt("acc%d" % g, [128, 4, 2], F32) for g in range(2)]
-        sv = [kt("sv%d" % g, [128, 3, 4], F32) for g in range(2)]
+        sm = [kt("sm%d" % g, [128, 4], F32) for g in range(2)]
+        ob = [[kt("ob%d%d" % (h, ip), [128, 2, 512], BF16) for ip in range(4)] for h in range(2)]
         pin = [kt("pin%d" % h, [128, N, 4], BF16) for h in range(2)]
         pc = [kt("pc%d" % h, [128, N], U32) for h in range(2)]
         ps = [kt("ps%d" % h, [128, N], U8) for h in range(2)]
+        hold = {}
 
-        nc.vector.memset(zero[:], 0.0)
-        for k in "og":
-            nc.vector.memset(ws_sb[k][:].rearrange("p g n -> p (g n)").bitcast(I32), 0)
-        nc.vector.memset(bg_rows[:], 0.0)
-        nc.vector.memset(warm[:], 0.0)
-        nc.vector.memset(u_row[:], 0.0)
-        nc.vector.memset(ones[:], 1.0)
-        nc.scalar.activation(out=warm[:], in_=warm[:], func=ACT.Tanh)
+        def copy(eng, o, i):
+            if eng == "S":
+                nc.scalar.copy(out=o, in_=i)
+            elif eng == "V":
+                nc.vector.tensor_copy(out=o, in_=i)
+            else:
+                nc.gpsimd.tensor_scalar(out=o, in0=i, scalar1=1.0, scalar2=0.0, op0=MULT, op1=ADD)
+
+        def load_rows(tiles, name, src, g, j0, j1):
+            t = kt("%s%d%d" % (name, g, j0), [128, j1 - j0, 1024], BF16)
+            nc.sync.dma_start(out=t[:], in_=src[512 * g : 512 * (g + 1), :].rearrange("(p j) d -> p j d", j=4)[:, j0:j1, :])
+            for j in range(j0, j1):
+                tiles[g, j] = t[:, j - j0, :]
 
         def load_z(g, j0, j1):
-            nc.sync.dma_start(
-                out=z_sb[g][:, j0:j1, :],
-                in_=z[512 * g : 512 * (g + 1), :].rearrange("(p j) d -> p j d", j=4)[:, j0:j1, :],
-            )
+            load_rows(z_sb, "z", z, g, j0, j1)
+
+        def load_r(g, j0, j1):
+            load_rows(r_sb, "r", r, g, j0, j1)
 
         def load_scales(eng, k, src):
             for b in range(4):
@@ -82,143 +88,48 @@ def tile_adversarialsdfconditionalpricingmoments_x2_kernel(
                     in_=src[:, 4 * b : 4 * b + 4, :].rearrange("g q n -> q g n").bitcast(I32),
                 )
 
-        def load_words(k, src, c0, c1):
+        def load_words(k, src, a):
             nc.sync.dma_start(
-                out=w_sb[k][:, :, c0:c1].bitcast(I32), in_=src.rearrange("g p n -> p g n")[:, :, c0:c1].bitcast(I32)
+                out=w_sb[k, a][:].bitcast(I32), in_=src.rearrange("g p n -> p g n")[:, :, 1024 * a : 1024 * (a + 1)].bitcast(I32)
             )
 
-        def load_r(g, j0, j1):
-            nc.sync.dma_start(
-                out=r_sb[g][:, j0:j1, :],
-                in_=r[512 * g : 512 * (g + 1), :].rearrange("(p j) i -> p j i", j=4)[:, j0:j1, :],
-            )
+        def bank(shape):
+            return psum.tile(shape, F32, name="bank", tag="bank")
 
-        load_z(0, 0, 2)
-        load_z(0, 2, 4)
-        load_scales(nc.scalar, "o", wo_scales)
-        load_words("o", wo_words, 0, 2 * N)
-        load_r(0, 0, 2)
-        load_r(0, 2, 4)
-        load_words("g", wg_words, 0, 2 * N)
-        load_z(1, 0, 4)
-        load_r(1, 0, 4)
-        make_identity(nc, ident[:])
-        nc.gpsimd.dma_start(out=bg_rows[0:8, :], in_=bg.rearrange("(a p) -> a p", p=128))
-        nc.gpsimd.dma_start(out=v_sb[:], in_=v.rearrange("(g p j) -> p g j", p=128, j=4))
-        nc.gpsimd.dma_start(out=u_row[0:1, :], in_=u.unsqueeze(0))
-        load_scales(nc.gpsimd, "g", wg_scales)
-
-        def bank(tag, shape):
-            return psum.tile(shape, F32, name=tag, tag=tag)
-
-        hold = {}
-
-        def zT(g, h, j0, j1):
-            n = 128 * (j1 - j0)
-            t = bank("tr", [128, 2, n])
-            w = z_sb[g][:].rearrange("p j d -> p (j d)").bitcast(F32).rearrange("p (j w) -> p j w", j=4)
-            for j in range(j0, j1):
+        def zT(g, j):
+            t = bank([128, 2, 2, 128])
+            w = z_sb[g, j].bitcast(F32)
+            for h in range(2):
                 for e in range(2):
-                    nc.tensor.transpose(
-                        t[:, e, 128 * (j - j0) : 128 * (j - j0 + 1)], w[:, j, 256 * h + e : 256 * (h + 1) : 2], ident[:]
-                    )
-            hold["z", g, h, j0] = t
+                    nc.tensor.transpose(t[:, h, e, :], w[:, 256 * h + e : 256 * (h + 1) : 2], ident[:])
+            hold["z", g, j] = t
 
-        def zE(g, h, j0, j1, eng):
-            o = zin[g][h][:, 128 * j0 : 128 * j1, :].rearrange("p c k -> p (c k)").bitcast(F32).rearrange("p (c e) -> p c e", e=2)
-            i = hold["z", g, h, j0][:].rearrange("p e c -> p c e")
-            if eng == "S":
-                nc.scalar.copy(out=o, in_=i)
-            else:
-                nc.vector.tensor_copy(out=o, in_=i)
+        def zE(g, j, eng="S"):
+            w = zin[g][j // 2][:].rearrange("p h c k -> p (h c k)").bitcast(F32).rearrange("p (h a c e) -> p h a c e", h=2, a=2, e=2)
+            copy(eng, w[:, :, j % 2, :, :], hold["z", g, j][:].rearrange("p h e c -> p h c e"))
 
-        def dummy(n):
-            for k in range(n):
-                t = bank("mm", [128, 512])
-                nc.tensor.matmul(t[:], zero[:, 0:128], zero[:], start=True, stop=True)
-
-        def zQ(g, h, c0, c1):
+        def zQ(g, h, j0, j1):
+            c = slice(128 * j0, 128 * j1)
             nc.vector.quantize_mx(
-                out=zc[g][h][:, c0:c1].bitcast(E4M3),
-                scales=zs[g][h][:, c0:c1],
-                in_=zin[g][h][:, c0:c1, :].rearrange("p c k -> p (c k)"),
+                out=zc[g][h][:, c].bitcast(E4M3),
+                scales=zs[g][h][:, c],
+                in_=zin[g][j0 // 2][:, h, 128 * (j0 % 2) : 128 * (j0 % 2 + j1 - j0), :].rearrange("p c k -> p (c k)"),
             )
 
         def bgT():
             nc.scalar.copy(out=eye[:], in_=ident[:, 0:8])
-            t = bank("tr", [128, 8])
+            t = bank([128, 8])
             nc.tensor.matmul(t[:], bg_rows[:], eye[:], start=True, stop=True)
             nc.scalar.copy(out=bg_t[:], in_=t[:])
 
-        def wgM(g, qt):
-            t = bank("mm", [128, 512])
-            for h in range(2):
-                nc.tensor.matmul_mx(
-                    out=t[:],
-                    lhsT=w_sb["g"][:, h, 256 * qt : 256 * (qt + 1)].bitcast(E2M1),
-                    lhsT_scale=ws_sb["g"][:, h, 128 * qt : 128 * (qt + 1)],
-                    rhs=zc[g][h][:].bitcast(E4M3),
-                    rhs_scale=zs[g][h][:],
-                    start=h == 0,
-                    stop=h == 1,
-                )
-            hold["x", g, qt] = t
-
-        def tanh(g, qt):
-            t = work.tile([128, 512], F32, name="th", bufs=12)
-            nc.scalar.activation(out=t[:], in_=hold["x", g, qt][:], func=ACT.Tanh, bias=bg_t[:, qt : qt + 1])
-            hold["t", g, qt] = t
-
-        def uB():
-            for g in range(2):
-                t = bank("tr", [128, 512])
-                nc.tensor.matmul(t[:], ones[:], u_row[:, 512 * g : 512 * (g + 1)], start=True, stop=True)
-                nc.scalar.copy(
-                    out=u_bc[:, g, :].rearrange("p (w c e) -> p w c e", w=2, e=2),
-                    in_=t[:].rearrange("p (c w e) -> p w c e", w=2, e=2),
-                )
-
-        def fU(g, qt, eng="V"):
-            t = work.tile([128, 512], BF16, name="fb", bufs=8)
-            (nc.vector if eng == "V" else nc.gpsimd).tensor_tensor(
-                out=t[:].rearrange("p (w c e) -> p w c e", w=2, e=2),
-                in0=hold["t", g, qt][:].rearrange("p (w e c) -> p w c e", w=2, e=2),
-                in1=u_bc[:, g, :].rearrange("p (w c e) -> p w c e", w=2, e=2),
-                op=MULT,
-            )
-            hold["b", g, qt] = t
-
-        def fT(g, qp):
-            t = bank("tr", [128, 2, 256])
-            for k in range(2):
-                w = hold["b", g, 2 * qp + k][:].bitcast(F32)
-                for e in range(2):
-                    nc.tensor.transpose(t[:, e, 128 * k : 128 * (k + 1)], w[:, 128 * e : 128 * (e + 1)], ident[:])
-            hold["f", g, qp] = t
-
-        def fE(g, qp, eng="S"):
-            w = fin[g][:].rearrange("p c k -> p (c k)").bitcast(F32).rearrange("p (h j b a e) -> p h j b a e", h=2, j=4, b=2, a=64)
-            o = w[:, qp // 2, :, qp % 2, :, :]
-            i = hold["f", g, qp][:].rearrange("p e (a j) -> p j a e", j=4)
-            if eng == "S":
-                nc.scalar.copy(out=o, in_=i)
-            else:
-                nc.vector.tensor_copy(out=o, in_=i)
-
-        def fQ(g, h):
-            c = slice(512 * h, 512 * (h + 1))
-            nc.vector.quantize_mx(
-                out=fc[g][:, c].bitcast(E4M3), scales=fs[g][:, c], in_=fin[g][:, c, :].rearrange("p c k -> p (c k)")
-            )
-
         def omM(g, j, nh):
-            t = bank("mm", [128, 512])
+            t = bank([128, 512])
             for h in range(2):
                 nc.tensor.matmul_mx(
                     out=t[:],
                     lhsT=zc[g][h][:, 128 * j : 128 * (j + 1)].bitcast(E4M3),
                     lhsT_scale=zs[g][h][:, 128 * j : 128 * (j + 1)],
-                    rhs=w_sb["o"][:, h, 1024 * nh : 1024 * (nh + 1)].bitcast(E2M1),
+                    rhs=w_sb["o", nh][:, h, :].bitcast(E2M1),
                     rhs_scale=ws_sb["o"][:, h, 512 * nh : 512 * (nh + 1)],
                     start=h == 0,
                     stop=h == 1,
@@ -231,112 +142,121 @@ def tile_adversarialsdfconditionalpricingmoments_x2_kernel(
                 out=junk[:],
                 in0=hold["o", g, j, nh][:],
                 scalar=1.0,
-                in1=r_sb[g][:, j, 512 * nh : 512 * (nh + 1)],
+                in1=r_sb[g, j][:, 512 * nh : 512 * (nh + 1)],
                 op0=MULT,
                 op1=MULT,
                 accum_out=acc[g][:, j, nh : nh + 1],
             )
 
-        def sd(g):
-            a, b, c = (sv[g][:, k, :] for k in range(3))
-            nc.vector.tensor_tensor(out=a, in0=acc[g][:, :, 0], in1=acc[g][:, :, 1], op=ADD)
-            nc.vector.tensor_scalar(out=b, in0=a, scalar1=-1.0 / 32, scalar2=1.0, op0=MULT, op1=ADD)
-            nc.vector.tensor_tensor(out=c, in0=b, in1=v_sb[:, g, :], op=MULT)
+        def sd(g, j0, j1):
+            nc.vector.scalar_tensor_tensor(
+                out=sm[g][:, j0:j1], in0=acc[g][:, j0:j1, 0], scalar=-32.0, in1=acc[g][:, j0:j1, 1], op0=ADD, op1=ADD
+            )
 
-        def dS(g, j, eng="V"):
-            a = dict(out=dsc[g][:, j, :], in0=r_sb[g][:, j, :], scalar1=sv[g][:, 2, j : j + 1], op0=MULT)
-            if eng == "V":
-                nc.vector.tensor_scalar(scalar2=None, **a)
-            else:
-                nc.gpsimd.tensor_scalar(scalar2=0.0, op1=ADD, **a)
+        def dS(g, j, c0=0, c1=N):
+            nc.vector.tensor_scalar(
+                out=dsc[g][:, j, c0:c1],
+                in0=r_sb[g, j][:, c0:c1],
+                scalar1=sm[g][:, j : j + 1],
+                scalar2=nv[:, g, j : j + 1],
+                op0=MULT,
+                op1=MULT,
+            )
 
         def dI(g, c0, c1, eng="S"):
-            o, i = din[g][:, c0:c1, :], dsc[g][:, :, c0:c1].rearrange("p j c -> p c j")
-            if eng == "S":
-                nc.scalar.copy(out=o, in_=i)
-            else:
-                nc.vector.tensor_copy(out=o, in_=i)
+            copy(eng, din[g][:, c0:c1, :], dsc[g][:, :, c0:c1].rearrange("p j c -> p c j"))
 
         def dQ(g, c0, c1):
             nc.vector.quantize_mx(
                 out=dc[g][:, c0:c1].bitcast(E4M3), scales=ds[g][:, c0:c1], in_=din[g][:, c0:c1, :].rearrange("p c k -> p (c k)")
             )
 
+        def wgM(g, qt):
+            t = bank([128, 512])
+            for h in range(2):
+                nc.tensor.matmul_mx(
+                    out=t[:],
+                    lhsT=w_sb["g", qt // 4][:, h, 256 * (qt % 4) : 256 * (qt % 4 + 1)].bitcast(E2M1),
+                    lhsT_scale=ws_sb["g"][:, h, 128 * qt : 128 * (qt + 1)],
+                    rhs=zc[g][h][:].bitcast(E4M3),
+                    rhs_scale=zs[g][h][:],
+                    start=h == 0,
+                    stop=h == 1,
+                )
+            hold["x", g, qt] = t
+
+        def tanh(g, qt):
+            t = work.tile([128, 512], F32, name="th", bufs=THB)
+            nc.scalar.activation(out=t[:], in_=hold["x", g, qt][:], func=ACT.Tanh, bias=bg_t[:, qt : qt + 1])
+            hold["t", g, qt] = t
+
+        def wg(g, qt):
+            wgM(g, qt)
+            tanh(g, qt)
+
+        def fT(g, qt):
+            t = bank([128, 4, 128])
+            for j in range(4):
+                nc.tensor.transpose(t[:, j, :], hold["t", g, qt][:, 128 * j : 128 * (j + 1)], ident[:])
+            hold["f", g, qt] = t
+
+        def fU(g, qt):
+            nc.vector.tensor_tensor(
+                out=fin[g][:, 128 * qt : 128 * (qt + 1), :],
+                in0=hold["f", g, qt][:].rearrange("p j c -> p c j"),
+                in1=u_sb[:, g, :].unsqueeze(1).to_broadcast([128, 128, 4]),
+                op=MULT,
+            )
+
+        def fQ(g, c0, c1):
+            nc.vector.quantize_mx(
+                out=fc[g][:, c0:c1].bitcast(E4M3), scales=fs[g][:, c0:c1], in_=fin[g][:, c0:c1, :].rearrange("p c k -> p (c k)")
+            )
+
         def outM(h, it):
-            t = bank("mm", [128, 512])
+            t = bank([128, 512])
+            i, c = slice(128 * it, 128 * (it + 1)), slice(512 * h, 512 * (h + 1))
             for g in range(2):
                 nc.tensor.matmul_mx(
                     out=t[:],
-                    lhsT=dc[g][:, 128 * it : 128 * (it + 1)].bitcast(E4M3),
-                    lhsT_scale=ds[g][:, 128 * it : 128 * (it + 1)],
-                    rhs=fc[g][:, 512 * h : 512 * (h + 1)].bitcast(E4M3),
-                    rhs_scale=fs[g][:, 512 * h : 512 * (h + 1)],
+                    lhsT=dc[g][:, i].bitcast(E4M3),
+                    lhsT_scale=ds[g][:, i],
+                    rhs=fc[g][:, c].bitcast(E4M3),
+                    rhs_scale=fs[g][:, c],
                     start=g == 0,
                     stop=g == 1,
                 )
             hold["out", h, it] = t
 
         def outE(h, it, eng="S"):
-            t = work.tile([128, 512], F32, name="osb", bufs=8)
-            o = t[:].rearrange("p (c j) -> p c j", j=4)
-            i = hold["out", h, it][:].rearrange("p (j c) -> p c j", j=4)
+            t = work.tile([128, 512], F32, name="osb", bufs=OSB)
             if eng == "S":
-                nc.scalar.mul(out=o, in_=i, mul=1.0 / 32)
+                nc.scalar.mul(out=t[:], in_=hold["out", h, it][:], mul=1.0 / 32)
             else:
-                nc.vector.tensor_scalar(out=o, in0=i, scalar1=1.0 / 32, scalar2=None, op0=MULT)
+                nc.vector.tensor_scalar(out=t[:], in0=hold["out", h, it][:], scalar1=1.0 / 32, scalar2=None, op0=MULT)
             nc.sync.dma_start(out=out_0[128 * it : 128 * (it + 1), 512 * h : 512 * (h + 1)], in_=t[:])
             hold["os", h, it] = t
 
+        def out(h, it, eng="S"):
+            outM(h, it)
+            outE(h, it, eng)
+
         def pB(h, it, eng="V"):
-            t = work.tile([128, 512], BF16, name="ob", bufs=8)
-            o = t[:].rearrange("p (w c e) -> p w c e", w=2, e=2)
-            i = hold["os", h, it][:].rearrange("p (c w e) -> p w c e", w=2, e=2)
-            if eng == "V":
-                nc.vector.tensor_copy(out=o, in_=i)
-            else:
-                nc.gpsimd.tensor_scalar(out=o, in0=i, scalar1=1.0, scalar2=0.0, op0=MULT, op1=ADD)
-            hold["ob", h, it] = t
+            o = ob[h][it // 2][:, it % 2, :].rearrange("p (e c b) -> p e c b", e=2, b=2)
+            copy(eng, o, hold["os", h, it][:].rearrange("p (c e b) -> p e c b", e=2, b=2))
 
         def pT(h, ip):
-            t = bank("tr", [128, 2, 256])
+            t = bank([128, 2, 256])
             for k in range(2):
-                w = hold["ob", h, 2 * ip + k][:].bitcast(F32)
+                w = ob[h][ip][:, k, :].bitcast(F32)
                 for e in range(2):
                     nc.tensor.transpose(t[:, e, 128 * k : 128 * (k + 1)], w[:, 128 * e : 128 * (e + 1)], ident[:])
             hold["pt", h, ip] = t
 
-        def pE(h, ip, eng):
+        def pE(h, ip, eng="S"):
             c = slice(256 * ip, 256 * (ip + 1))
             o = pin[h][:, c, :].rearrange("p c k -> p (c k)").bitcast(F32).rearrange("p (c e) -> p c e", e=2)
-            i = hold["pt", h, ip][:].rearrange("p e c -> p c e")
-            if eng == "S":
-                nc.scalar.copy(out=o, in_=i)
-            else:
-                nc.vector.tensor_copy(out=o, in_=i)
-
-        def pM(h, it):
-            t = bank("tr", [128, 4, 128])
-            for j in range(4):
-                c = slice(512 * h + 128 * j, 512 * h + 128 * (j + 1))
-                for g in range(2):
-                    nc.tensor.matmul_mx(
-                        out=t[:, j, :],
-                        lhsT=fc[g][:, c].bitcast(E4M3),
-                        lhsT_scale=fs[g][:, c],
-                        rhs=dc[g][:, 128 * it : 128 * (it + 1)].bitcast(E4M3),
-                        rhs_scale=ds[g][:, 128 * it : 128 * (it + 1)],
-                        start=g == 0,
-                        stop=g == 1,
-                    )
-            hold["pm", h, it] = t
-
-        def pD(h, it, eng):
-            o = pin[h][:, 128 * it : 128 * (it + 1), :]
-            i = hold["pm", h, it][:].rearrange("p j c -> p c j")
-            if eng == "S":
-                nc.scalar.mul(out=o, in_=i, mul=1.0 / 32)
-            else:
-                nc.vector.tensor_scalar(out=o, in0=i, scalar1=1.0 / 32, scalar2=None, op0=MULT)
+            copy(eng, o, hold["pt", h, ip][:].rearrange("p e c -> p c e"))
 
         def pQ(h, c0, c1):
             nc.vector.quantize_mx(
@@ -354,143 +274,178 @@ def tile_adversarialsdfconditionalpricingmoments_x2_kernel(
                     out=out_2[h, 4 * b : 4 * b + 4, :].bitcast(I32), in_=ps[h][32 * b : 32 * b + 4, :].bitcast(I32)
                 )
 
+        nc.vector.memset(ws_sb["o"][:].rearrange("p g n -> p (g n)").bitcast(I32), 0)
+        load_z(0, 0, 1)
+        load_scales(nc.scalar, "o", wo_scales)
+        load_z(0, 1, 2)
+        load_words("o", wo_words, 0)
+        load_z(0, 2, 4)
+        load_r(0, 0, 1)
+        load_words("o", wo_words, 1)
+        load_r(0, 1, 2)
+        load_r(0, 2, 4)
+        load_z(1, 0, 2)
+        load_r(1, 0, 2)
+        load_z(1, 2, 4)
+        load_r(1, 2, 4)
+        make_identity(nc, ident[:])
+        nc.vector.memset(bg_rows[:], 0.0)
+        nc.vector.memset(ws_sb["g"][:].rearrange("p g n -> p (g n)").bitcast(I32), 0)
+        load_words("g", wg_words, 0)
+        load_scales(nc.sync, "g", wg_scales)
+        load_words("g", wg_words, 1)
+        nc.gpsimd.dma_start(out=bg_rows[0:8, :], in_=bg.rearrange("(a p) -> a p", p=128))
+        nc.gpsimd.dma_start(out=v_sb[:], in_=v.rearrange("(g p j) -> p g j", p=128, j=4))
+        nc.gpsimd.dma_start(out=u_sb[:], in_=u.rearrange("(g p j) -> p g j", p=128, j=4))
+        nc.gpsimd.tensor_scalar(out=nv[:], in0=v_sb[:], scalar1=-1.0 / 32, scalar2=0.0, op0=MULT, op1=ADD)
 
-        dummy(7)
-        for j in (0, 2):
+        def om(g, j, nh):
+            omM(g, j, nh)
+            omR(g, j, nh)
+
+        def zTE(g, j0, j1):
+            for j in range(j0, j1):
+                zT(g, j)
+                zE(g, j)
+
+        def zQQ(g, j0, j1):
             for h in range(2):
-                zT(0, h, j, j + 2)
-                zE(0, h, j, j + 2, "SV"[h])
-            for h in range(2):
-                zQ(0, h, 128 * j, 128 * (j + 2))
-            if j == 2:
-                dummy(2)
-        om = [(j, nh) for j in range(4) for nh in range(2)]
-        for k in range(8):
-            omM(0, *om[k])
-            omR(0, *om[k])
-            if k == 3:
-                bgT()
-                uB()
-        for q in range(4):
-            wgM(0, q)
-            tanh(0, q)
-        sd(0)
-        fU(0, 0)
-        fU(0, 1)
+                zQ(g, h, j0, j1)
+
+        def fTU(g, qt):
+            fT(g, qt)
+            fU(g, qt)
+
+        for j in range(2):
+            zTE(0, j, j + 1)
+            zQQ(0, j, j + 1)
+        zTE(0, 2, 4)
+        om(0, 0, 0)
+        zQQ(0, 2, 4)
+        om(0, 0, 1)
+        om(0, 1, 0)
+        om(0, 1, 1)
+        bgT()
+        om(0, 2, 0)
+        om(0, 2, 1)
+        zTE(1, 0, 2)
+        om(0, 3, 0)
+        zQQ(1, 0, 2)
+        om(0, 3, 1)
+        zTE(1, 2, 4)
+        om(1, 0, 0)
+        sd(0, 0, 4)
+        om(1, 0, 1)
+        zQQ(1, 2, 4)
         for j in range(4):
             dS(0, j)
-        for j in (0, 2):
-            for h in range(2):
-                zT(1, h, j, j + 2)
-                zE(1, h, j, j + 2, "S")
-            for h in range(2):
-                zQ(1, h, 128 * j, 128 * (j + 2))
-        fU(0, 2)
-        fU(0, 3)
-        for k in range(4):
-            for i in (2 * k, 2 * k + 1):
-                omM(1, *om[i])
-                omR(1, *om[i])
-            wgM(1, k)
-            tanh(1, k)
-            if k:
-                fU(1, k - 1)
-            dI(0, 256 * k, 256 * (k + 1))
-            if k == 1:
-                fT(0, 0)
-                fT(0, 1)
-                fE(0, 0)
-                fE(0, 1)
-        sd(1)
-        fU(1, 3)
+        om(1, 1, 0)
+        om(1, 1, 1)
+        wg(0, 0)
+        dI(0, 0, 256, DI0)
+        om(1, 2, 0)
+        om(1, 2, 1)
+        wg(0, 1)
+        dI(0, 256, 512, DI0)
+        om(1, 3, 0)
+        om(1, 3, 1)
+
+        wg(0, 2)
+        wg(0, 3)
+        fT(0, 0)
+        fT(0, 1)
+        fU(0, 0)
+        sd(1, 0, 4)
+        fU(0, 1)
         for j in range(4):
             dS(1, j)
-        for q in range(4, 6):
-            wgM(0, q)
-            tanh(0, q)
-        dI(1, 0, 256)
-        fT(1, 0)
-        fT(1, 1)
-        dI(1, 256, 512, "V")
-        fE(1, 0, "V")
-        fE(1, 1)
-        fQ(0, 0)
+        for qt in range(4):
+            wg(1, qt)
         dQ(0, 0, 512)
-        dQ(1, 256, 512)
-        dQ(1, 0, 256)
-        fQ(1, 0)
-        for q in range(6, 8):
-            wgM(0, q)
-            tanh(0, q)
-        dI(1, 512, 768)
-        for q in range(4, 6):
-            wgM(1, q)
-            tanh(1, q)
-        for q in range(4, 8):
-            fU(0, q)
-        for it in range(4):
-            outM(0, it)
-            outE(0, it, "S")
+        dI(1, 0, 256, "V")
+        dI(1, 256, 512, "S")
+        fTU(0, 2)
+        fTU(0, 3)
+        for qt in range(4):
+            fTU(1, qt)
+            if qt == 0:
+                fQ(0, 0, 512)
+        for qt in range(4, 8):
+            wg(0, qt)
+        dQ(1, 0, 512)
+        fQ(1, 0, 512)
+        for k in range(2, 4):
+            dI(0, 256 * k, 256 * (k + 1), "SV"[k % 2])
+        for qt in range(4, 6):
+            wg(1, qt)
+        dI(1, 512, 768, "V")
         dQ(0, 512, 1024)
         dI(1, 768, 1024, "V")
-        dQ(1, 512, 1024)
-        for q in range(6, 8):
-            wgM(1, q)
-            tanh(1, q)
-        fT(0, 2)
-        fT(0, 3)
-        fE(0, 2, "V")
-        fE(0, 3)
-        for q in range(4, 8):
-            fU(1, q)
-        for it in range(4, 8):
-            outM(0, it)
-            outE(0, it, "S")
-        for it in range(4):
-            pB(0, it, "G")
-        fQ(0, 1)
-        fT(1, 2)
-        fT(1, 3)
-        fE(1, 2, "V")
-        fE(1, 3)
-        fQ(1, 1)
-        for ip in range(2):
-            pT(0, ip)
-            pE(0, ip, "S")
-        for it in range(4, 8):
-            pB(0, it, "G")
-        for it in range(4):
-            outM(1, it)
-            outE(1, it, "S")
+        out(0, 0)
+        out(0, 1)
+        for qt in range(4, 8):
+            fTU(0, qt)
+            if qt == 4:
+                dQ(1, 512, 1024)
+        out(0, 2)
+        out(0, 3)
+        wg(1, 6)
+        wg(1, 7)
+        pB(0, 0, PB)
+        pB(0, 1, PB)
+        out(0, 4)
+        for qt in range(4, 8):
+            fTU(1, qt)
+            if qt == 4:
+                fQ(0, 512, 1024)
+        pB(0, 2, PB)
+        pB(0, 3, PB)
+        for it in range(5, 8):
+            out(0, it)
+        pT(0, 0)
+        pT(0, 1)
+        pB(0, 4)
+        fQ(1, 512, 1024)
+        pE(0, 0)
+        pE(0, 1)
+        for it in range(5, 8):
+            pB(0, it)
+        out(1, 0)
+        out(1, 1)
+        pT(0, 2)
+        pT(0, 3)
         pQ(0, 0, 512)
         pW(0, 0, 512)
-        for ip in range(2, 4):
-            pT(0, ip)
-            pE(0, ip, "SV"[ip % 2])
+        pE(0, 2, "V")
+        pE(0, 3, "V")
+        out(1, 2)
+        out(1, 3)
+        pB(1, 0)
+        pB(1, 1)
         pQ(0, 512, 1024)
         pW(0, 512, 1024)
         pS(0)
-        for it in range(4):
-            pB(1, it, "GV"[it % 2])
-        for it in range(6, 8):
-            pM(1, it)
-            pD(1, it, "SV"[it % 2])
-        for it in range(4, 6):
-            outM(1, it)
-            outE(1, it, "S")
-            pB(1, it, "V")
-        pQ(1, 768, 1024)
-        for ip in range(2):
-            pT(1, ip)
-            pE(1, ip, "VS"[ip])
+        out(1, 4)
+        out(1, 5)
+        pB(1, 2)
+        pB(1, 3)
+        pT(1, 0)
+        out(1, 6)
+        out(1, 7)
+        pT(1, 1)
+        pE(1, 0, "V")
+        pB(1, 4)
+        pB(1, 5)
+        pT(1, 2)
+        pE(1, 1, "V")
+        pB(1, 6)
+        pB(1, 7)
+        pT(1, 3)
+        pE(1, 2)
         pQ(1, 0, 512)
         pW(1, 0, 512)
-        for it in range(6, 8):
-            outM(1, it)
-            outE(1, it, "S")
-            if it == 6:
-                pT(1, 2)
-                pE(1, 2, "V")
+        pE(1, 3)
         pQ(1, 512, 768)
+        pQ(1, 768, 1024)
         pW(1, 512, 1024)
         pS(1)

@@ -15,8 +15,8 @@ MULT = mybir.AluOpType.mult
 ACT = mybir.ActivationFunctionType
 
 T, D, N, Q = 1024, 1024, 1024, 1024
-THB, OSB = 12, 12
-DI0, PB = "S", "S"
+THB, OSB = 12, 10
+DI0, PB = "G", "G"
 FLOPS = 3 * 2 * 1024 * 1024 * 1024
 
 
@@ -42,6 +42,8 @@ def tile_adversarialsdfconditionalpricingmoments_x2_kernel(
         v_sb = kt("v", [128, 2, 4], BF16)
         nv = kt("nv", [128, 2, 4], F32)
         u_sb = kt("u", [128, 2, 4], BF16)
+        zero = kt("zero", [128, 512], BF16)
+        warm = kt("warm", [128, 1], F32)
         eye = kt("eye", [128, 8], BF16)
         zin = [[kt("zin%d%d" % (g, a), [128, 2, 256, 4], BF16) for a in range(2)] for g in range(2)]
         zc = [[kt("zc%d%d" % (g, h), [128, 512], U32) for h in range(2)] for g in range(2)]
@@ -68,6 +70,12 @@ def tile_adversarialsdfconditionalpricingmoments_x2_kernel(
                 nc.vector.tensor_copy(out=o, in_=i)
             else:
                 nc.gpsimd.tensor_scalar(out=o, in0=i, scalar1=1.0, scalar2=0.0, op0=MULT, op1=ADD)
+
+        def scale(eng, o, i):
+            if eng == "S":
+                nc.scalar.mul(out=o, in_=i, mul=1.0 / 32)
+            else:
+                nc.vector.tensor_scalar(out=o, in0=i, scalar1=1.0 / 32, scalar2=None, op0=MULT)
 
         def load_rows(tiles, name, src, g, j0, j1):
             t = kt("%s%d%d" % (name, g, j0), [128, j1 - j0, 1024], BF16)
@@ -96,13 +104,27 @@ def tile_adversarialsdfconditionalpricingmoments_x2_kernel(
         def bank(shape):
             return psum.tile(shape, F32, name="bank", tag="bank")
 
+        def zS(g, j):
+            t = work.tile([128, 2, 2, 128], U32, name="zsort", bufs=2)
+            nc.scalar.copy(out=t[:], in_=z_sb[g, j].bitcast(U32).rearrange("p (h c e) -> p h e c", h=2, e=2))
+            hold["zs", g, j] = t
+
         def zT(g, j):
             t = bank([128, 2, 2, 128])
             w = z_sb[g, j].bitcast(F32)
             for h in range(2):
                 for e in range(2):
-                    nc.tensor.transpose(t[:, h, e, :], w[:, 256 * h + e : 256 * (h + 1) : 2], ident[:])
+                    if ("zs", g, j) in hold:
+                        src = hold["zs", g, j][:, h, e, :].bitcast(F32)
+                    else:
+                        src = w[:, 256 * h + e : 256 * (h + 1) : 2]
+                    nc.tensor.transpose(t[:, h, e, :], src, ident[:])
             hold["z", g, j] = t
+
+        def warm_pe(n):
+            for k in range(n):
+                t = bank([128, 512])
+                nc.tensor.matmul(t[:], zero[:, 0:128], zero[:], start=True, stop=True)
 
         def zE(g, j, eng="S"):
             w = zin[g][j // 2][:].rearrange("p h c k -> p (h c k)").bitcast(F32).rearrange("p (h a c e) -> p h a c e", h=2, a=2, e=2)
@@ -201,10 +223,11 @@ def tile_adversarialsdfconditionalpricingmoments_x2_kernel(
             hold["f", g, qt] = t
 
         def fU(g, qt):
+            cols = fin[g][:, 512 * (qt // 4) : 512 * (qt // 4 + 1), :].rearrange("p (s m) j -> p s m j", s=4)
             nc.vector.tensor_tensor(
-                out=fin[g][:, 128 * qt : 128 * (qt + 1), :],
-                in0=hold["f", g, qt][:].rearrange("p j c -> p c j"),
-                in1=u_sb[:, g, :].unsqueeze(1).to_broadcast([128, 128, 4]),
+                out=cols[:, :, 32 * (qt % 4) : 32 * (qt % 4 + 1), :],
+                in0=hold["f", g, qt][:].rearrange("p j (m s) -> p s m j", s=4),
+                in1=u_sb[:, g, :].unsqueeze(1).unsqueeze(1).to_broadcast([128, 4, 32, 4]),
                 op=MULT,
             )
 
@@ -230,10 +253,7 @@ def tile_adversarialsdfconditionalpricingmoments_x2_kernel(
 
         def outE(h, it, eng="S"):
             t = work.tile([128, 512], F32, name="osb", bufs=OSB)
-            if eng == "S":
-                nc.scalar.mul(out=t[:], in_=hold["out", h, it][:], mul=1.0 / 32)
-            else:
-                nc.vector.tensor_scalar(out=t[:], in0=hold["out", h, it][:], scalar1=1.0 / 32, scalar2=None, op0=MULT)
+            scale(eng, t[:].rearrange("p (m s) -> p m s", s=4), hold["out", h, it][:].rearrange("p (s m) -> p m s", s=4))
             nc.sync.dma_start(out=out_0[128 * it : 128 * (it + 1), 512 * h : 512 * (h + 1)], in_=t[:])
             hold["os", h, it] = t
 
@@ -258,6 +278,26 @@ def tile_adversarialsdfconditionalpricingmoments_x2_kernel(
             o = pin[h][:, c, :].rearrange("p c k -> p (c k)").bitcast(F32).rearrange("p (c e) -> p c e", e=2)
             copy(eng, o, hold["pt", h, ip][:].rearrange("p e c -> p c e"))
 
+        def pM(h, it):
+            t = bank([128, 4, 128])
+            i = slice(128 * it, 128 * (it + 1))
+            for s in range(4):
+                c = slice(512 * h + 128 * s, 512 * h + 128 * (s + 1))
+                for g in range(2):
+                    nc.tensor.matmul_mx(
+                        out=t[:, s, :],
+                        lhsT=fc[g][:, c].bitcast(E4M3),
+                        lhsT_scale=fs[g][:, c],
+                        rhs=dc[g][:, i].bitcast(E4M3),
+                        rhs_scale=ds[g][:, i],
+                        start=g == 0,
+                        stop=g == 1,
+                    )
+            hold["pm", h, it] = t
+
+        def pD(h, it, eng="V"):
+            scale(eng, pin[h][:, 128 * it : 128 * (it + 1), :], hold["pm", h, it][:].rearrange("p s c -> p c s"))
+
         def pQ(h, c0, c1):
             nc.vector.quantize_mx(
                 out=pc[h][:, c0:c1].bitcast(E4M3), scales=ps[h][:, c0:c1], in_=pin[h][:, c0:c1, :].rearrange("p c k -> p (c k)")
@@ -268,36 +308,40 @@ def tile_adversarialsdfconditionalpricingmoments_x2_kernel(
                 out=out_1[h].rearrange("p m t -> p (m t)")[:, 4 * c0 : 4 * c1].bitcast(I32), in_=pc[h][:, c0:c1].bitcast(I32)
             )
 
-        def pS(h, eng=None):
+        def pS(h, engs):
             for b in range(4):
-                (eng or nc.sync).dma_start(
+                engs[b % len(engs)].dma_start(
                     out=out_2[h, 4 * b : 4 * b + 4, :].bitcast(I32), in_=ps[h][32 * b : 32 * b + 4, :].bitcast(I32)
                 )
 
         nc.vector.memset(ws_sb["o"][:].rearrange("p g n -> p (g n)").bitcast(I32), 0)
+        nc.vector.memset(zero[:], 0.0)
+        nc.vector.memset(ident[:], 0.0)
+        make_identity(nc, ident[:], nomemset=True)
+        nc.vector.memset(bg_rows[:], 0.0)
+        nc.vector.memset(ws_sb["g"][:].rearrange("p g n -> p (g n)").bitcast(I32), 0)
         load_z(0, 0, 1)
-        load_scales(nc.scalar, "o", wo_scales)
         load_z(0, 1, 2)
-        load_words("o", wo_words, 0)
         load_z(0, 2, 4)
+        load_words("o", wo_words, 0)
+        load_scales(nc.scalar, "o", wo_scales)
         load_r(0, 0, 1)
         load_words("o", wo_words, 1)
         load_r(0, 1, 2)
-        load_r(0, 2, 4)
         load_z(1, 0, 2)
-        load_r(1, 0, 2)
-        load_z(1, 2, 4)
-        load_r(1, 2, 4)
-        make_identity(nc, ident[:])
-        nc.vector.memset(bg_rows[:], 0.0)
-        nc.vector.memset(ws_sb["g"][:].rearrange("p g n -> p (g n)").bitcast(I32), 0)
+        load_r(0, 2, 4)
         load_words("g", wg_words, 0)
         load_scales(nc.sync, "g", wg_scales)
+        load_z(1, 2, 4)
+        nc.sync.dma_start(out=v_sb[:], in_=v.rearrange("(g p j) -> p g j", p=128, j=4))
+        load_r(1, 0, 2)
+        load_r(1, 2, 4)
         load_words("g", wg_words, 1)
+        nc.sync.dma_start(out=u_sb[:], in_=u.rearrange("(g p j) -> p g j", p=128, j=4))
         nc.gpsimd.dma_start(out=bg_rows[0:8, :], in_=bg.rearrange("(a p) -> a p", p=128))
-        nc.gpsimd.dma_start(out=v_sb[:], in_=v.rearrange("(g p j) -> p g j", p=128, j=4))
-        nc.gpsimd.dma_start(out=u_sb[:], in_=u.rearrange("(g p j) -> p g j", p=128, j=4))
         nc.gpsimd.tensor_scalar(out=nv[:], in0=v_sb[:], scalar1=-1.0 / 32, scalar2=0.0, op0=MULT, op1=ADD)
+        nc.scalar.activation(out=warm[:], in_=zero[:, 0:1], func=ACT.Tanh)
+        warm_pe(3)
 
         def om(g, j, nh):
             omM(g, j, nh)
@@ -316,136 +360,126 @@ def tile_adversarialsdfconditionalpricingmoments_x2_kernel(
             fT(g, qt)
             fU(g, qt)
 
-        for j in range(2):
-            zTE(0, j, j + 1)
-            zQQ(0, j, j + 1)
+        def dSS(g, a):
+            for j in range(4):
+                dS(g, j, 512 * a, 512 * (a + 1))
+
+        def dII(g, a, eng):
+            for k in (2 * a, 2 * a + 1):
+                dI(g, 256 * k, 256 * (k + 1), eng)
+
+        zTE(0, 0, 1)
+        zQQ(0, 0, 1)
+        zTE(0, 1, 2)
+        zQQ(0, 1, 2)
+        warm_pe(2)
         zTE(0, 2, 4)
         om(0, 0, 0)
         zQQ(0, 2, 4)
         om(0, 0, 1)
+        bgT()
         om(0, 1, 0)
         om(0, 1, 1)
-        bgT()
+        zS(1, 0)
+        zS(1, 1)
         om(0, 2, 0)
         om(0, 2, 1)
+        omM(0, 3, 0)
+        omM(0, 3, 1)
         zTE(1, 0, 2)
-        om(0, 3, 0)
+        omR(0, 3, 0)
         zQQ(1, 0, 2)
-        om(0, 3, 1)
-        zTE(1, 2, 4)
-        om(1, 0, 0)
-        sd(0, 0, 4)
-        om(1, 0, 1)
-        zQQ(1, 2, 4)
-        for j in range(4):
-            dS(0, j)
-        om(1, 1, 0)
-        om(1, 1, 1)
+        omR(0, 3, 1)
         wg(0, 0)
-        dI(0, 0, 256, DI0)
-        om(1, 2, 0)
-        om(1, 2, 1)
+        zS(1, 2)
+        zS(1, 3)
         wg(0, 1)
-        dI(0, 256, 512, DI0)
-        om(1, 3, 0)
-        om(1, 3, 1)
-
         wg(0, 2)
+        omM(1, 0, 0)
+        sd(0, 0, 4)
+        omR(1, 0, 0)
+        dSS(0, 0)
+        om(1, 0, 1)
+        zTE(1, 2, 4)
+        om(1, 1, 0)
+        omM(1, 1, 1)
         wg(0, 3)
-        fT(0, 0)
-        fT(0, 1)
-        fU(0, 0)
+        wg(0, 4)
+        dII(0, 0, "S")
+        zQQ(1, 2, 4)
+        dSS(0, 1)
+        dII(0, 1, DI0)
+        omR(1, 1, 1)
+        for j in (2, 3):
+            om(1, j, 0)
+            om(1, j, 1)
+
+        for qt in range(4):
+            wg(1, qt)
+        dQ(0, 0, 256)
         sd(1, 0, 4)
-        fU(0, 1)
-        for j in range(4):
-            dS(1, j)
+        dQ(0, 256, 512)
+        dSS(1, 0)
+        dSS(1, 1)
+        dII(1, 0, "S")
+        dII(1, 1, DI0)
         for qt in range(4):
-            wg(1, qt)
-        dQ(0, 0, 512)
-        dI(1, 0, 256, "V")
-        dI(1, 256, 512, "S")
-        fTU(0, 2)
-        fTU(0, 3)
-        for qt in range(4):
-            fTU(1, qt)
-            if qt == 0:
-                fQ(0, 0, 512)
-        for qt in range(4, 8):
-            wg(0, qt)
-        dQ(1, 0, 512)
-        fQ(1, 0, 512)
-        for k in range(2, 4):
-            dI(0, 256 * k, 256 * (k + 1), "SV"[k % 2])
-        for qt in range(4, 6):
-            wg(1, qt)
-        dI(1, 512, 768, "V")
-        dQ(0, 512, 1024)
-        dI(1, 768, 1024, "V")
-        out(0, 0)
-        out(0, 1)
-        for qt in range(4, 8):
             fTU(0, qt)
-            if qt == 4:
-                dQ(1, 512, 1024)
-        out(0, 2)
-        out(0, 3)
-        wg(1, 6)
-        wg(1, 7)
-        pB(0, 0, PB)
-        pB(0, 1, PB)
-        out(0, 4)
-        for qt in range(4, 8):
+        wg(0, 5)
+        wg(0, 6)
+        for qt in range(4):
             fTU(1, qt)
-            if qt == 4:
-                fQ(0, 512, 1024)
-        pB(0, 2, PB)
-        pB(0, 3, PB)
-        for it in range(5, 8):
+        wg(0, 7)
+        for qt in range(4, 8):
+            wg(1, qt)
+        fQ(0, 0, 512)
+        fQ(1, 0, 512)
+        dQ(1, 0, 512)
+        dQ(0, 512, 1024)
+        dQ(1, 512, 1024)
+        for g in range(2):
+            for it in (2 * g, 2 * g + 1):
+                out(0, it)
+                pB(0, it, PB)
+            for qt in range(4, 8):
+                fTU(g, qt)
+            fQ(g, 512, 1024)
+        for it in range(4, 8):
             out(0, it)
+            pB(0, it, PB)
         pT(0, 0)
         pT(0, 1)
-        pB(0, 4)
-        fQ(1, 512, 1024)
-        pE(0, 0)
-        pE(0, 1)
-        for it in range(5, 8):
-            pB(0, it)
-        out(1, 0)
-        out(1, 1)
-        pT(0, 2)
-        pT(0, 3)
-        pQ(0, 0, 512)
-        pW(0, 0, 512)
-        pE(0, 2, "V")
-        pE(0, 3, "V")
-        out(1, 2)
-        out(1, 3)
-        pB(1, 0)
-        pB(1, 1)
+        pE(0, 0, "V")
+        pE(0, 1, "V")
+        for it in range(6):
+            out(1, it)
+            if it == 0:
+                pQ(0, 0, 512)
+                pW(0, 0, 512)
+            if it < 4:
+                pB(1, it)
+        for h, ip in ((0, 2), (0, 3), (1, 0), (1, 1)):
+            pT(h, ip)
+            pE(h, ip, "VS"[ip % 2])
+            if ip == 2:
+                pB(1, 4)
+                pB(1, 5)
+        pM(1, 6)
+        pM(1, 7)
         pQ(0, 512, 1024)
         pW(0, 512, 1024)
-        pS(0)
-        out(1, 4)
-        out(1, 5)
-        pB(1, 2)
-        pB(1, 3)
-        pT(1, 0)
-        out(1, 6)
-        out(1, 7)
-        pT(1, 1)
-        pE(1, 0, "V")
-        pB(1, 4)
-        pB(1, 5)
+        pS(0, [nc.sync])
+        pD(1, 6, "V")
+        pD(1, 7, "S")
         pT(1, 2)
-        pE(1, 1, "V")
-        pB(1, 6)
-        pB(1, 7)
-        pT(1, 3)
-        pE(1, 2)
         pQ(1, 0, 512)
         pW(1, 0, 512)
-        pE(1, 3)
-        pQ(1, 512, 768)
+        pE(1, 2, "V")
+        outM(1, 6)
+        outM(1, 7)
+        outE(1, 6)
         pQ(1, 768, 1024)
+        pQ(1, 512, 768)
         pW(1, 512, 1024)
-        pS(1)
+        pS(1, [nc.sync])
+        outE(1, 7)

@@ -223,11 +223,15 @@ def tile_adversarialsdfconditionalpricingmoments_x2_kernel(
             hold["f", g, qt] = t
 
         def fU(g, qt):
-            cols = fin[g][:, 512 * (qt // 4) : 512 * (qt // 4 + 1), :].rearrange("p (s m) j -> p s m j", s=4)
+            cols = fin[g][:, 512 * (qt // 4) : 512 * (qt // 4 + 1), :]
+            if qt < 4:
+                cols = cols.rearrange("p (m s) j -> p m s j", s=4)
+            else:
+                cols = cols.rearrange("p (s m) j -> p m s j", s=4)
             nc.vector.tensor_tensor(
-                out=cols[:, :, 32 * (qt % 4) : 32 * (qt % 4 + 1), :],
-                in0=hold["f", g, qt][:].rearrange("p j (m s) -> p s m j", s=4),
-                in1=u_sb[:, g, :].unsqueeze(1).unsqueeze(1).to_broadcast([128, 4, 32, 4]),
+                out=cols[:, 32 * (qt % 4) : 32 * (qt % 4 + 1), :, :],
+                in0=hold["f", g, qt][:].rearrange("p j (m s) -> p m s j", s=4),
+                in1=u_sb[:, g, :].unsqueeze(1).unsqueeze(1).to_broadcast([128, 32, 4, 4]),
                 op=MULT,
             )
 
@@ -253,7 +257,7 @@ def tile_adversarialsdfconditionalpricingmoments_x2_kernel(
 
         def outE(h, it, eng="S"):
             t = work.tile([128, 512], F32, name="osb", bufs=OSB)
-            scale(eng, t[:].rearrange("p (m s) -> p m s", s=4), hold["out", h, it][:].rearrange("p (s m) -> p m s", s=4))
+            scale(eng, t[:].rearrange("p (m s) -> p m s", s=4), hold["out", h, it][:].rearrange(("p (m s) -> p m s", "p (s m) -> p m s")[h], s=4))
             nc.sync.dma_start(out=out_0[128 * it : 128 * (it + 1), 512 * h : 512 * (h + 1)], in_=t[:])
             hold["os", h, it] = t
 

@@ -15,8 +15,7 @@ MULT = mybir.AluOpType.mult
 ACT = mybir.ActivationFunctionType
 
 T, D, N, Q = 1024, 1024, 1024, 1024
-THB, OSB = 12, 10
-DI0, PB = "G", "G"
+THB, OSB = 12, 5
 FLOPS = 3 * 2 * 1024 * 1024 * 1024
 
 
@@ -256,10 +255,11 @@ def tile_adversarialsdfconditionalpricingmoments_x2_kernel(
             hold["out", h, it] = t
 
         def outE(h, it, eng="S"):
-            t = work.tile([128, 512], F32, name="osb", bufs=OSB)
-            scale(eng, t[:].rearrange("p (m s) -> p m s", s=4), hold["out", h, it][:].rearrange(("p (m s) -> p m s", "p (s m) -> p m s")[h], s=4))
-            nc.sync.dma_start(out=out_0[128 * it : 128 * (it + 1), 512 * h : 512 * (h + 1)], in_=t[:])
-            hold["os", h, it] = t
+            if it % 2 == 0:
+                hold["os", h, it // 2] = work.tile([128, 2, 512], F32, name="osb", bufs=OSB)
+            t = hold["os", h, it // 2][:, it % 2, :]
+            scale(eng, t.rearrange("p (m s) -> p m s", s=4), hold["out", h, it][:].rearrange(("p (m s) -> p m s", "p (s m) -> p m s")[h], s=4))
+            nc.sync.dma_start(out=out_0[128 * it : 128 * (it + 1), 512 * h : 512 * (h + 1)], in_=t)
 
         def out(h, it, eng="S"):
             outM(h, it)
@@ -267,7 +267,11 @@ def tile_adversarialsdfconditionalpricingmoments_x2_kernel(
 
         def pB(h, it, eng="V"):
             o = ob[h][it // 2][:, it % 2, :].rearrange("p (e c b) -> p e c b", e=2, b=2)
-            copy(eng, o, hold["os", h, it][:].rearrange("p (c e b) -> p e c b", e=2, b=2))
+            copy(eng, o, hold["os", h, it // 2][:, it % 2, :].rearrange("p (c e b) -> p e c b", e=2, b=2))
+
+        def pB2(h, ip):
+            o = ob[h][ip][:].rearrange("p k (e c b) -> p k e c b", e=2, b=2)
+            copy("V", o, hold["os", h, ip][:].rearrange("p k (c e b) -> p k e c b", e=2, b=2))
 
         def pT(h, ip):
             t = bank([128, 2, 256])
@@ -364,10 +368,6 @@ def tile_adversarialsdfconditionalpricingmoments_x2_kernel(
             fT(g, qt)
             fU(g, qt)
 
-        def dSS(g, a):
-            for j in range(4):
-                dS(g, j, 512 * a, 512 * (a + 1))
-
         def dII(g, a, eng):
             for k in (2 * a, 2 * a + 1):
                 dI(g, 256 * k, 256 * (k + 1), eng)
@@ -384,56 +384,53 @@ def tile_adversarialsdfconditionalpricingmoments_x2_kernel(
         bgT()
         om(0, 1, 0)
         om(0, 1, 1)
-        zS(1, 0)
-        zS(1, 1)
-        om(0, 2, 0)
-        om(0, 2, 1)
-        omM(0, 3, 0)
-        omM(0, 3, 1)
+        omM(0, 2, 0)
+        omM(0, 2, 1)
         zTE(1, 0, 2)
-        omR(0, 3, 0)
+        omR(0, 2, 0)
+        omR(0, 2, 1)
+        om(0, 3, 0)
         zQQ(1, 0, 2)
-        omR(0, 3, 1)
-        wg(0, 0)
-        zS(1, 2)
-        zS(1, 3)
-        wg(0, 1)
-        wg(0, 2)
+        om(0, 3, 1)
+        zTE(1, 2, 4)
         omM(1, 0, 0)
+        omM(1, 0, 1)
+        wg(0, 0)
+        wg(0, 1)
         sd(0, 0, 4)
         omR(1, 0, 0)
-        dSS(0, 0)
-        om(1, 0, 1)
-        zTE(1, 2, 4)
-        om(1, 1, 0)
-        omM(1, 1, 1)
-        wg(0, 3)
-        wg(0, 4)
-        dII(0, 0, "S")
+        omR(1, 0, 1)
         zQQ(1, 2, 4)
-        dSS(0, 1)
-        dII(0, 1, DI0)
-        omR(1, 1, 1)
+        for j in range(4):
+            dS(0, j)
+        dII(0, 1, "G")
+        om(1, 1, 0)
+        om(1, 1, 1)
+        wg(0, 2)
+        wg(0, 3)
+        dII(0, 0, "S")
         for j in (2, 3):
             om(1, j, 0)
             om(1, j, 1)
-
         for qt in range(4):
             wg(1, qt)
+        for qt in range(4):
+            fT(0, qt)
         dQ(0, 0, 256)
         sd(1, 0, 4)
         dQ(0, 256, 512)
-        dSS(1, 0)
-        dSS(1, 1)
-        dII(1, 0, "S")
-        dII(1, 1, DI0)
-        for qt in range(4):
-            fTU(0, qt)
+        for j in range(4):
+            dS(1, j)
+        wg(0, 4)
         wg(0, 5)
+        dII(1, 0, "S")
+        dII(1, 1, "G")
+        for qt in range(4):
+            fU(0, qt)
         wg(0, 6)
+        wg(0, 7)
         for qt in range(4):
             fTU(1, qt)
-        wg(0, 7)
         for qt in range(4, 8):
             wg(1, qt)
         fQ(0, 0, 512)
@@ -441,49 +438,50 @@ def tile_adversarialsdfconditionalpricingmoments_x2_kernel(
         dQ(1, 0, 512)
         dQ(0, 512, 1024)
         dQ(1, 512, 1024)
-        for g in range(2):
-            for it in (2 * g, 2 * g + 1):
-                out(0, it)
-                pB(0, it, PB)
-            for qt in range(4, 8):
-                fTU(g, qt)
-            fQ(g, 512, 1024)
+        for qt in range(4, 8):
+            fTU(0, qt)
+        for it in range(4):
+            out(0, it)
+            pB(0, it, "G")
+        for qt in range(4, 8):
+            fTU(1, qt)
+        pT(0, 0)
+        pE(0, 0, "S")
         for it in range(4, 8):
             out(0, it)
-            pB(0, it, PB)
-        pT(0, 0)
         pT(0, 1)
-        pE(0, 0, "V")
-        pE(0, 1, "V")
+        pE(0, 1, "S")
+        fQ(0, 512, 1024)
+        fQ(1, 512, 1024)
+        pB2(0, 2)
+        pB2(0, 3)
+        pQ(0, 0, 512)
+        pW(0, 0, 512)
         for it in range(6):
             out(1, it)
-            if it == 0:
-                pQ(0, 0, 512)
-                pW(0, 0, 512)
-            if it < 4:
-                pB(1, it)
+            if it in (1, 3):
+                pB2(1, it // 2)
         for h, ip in ((0, 2), (0, 3), (1, 0), (1, 1)):
             pT(h, ip)
             pE(h, ip, "VS"[ip % 2])
             if ip == 2:
-                pB(1, 4)
-                pB(1, 5)
-        pM(1, 6)
-        pM(1, 7)
+                pB2(1, 2)
         pQ(0, 512, 1024)
         pW(0, 512, 1024)
         pS(0, [nc.sync])
-        pD(1, 6, "V")
-        pD(1, 7, "S")
+        pM(1, 6)
+        pM(1, 7)
+        pD(1, 6, "S")
         pT(1, 2)
         pQ(1, 0, 512)
         pW(1, 0, 512)
-        pE(1, 2, "V")
+        pD(1, 7, "S")
+        pE(1, 2, "S")
         outM(1, 6)
         outM(1, 7)
-        outE(1, 6)
         pQ(1, 768, 1024)
         pQ(1, 512, 768)
+        outE(1, 6)
         pW(1, 512, 1024)
         pS(1, [nc.sync])
         outE(1, 7)

@@ -47,9 +47,9 @@ def tile_adversarialsdfconditionalpricingmoments_x2_kernel(
         zin = [[kt("zin%d%d" % (g, a), [128, 2, 256, 4], BF16) for a in range(2)] for g in range(2)]
         zc = [[kt("zc%d%d" % (g, h), [128, 512], U32) for h in range(2)] for g in range(2)]
         zs = [[kt("zs%d%d" % (g, h), [128, 512], U8) for h in range(2)] for g in range(2)]
-        fin = [kt("fin%d" % g, [128, Q, 4], BF16) for g in range(2)]
-        fc = [kt("fc%d" % g, [128, Q], U32) for g in range(2)]
-        fs = [kt("fs%d" % g, [128, Q], U8) for g in range(2)]
+        fin = [kt("fin%d" % h, [128, 2, 512, 4], BF16) for h in range(2)]
+        fc = [kt("fc%d" % h, [128, 2, 512], U32) for h in range(2)]
+        fs = [kt("fs%d" % h, [128, 2, 512], U8) for h in range(2)]
         dsc = [kt("dsc%d" % g, [128, 4, N], BF16) for g in range(2)]
         din = [kt("din%d" % g, [128, N, 4], BF16) for g in range(2)]
         dc = [kt("dc%d" % g, [128, N], U32) for g in range(2)]
@@ -222,7 +222,7 @@ def tile_adversarialsdfconditionalpricingmoments_x2_kernel(
             hold["f", g, qt] = t
 
         def fU(g, qt):
-            cols = fin[g][:, 512 * (qt // 4) : 512 * (qt // 4 + 1), :]
+            cols = fin[qt // 4][:, g, :, :]
             if qt < 4:
                 cols = cols.rearrange("p (m s) j -> p m s j", s=4)
             else:
@@ -234,21 +234,23 @@ def tile_adversarialsdfconditionalpricingmoments_x2_kernel(
                 op=MULT,
             )
 
-        def fQ(g, c0, c1):
+        def fQ(h, g0=0, g1=2):
             nc.vector.quantize_mx(
-                out=fc[g][:, c0:c1].bitcast(E4M3), scales=fs[g][:, c0:c1], in_=fin[g][:, c0:c1, :].rearrange("p c k -> p (c k)")
+                out=fc[h][:, g0:g1, :].rearrange("p g c -> p (g c)").bitcast(E4M3),
+                scales=fs[h][:, g0:g1, :].rearrange("p g c -> p (g c)"),
+                in_=fin[h][:, g0:g1, :, :].rearrange("p g c k -> p (g c k)"),
             )
 
         def outM(h, it):
             t = bank([128, 512])
-            i, c = slice(128 * it, 128 * (it + 1)), slice(512 * h, 512 * (h + 1))
+            i = slice(128 * it, 128 * (it + 1))
             for g in range(2):
                 nc.tensor.matmul_mx(
                     out=t[:],
                     lhsT=dc[g][:, i].bitcast(E4M3),
                     lhsT_scale=ds[g][:, i],
-                    rhs=fc[g][:, c].bitcast(E4M3),
-                    rhs_scale=fs[g][:, c],
+                    rhs=fc[h][:, g, :].bitcast(E4M3),
+                    rhs_scale=fs[h][:, g, :],
                     start=g == 0,
                     stop=g == 1,
                 )
@@ -290,12 +292,12 @@ def tile_adversarialsdfconditionalpricingmoments_x2_kernel(
             t = bank([128, 4, 128])
             i = slice(128 * it, 128 * (it + 1))
             for s in range(4):
-                c = slice(512 * h + 128 * s, 512 * h + 128 * (s + 1))
+                c = slice(128 * s, 128 * (s + 1))
                 for g in range(2):
                     nc.tensor.matmul_mx(
                         out=t[:, s, :],
-                        lhsT=fc[g][:, c].bitcast(E4M3),
-                        lhsT_scale=fs[g][:, c],
+                        lhsT=fc[h][:, g, c].bitcast(E4M3),
+                        lhsT_scale=fs[h][:, g, c],
                         rhs=dc[g][:, i].bitcast(E4M3),
                         rhs_scale=ds[g][:, i],
                         start=g == 0,
@@ -338,15 +340,15 @@ def tile_adversarialsdfconditionalpricingmoments_x2_kernel(
         load_r(0, 1, 2)
         load_z(1, 0, 2)
         load_r(0, 2, 4)
+        load_z(1, 2, 4)
         load_words("g", wg_words, 0)
         load_scales(nc.sync, "g", wg_scales)
-        load_z(1, 2, 4)
-        nc.sync.dma_start(out=v_sb[:], in_=v.rearrange("(g p j) -> p g j", p=128, j=4))
         load_r(1, 0, 2)
         load_r(1, 2, 4)
         load_words("g", wg_words, 1)
         nc.sync.dma_start(out=u_sb[:], in_=u.rearrange("(g p j) -> p g j", p=128, j=4))
         nc.gpsimd.dma_start(out=bg_rows[0:8, :], in_=bg.rearrange("(a p) -> a p", p=128))
+        nc.gpsimd.dma_start(out=v_sb[:], in_=v.rearrange("(g p j) -> p g j", p=128, j=4))
         nc.gpsimd.tensor_scalar(out=nv[:], in0=v_sb[:], scalar1=-1.0 / 32, scalar2=0.0, op0=MULT, op1=ADD)
         nc.scalar.activation(out=warm[:], in_=zero[:, 0:1], func=ACT.Tanh)
         warm_pe(3)
@@ -384,31 +386,35 @@ def tile_adversarialsdfconditionalpricingmoments_x2_kernel(
         bgT()
         om(0, 1, 0)
         om(0, 1, 1)
-        omM(0, 2, 0)
-        omM(0, 2, 1)
-        zTE(1, 0, 2)
-        omR(0, 2, 0)
-        omR(0, 2, 1)
-        om(0, 3, 0)
+        zS(1, 0)
+        zS(1, 1)
+        om(0, 2, 0)
+        sd(0, 0, 2)
+        om(0, 2, 1)
+        omM(0, 3, 0)
+        omM(0, 3, 1)
+        zTE(1, 0, 4)
+        dS(0, 0)
+        omR(0, 3, 0)
+        omR(0, 3, 1)
         zQQ(1, 0, 2)
-        om(0, 3, 1)
-        zTE(1, 2, 4)
-        omM(1, 0, 0)
-        omM(1, 0, 1)
         wg(0, 0)
         wg(0, 1)
-        sd(0, 0, 4)
+        omM(1, 0, 0)
+        omM(1, 0, 1)
+        sd(0, 2, 4)
+        dS(0, 1)
+        zQQ(1, 2, 4)
+        dS(0, 2)
+        dS(0, 3)
+        dII(0, 1, "G")
         omR(1, 0, 0)
         omR(1, 0, 1)
-        zQQ(1, 2, 4)
-        for j in range(4):
-            dS(0, j)
-        dII(0, 1, "G")
-        om(1, 1, 0)
-        om(1, 1, 1)
         wg(0, 2)
         wg(0, 3)
         dII(0, 0, "S")
+        om(1, 1, 0)
+        om(1, 1, 1)
         for j in (2, 3):
             om(1, j, 0)
             om(1, j, 1)
@@ -416,56 +422,57 @@ def tile_adversarialsdfconditionalpricingmoments_x2_kernel(
             wg(1, qt)
         for qt in range(4):
             fT(0, qt)
-        dQ(0, 0, 256)
+        dQ(0, 0, 512)
         sd(1, 0, 4)
-        dQ(0, 256, 512)
+        dQ(0, 512, 1024)
         for j in range(4):
             dS(1, j)
         wg(0, 4)
         wg(0, 5)
-        dII(1, 0, "S")
+        dI(1, 0, 256, "S")
         dII(1, 1, "G")
         for qt in range(4):
             fU(0, qt)
         wg(0, 6)
         wg(0, 7)
+        dI(1, 256, 512, "S")
         for qt in range(4):
             fTU(1, qt)
         for qt in range(4, 8):
             wg(1, qt)
-        fQ(0, 0, 512)
-        fQ(1, 0, 512)
+        fQ(0, 0, 1)
+        fQ(0, 1, 2)
         dQ(1, 0, 512)
-        dQ(0, 512, 1024)
         dQ(1, 512, 1024)
         for qt in range(4, 8):
             fTU(0, qt)
-        for it in range(4):
+        for it in range(2):
             out(0, it)
             pB(0, it, "G")
         for qt in range(4, 8):
             fTU(1, qt)
-        pT(0, 0)
-        pE(0, 0, "S")
-        for it in range(4, 8):
+        for it in range(2, 8):
             out(0, it)
-        pT(0, 1)
-        pE(0, 1, "S")
-        fQ(0, 512, 1024)
-        fQ(1, 512, 1024)
-        pB2(0, 2)
-        pB2(0, 3)
+        pT(0, 0)
+        fQ(1, 0, 1)
+        fQ(1, 1, 2)
+        pE(0, 0, "S")
+        for ip in range(1, 4):
+            pB2(0, ip)
+        for it in range(6):
+            out(1, it, "SVSSSS"[it])
+            if it in (2, 4):
+                pB2(1, it // 2 - 1)
+        for h, ip in ((0, 1), (0, 2), (0, 3), (1, 0), (1, 1)):
+            pT(h, ip)
+        pE(0, 1, "V")
+        pE(0, 2, "S")
+        pB2(1, 2)
         pQ(0, 0, 512)
         pW(0, 0, 512)
-        for it in range(6):
-            out(1, it)
-            if it in (1, 3):
-                pB2(1, it // 2)
-        for h, ip in ((0, 2), (0, 3), (1, 0), (1, 1)):
-            pT(h, ip)
-            pE(h, ip, "VS"[ip % 2])
-            if ip == 2:
-                pB2(1, 2)
+        pE(0, 3, "S")
+        pE(1, 0, "S")
+        pE(1, 1, "S")
         pQ(0, 512, 1024)
         pW(0, 512, 1024)
         pS(0, [nc.sync])
@@ -476,12 +483,11 @@ def tile_adversarialsdfconditionalpricingmoments_x2_kernel(
         pQ(1, 0, 512)
         pW(1, 0, 512)
         pD(1, 7, "S")
-        pE(1, 2, "S")
+        pE(1, 2, "V")
         outM(1, 6)
         outM(1, 7)
-        pQ(1, 768, 1024)
-        pQ(1, 512, 768)
         outE(1, 6)
-        pW(1, 512, 1024)
-        pS(1, [nc.sync])
         outE(1, 7)
+        pQ(1, 512, 1024)
+        pW(1, 512, 1024)
+        pS(1, [nc.sync, nc.scalar])

@@ -34,7 +34,8 @@ def tile_adversarialsdfconditionalpricingmoments_x2_kernel(
 
         ident = kt("ident", [128, 128], F32)
         z_sb, r_sb = {}, {}
-        w_sb = {(k, a): kt("w%s%d" % (k, a), [128, 2, 1024], U8) for k in "og" for a in range(2)}
+        wo_sb = kt("wo", [128, 2, 2048], U8)
+        wg_sb = [kt("wg%d" % a, [128, 2, 1024], U8) for a in range(2)]
         ws_sb = {k: kt("ws" + k, [128, 2, N], U8) for k in "og"}
         bg_rows = kt("bg_rows", [128, 128], BF16)
         bg_t = kt("bg_t", [128, 8], F32)
@@ -55,7 +56,7 @@ def tile_adversarialsdfconditionalpricingmoments_x2_kernel(
         dc = [kt("dc%d" % g, [128, N], U32) for g in range(2)]
         ds = [kt("ds%d" % g, [128, N], U8) for g in range(2)]
         acc = [kt("acc%d" % g, [128, 4, 2], F32) for g in range(2)]
-        sm = [kt("sm%d" % g, [128, 4], F32) for g in range(2)]
+        sm = {}
         ob = [[kt("ob%d%d" % (h, ip), [128, 2, 512], BF16) for ip in range(4)] for h in range(2)]
         pin = [kt("pin%d" % h, [128, N, 4], BF16) for h in range(2)]
         pc = [kt("pc%d" % h, [128, N], U32) for h in range(2)]
@@ -95,9 +96,9 @@ def tile_adversarialsdfconditionalpricingmoments_x2_kernel(
                     in_=src[:, 4 * b : 4 * b + 4, :].rearrange("g q n -> q g n").bitcast(I32),
                 )
 
-        def load_words(k, src, a):
+        def load_wg(a):
             nc.sync.dma_start(
-                out=w_sb[k, a][:].bitcast(I32), in_=src.rearrange("g p n -> p g n")[:, :, 1024 * a : 1024 * (a + 1)].bitcast(I32)
+                out=wg_sb[a][:].bitcast(I32), in_=wg_words.rearrange("g p n -> p g n")[:, :, 1024 * a : 1024 * (a + 1)].bitcast(I32)
             )
 
         def bank(shape):
@@ -150,7 +151,7 @@ def tile_adversarialsdfconditionalpricingmoments_x2_kernel(
                     out=t[:],
                     lhsT=zc[g][h][:, 128 * j : 128 * (j + 1)].bitcast(E4M3),
                     lhsT_scale=zs[g][h][:, 128 * j : 128 * (j + 1)],
-                    rhs=w_sb["o", nh][:, h, :].bitcast(E2M1),
+                    rhs=wo_sb[:, h, 1024 * nh : 1024 * (nh + 1)].bitcast(E2M1),
                     rhs_scale=ws_sb["o"][:, h, 512 * nh : 512 * (nh + 1)],
                     start=h == 0,
                     stop=h == 1,
@@ -170,18 +171,22 @@ def tile_adversarialsdfconditionalpricingmoments_x2_kernel(
             )
 
         def sd(g, j0, j1):
+            t = kt("sm%d%d" % (g, j0), [128, j1 - j0], F32)
             nc.vector.scalar_tensor_tensor(
-                out=sm[g][:, j0:j1], in0=acc[g][:, j0:j1, 0], scalar=-32.0, in1=acc[g][:, j0:j1, 1], op0=ADD, op1=ADD
+                out=t[:], in0=acc[g][:, j0:j1, 0], scalar=-32.0, in1=acc[g][:, j0:j1, 1], op0=ADD, op1=ADD
             )
+            for j in range(j0, j1):
+                sm[g, j] = t[:, j - j0 : j - j0 + 1]
 
-        def dS(g, j, c0=0, c1=N):
-            nc.vector.tensor_scalar(
-                out=dsc[g][:, j, c0:c1],
-                in0=r_sb[g, j][:, c0:c1],
-                scalar1=sm[g][:, j : j + 1],
-                scalar2=nv[:, g, j : j + 1],
-                op0=MULT,
-                op1=MULT,
+        def dS(g, j, eng="V"):
+            if eng == "G":
+                t = kt("sm%d%d" % (g, j), [128, 1], F32)
+                nc.gpsimd.tensor_scalar(
+                    out=t[:], in0=acc[g][:, j, 0:1], scalar1=acc[g][:, j, 1:2], scalar2=-32.0, op0=ADD, op1=ADD
+                )
+                sm[g, j] = t[:]
+            (nc.gpsimd if eng == "G" else nc.vector).tensor_scalar(
+                out=dsc[g][:, j, :], in0=r_sb[g, j], scalar1=sm[g, j], scalar2=nv[:, g, j : j + 1], op0=MULT, op1=MULT
             )
 
         def dI(g, c0, c1, eng="S"):
@@ -197,7 +202,7 @@ def tile_adversarialsdfconditionalpricingmoments_x2_kernel(
             for h in range(2):
                 nc.tensor.matmul_mx(
                     out=t[:],
-                    lhsT=w_sb["g", qt // 4][:, h, 256 * (qt % 4) : 256 * (qt % 4 + 1)].bitcast(E2M1),
+                    lhsT=wg_sb[qt // 4][:, h, 256 * (qt % 4) : 256 * (qt % 4 + 1)].bitcast(E2M1),
                     lhsT_scale=ws_sb["g"][:, h, 128 * qt : 128 * (qt + 1)],
                     rhs=zc[g][h][:].bitcast(E4M3),
                     rhs_scale=zs[g][h][:],
@@ -324,8 +329,8 @@ def tile_adversarialsdfconditionalpricingmoments_x2_kernel(
                     out=out_2[h, 4 * b : 4 * b + 4, :].bitcast(I32), in_=ps[h][32 * b : 32 * b + 4, :].bitcast(I32)
                 )
 
-        nc.vector.memset(ws_sb["o"][:].rearrange("p g n -> p (g n)").bitcast(I32), 0)
         nc.vector.memset(zero[:], 0.0)
+        nc.vector.memset(ws_sb["o"][:].rearrange("p g n -> p (g n)").bitcast(I32), 0)
         nc.vector.memset(ident[:], 0.0)
         make_identity(nc, ident[:], nomemset=True)
         nc.vector.memset(bg_rows[:], 0.0)
@@ -333,25 +338,24 @@ def tile_adversarialsdfconditionalpricingmoments_x2_kernel(
         load_z(0, 0, 1)
         load_z(0, 1, 2)
         load_z(0, 2, 4)
-        load_words("o", wo_words, 0)
+        nc.sync.dma_start(out=wo_sb[:].bitcast(I32), in_=wo_words.rearrange("g p n -> p g n").bitcast(I32))
         load_scales(nc.scalar, "o", wo_scales)
         load_r(0, 0, 1)
-        load_words("o", wo_words, 1)
         load_r(0, 1, 2)
         load_z(1, 0, 2)
         load_r(0, 2, 4)
         load_z(1, 2, 4)
-        load_words("g", wg_words, 0)
+        load_wg(0)
         load_scales(nc.sync, "g", wg_scales)
         load_r(1, 0, 2)
         load_r(1, 2, 4)
-        load_words("g", wg_words, 1)
+        load_wg(1)
         nc.sync.dma_start(out=u_sb[:], in_=u.rearrange("(g p j) -> p g j", p=128, j=4))
         nc.gpsimd.dma_start(out=bg_rows[0:8, :], in_=bg.rearrange("(a p) -> a p", p=128))
         nc.gpsimd.dma_start(out=v_sb[:], in_=v.rearrange("(g p j) -> p g j", p=128, j=4))
         nc.gpsimd.tensor_scalar(out=nv[:], in0=v_sb[:], scalar1=-1.0 / 32, scalar2=0.0, op0=MULT, op1=ADD)
         nc.scalar.activation(out=warm[:], in_=zero[:, 0:1], func=ACT.Tanh)
-        warm_pe(3)
+        warm_pe(4)
 
         def om(g, j, nh):
             omM(g, j, nh)
@@ -388,24 +392,24 @@ def tile_adversarialsdfconditionalpricingmoments_x2_kernel(
         om(0, 1, 1)
         zS(1, 0)
         zS(1, 1)
+        dS(0, 0, "G")
+        dS(0, 1, "G")
         om(0, 2, 0)
-        sd(0, 0, 2)
         om(0, 2, 1)
         omM(0, 3, 0)
         omM(0, 3, 1)
         zTE(1, 0, 4)
-        dS(0, 0)
         omR(0, 3, 0)
         omR(0, 3, 1)
-        zQQ(1, 0, 2)
+        zQ(1, 0, 0, 2)
+        sd(0, 2, 4)
+        zQ(1, 1, 0, 2)
         wg(0, 0)
         wg(0, 1)
         omM(1, 0, 0)
         omM(1, 0, 1)
-        sd(0, 2, 4)
-        dS(0, 1)
-        zQQ(1, 2, 4)
         dS(0, 2)
+        zQQ(1, 2, 4)
         dS(0, 3)
         dII(0, 1, "G")
         omR(1, 0, 0)
@@ -413,6 +417,7 @@ def tile_adversarialsdfconditionalpricingmoments_x2_kernel(
         wg(0, 2)
         wg(0, 3)
         dII(0, 0, "S")
+        dS(1, 0, "G")
         om(1, 1, 0)
         om(1, 1, 1)
         for j in (2, 3):
@@ -420,56 +425,54 @@ def tile_adversarialsdfconditionalpricingmoments_x2_kernel(
             om(1, j, 1)
         for qt in range(4):
             wg(1, qt)
-        for qt in range(4):
-            fT(0, qt)
+        for g in range(2):
+            for qt in range(4):
+                fT(g, qt)
         dQ(0, 0, 512)
-        sd(1, 0, 4)
+        sd(1, 1, 4)
         dQ(0, 512, 1024)
-        for j in range(4):
+        for j in range(1, 4):
             dS(1, j)
-        wg(0, 4)
-        wg(0, 5)
-        dI(1, 0, 256, "S")
+        dII(1, 0, "S")
         dII(1, 1, "G")
-        for qt in range(4):
-            fU(0, qt)
-        wg(0, 6)
-        wg(0, 7)
-        dI(1, 256, 512, "S")
-        for qt in range(4):
-            fTU(1, qt)
-        for qt in range(4, 8):
-            wg(1, qt)
+        for g in range(2):
+            for qt in range(4):
+                fU(g, qt)
+        for g in range(2):
+            for qt in range(4, 8):
+                wg(g, qt)
         fQ(0, 0, 1)
         fQ(0, 1, 2)
         dQ(1, 0, 512)
         dQ(1, 512, 1024)
         for qt in range(4, 8):
             fTU(0, qt)
-        for it in range(2):
+        for it in range(4):
             out(0, it)
             pB(0, it, "G")
         for qt in range(4, 8):
             fTU(1, qt)
-        for it in range(2, 8):
-            out(0, it)
         pT(0, 0)
+        pE(0, 0, "S")
+        for it in range(4, 8):
+            out(0, it)
+        pT(0, 1)
         fQ(1, 0, 1)
         fQ(1, 1, 2)
-        pE(0, 0, "S")
-        for ip in range(1, 4):
-            pB2(0, ip)
+        pE(0, 1, "S")
+        pB2(0, 2)
+        pB2(0, 3)
         for it in range(6):
-            out(1, it, "SVSSSS"[it])
+            out(1, it, "SSSSSS"[it])
+            if it == 0:
+                pQ(0, 0, 512)
+                pW(0, 0, 512)
             if it in (2, 4):
                 pB2(1, it // 2 - 1)
-        for h, ip in ((0, 1), (0, 2), (0, 3), (1, 0), (1, 1)):
+        for h, ip in ((0, 2), (0, 3), (1, 0), (1, 1)):
             pT(h, ip)
-        pE(0, 1, "V")
-        pE(0, 2, "S")
+        pE(0, 2, "V")
         pB2(1, 2)
-        pQ(0, 0, 512)
-        pW(0, 0, 512)
         pE(0, 3, "S")
         pE(1, 0, "S")
         pE(1, 1, "S")
@@ -478,16 +481,18 @@ def tile_adversarialsdfconditionalpricingmoments_x2_kernel(
         pS(0, [nc.sync])
         pM(1, 6)
         pM(1, 7)
-        pD(1, 6, "S")
+        pD(1, 6, "V")
         pT(1, 2)
         pQ(1, 0, 512)
         pW(1, 0, 512)
         pD(1, 7, "S")
-        pE(1, 2, "V")
+        pE(1, 2, "S")
         outM(1, 6)
         outM(1, 7)
+        pQ(1, 768, 1024)
+        pW(1, 768, 1024)
         outE(1, 6)
+        pQ(1, 512, 768)
+        pW(1, 512, 768)
+        pS(1, [nc.sync])
         outE(1, 7)
-        pQ(1, 512, 1024)
-        pW(1, 512, 1024)
-        pS(1, [nc.sync, nc.scalar])

@@ -392,24 +392,24 @@ def tile_adversarialsdfconditionalpricingmoments_x2_kernel(
         om(0, 1, 1)
         zS(1, 0)
         zS(1, 1)
-        dS(0, 0, "G")
-        dS(0, 1, "G")
         om(0, 2, 0)
+        sd(0, 0, 2)
         om(0, 2, 1)
         omM(0, 3, 0)
         omM(0, 3, 1)
         zTE(1, 0, 4)
+        dS(0, 0)
         omR(0, 3, 0)
         omR(0, 3, 1)
-        zQ(1, 0, 0, 2)
-        sd(0, 2, 4)
-        zQ(1, 1, 0, 2)
+        zQQ(1, 0, 2)
         wg(0, 0)
         wg(0, 1)
         omM(1, 0, 0)
         omM(1, 0, 1)
-        dS(0, 2)
+        sd(0, 2, 4)
+        dS(0, 1)
         zQQ(1, 2, 4)
+        dS(0, 2)
         dS(0, 3)
         dII(0, 1, "G")
         omR(1, 0, 0)
@@ -417,7 +417,6 @@ def tile_adversarialsdfconditionalpricingmoments_x2_kernel(
         wg(0, 2)
         wg(0, 3)
         dII(0, 0, "S")
-        dS(1, 0, "G")
         om(1, 1, 0)
         om(1, 1, 1)
         for j in (2, 3):
@@ -425,22 +424,26 @@ def tile_adversarialsdfconditionalpricingmoments_x2_kernel(
             om(1, j, 1)
         for qt in range(4):
             wg(1, qt)
-        for g in range(2):
-            for qt in range(4):
-                fT(g, qt)
+        for qt in range(4):
+            fT(0, qt)
         dQ(0, 0, 512)
-        sd(1, 1, 4)
+        sd(1, 0, 4)
         dQ(0, 512, 1024)
-        for j in range(1, 4):
+        for j in range(4):
             dS(1, j)
-        dII(1, 0, "S")
+        wg(0, 4)
+        wg(0, 5)
+        dI(1, 0, 256, "S")
         dII(1, 1, "G")
-        for g in range(2):
-            for qt in range(4):
-                fU(g, qt)
-        for g in range(2):
-            for qt in range(4, 8):
-                wg(g, qt)
+        for qt in range(4):
+            fU(0, qt)
+        wg(0, 6)
+        wg(0, 7)
+        dI(1, 256, 512, "S")
+        for qt in range(4):
+            fTU(1, qt)
+        for qt in range(4, 8):
+            wg(1, qt)
         fQ(0, 0, 1)
         fQ(0, 1, 2)
         dQ(1, 0, 512)
@@ -452,14 +455,14 @@ def tile_adversarialsdfconditionalpricingmoments_x2_kernel(
             pB(0, it, "G")
         for qt in range(4, 8):
             fTU(1, qt)
-        pT(0, 0)
-        pE(0, 0, "S")
         for it in range(4, 8):
             out(0, it)
+        pT(0, 0)
         pT(0, 1)
         fQ(1, 0, 1)
         fQ(1, 1, 2)
-        pE(0, 1, "S")
+        pE(0, 0, "S")
+        pE(0, 1, "V")
         pB2(0, 2)
         pB2(0, 3)
         for it in range(6):

@@ -15,7 +15,9 @@ MULT = mybir.AluOpType.mult
 ACT = mybir.ActivationFunctionType
 
 T, D, N, Q = 1024, 1024, 1024, 1024
-THB, OSB = 12, 5
+ROOT = 32.0
+TANH_BUFS = 12
+OUT_BUFS = 5
 FLOPS = 3 * 2 * 1024 * 1024 * 1024
 
 
@@ -23,323 +25,308 @@ def tile_adversarialsdfconditionalpricingmoments_x2_kernel(
     tc, z, wo_words, wo_scales, wg_words, wg_scales, bg, r, v, u, out_0, out_1, out_2
 ):
     nc = tc.nc
+    scalar, vector, gpsimd = nc.scalar, nc.vector, nc.gpsimd
     with ExitStack() as ctx:
         keep = ctx.enter_context(tc.tile_pool(name="keep", bufs=1))
         work = ctx.enter_context(tc.tile_pool(name="work", bufs=4))
         psum = ctx.enter_context(tc.psum_pool(name="psum", bufs=8))
         ctx.enter_context(tc.manual_schedule())
 
-        def kt(name, shape, dtype):
+        def kept(name, shape, dtype):
             return keep.tile(shape, dtype, name=name, align_bytes=64)
-
-        ident = kt("ident", [128, 128], F32)
-        z_sb, r_sb = {}, {}
-        wo_sb = kt("wo", [128, 2, 2048], U8)
-        wg_sb = [kt("wg%d" % a, [128, 2, 1024], U8) for a in range(2)]
-        ws_sb = {k: kt("ws" + k, [128, 2, N], U8) for k in "og"}
-        bg_rows = kt("bg_rows", [128, 128], BF16)
-        bg_t = kt("bg_t", [128, 8], F32)
-        v_sb = kt("v", [128, 2, 4], BF16)
-        nv = kt("nv", [128, 2, 4], F32)
-        u_sb = kt("u", [128, 2, 4], BF16)
-        zero = kt("zero", [128, 512], BF16)
-        warm = kt("warm", [128, 1], F32)
-        eye = kt("eye", [128, 8], BF16)
-        zin = [[kt("zin%d%d" % (g, a), [128, 2, 256, 4], BF16) for a in range(2)] for g in range(2)]
-        zc = [[kt("zc%d%d" % (g, h), [128, 512], U32) for h in range(2)] for g in range(2)]
-        zs = [[kt("zs%d%d" % (g, h), [128, 512], U8) for h in range(2)] for g in range(2)]
-        fin = [kt("fin%d" % h, [128, 2, 512, 4], BF16) for h in range(2)]
-        fc = [kt("fc%d" % h, [128, 2, 512], U32) for h in range(2)]
-        fs = [kt("fs%d" % h, [128, 2, 512], U8) for h in range(2)]
-        dsc = [kt("dsc%d" % g, [128, 4, N], BF16) for g in range(2)]
-        din = [kt("din%d" % g, [128, N, 4], BF16) for g in range(2)]
-        dc = [kt("dc%d" % g, [128, N], U32) for g in range(2)]
-        ds = [kt("ds%d" % g, [128, N], U8) for g in range(2)]
-        acc = [kt("acc%d" % g, [128, 4, 2], F32) for g in range(2)]
-        sm = {}
-        ob = [[kt("ob%d%d" % (h, ip), [128, 2, 512], BF16) for ip in range(4)] for h in range(2)]
-        pin = [kt("pin%d" % h, [128, N, 4], BF16) for h in range(2)]
-        pc = [kt("pc%d" % h, [128, N], U32) for h in range(2)]
-        ps = [kt("ps%d" % h, [128, N], U8) for h in range(2)]
-        hold = {}
-
-        def copy(eng, o, i):
-            if eng == "S":
-                nc.scalar.copy(out=o, in_=i)
-            elif eng == "V":
-                nc.vector.tensor_copy(out=o, in_=i)
-            else:
-                nc.gpsimd.tensor_scalar(out=o, in0=i, scalar1=1.0, scalar2=0.0, op0=MULT, op1=ADD)
-
-        def scale(eng, o, i):
-            if eng == "S":
-                nc.scalar.mul(out=o, in_=i, mul=1.0 / 32)
-            else:
-                nc.vector.tensor_scalar(out=o, in0=i, scalar1=1.0 / 32, scalar2=None, op0=MULT)
-
-        def load_rows(tiles, name, src, g, j0, j1):
-            t = kt("%s%d%d" % (name, g, j0), [128, j1 - j0, 1024], BF16)
-            nc.sync.dma_start(out=t[:], in_=src[512 * g : 512 * (g + 1), :].rearrange("(p j) d -> p j d", j=4)[:, j0:j1, :])
-            for j in range(j0, j1):
-                tiles[g, j] = t[:, j - j0, :]
-
-        def load_z(g, j0, j1):
-            load_rows(z_sb, "z", z, g, j0, j1)
-
-        def load_r(g, j0, j1):
-            load_rows(r_sb, "r", r, g, j0, j1)
-
-        def load_scales(eng, k, src):
-            for b in range(4):
-                eng.dma_start(
-                    out=ws_sb[k][32 * b : 32 * b + 4, :, :].bitcast(I32),
-                    in_=src[:, 4 * b : 4 * b + 4, :].rearrange("g q n -> q g n").bitcast(I32),
-                )
-
-        def load_wg(a):
-            nc.sync.dma_start(
-                out=wg_sb[a][:].bitcast(I32), in_=wg_words.rearrange("g p n -> p g n")[:, :, 1024 * a : 1024 * (a + 1)].bitcast(I32)
-            )
 
         def bank(shape):
             return psum.tile(shape, F32, name="bank", tag="bank")
 
-        def zS(g, j):
-            t = work.tile([128, 2, 2, 128], U32, name="zsort", bufs=2)
-            nc.scalar.copy(out=t[:], in_=z_sb[g, j].bitcast(U32).rearrange("p (h c e) -> p h e c", h=2, e=2))
-            hold["zs", g, j] = t
+        ident = kept("ident", [128, 128], F32)
+        z_rows, r_rows = {}, {}
+        wo_sb = kept("wo", [128, 2, 2048], U8)
+        wg_sb = [kept("wg%d" % qh, [128, 2, 1024], U8) for qh in range(2)]
+        w_scale = {name: kept("ws" + name, [128, 2, N], U8) for name in "og"}
+        bg_rows = kept("bg_rows", [128, 128], BF16)
+        bg_cols = kept("bg_t", [128, 8], F32)
+        v_sb = kept("v", [128, 2, 4], BF16)
+        neg_v = kept("nv", [128, 2, 4], F32)
+        u_sb = kept("u", [128, 2, 4], BF16)
+        zero = kept("zero", [128, 512], BF16)
+        warm = kept("warm", [128, 1], F32)
+        eye = kept("eye", [128, 8], BF16)
+        z_in = [[kept("zin%d%d" % (g, jp), [128, 2, 256, 4], BF16) for jp in range(2)] for g in range(2)]
+        z_code = [[kept("zc%d%d" % (g, kg), [128, 512], U32) for kg in range(2)] for g in range(2)]
+        z_scale = [[kept("zs%d%d" % (g, kg), [128, 512], U8) for kg in range(2)] for g in range(2)]
+        f_in = [kept("fin%d" % qh, [128, 2, 512, 4], BF16) for qh in range(2)]
+        f_code = [kept("fc%d" % qh, [128, 2, 512], U32) for qh in range(2)]
+        f_scale = [kept("fs%d" % qh, [128, 2, 512], U8) for qh in range(2)]
+        d_rows = [kept("dsc%d" % g, [128, 4, N], BF16) for g in range(2)]
+        d_in = [kept("din%d" % g, [128, N, 4], BF16) for g in range(2)]
+        d_code = [kept("dc%d" % g, [128, N], U32) for g in range(2)]
+        d_scale = [kept("ds%d" % g, [128, N], U8) for g in range(2)]
+        sums = [kept("acc%d" % g, [128, 4, 2], F32) for g in range(2)]
+        neg_sdf = {}
+        out_bf = [[kept("ob%d%d" % (qh, ip), [128, 2, 512], BF16) for ip in range(4 - qh)] for qh in range(2)]
+        p_in = [kept("pin%d" % qh, [128, N, 4], BF16) for qh in range(2)]
+        p_code = [kept("pc%d" % qh, [128, N], U32) for qh in range(2)]
+        p_scale = [kept("ps%d" % qh, [128, N], U8) for qh in range(2)]
+        held = {}
 
-        def zT(g, j):
-            t = bank([128, 2, 2, 128])
-            w = z_sb[g, j].bitcast(F32)
-            for h in range(2):
-                for e in range(2):
-                    if ("zs", g, j) in hold:
-                        src = hold["zs", g, j][:, h, e, :].bitcast(F32)
-                    else:
-                        src = w[:, 256 * h + e : 256 * (h + 1) : 2]
-                    nc.tensor.transpose(t[:, h, e, :], src, ident[:])
-            hold["z", g, j] = t
+        def copy(eng, dst, src):
+            if eng is scalar:
+                scalar.copy(out=dst, in_=src)
+            elif eng is vector:
+                vector.tensor_copy(out=dst, in_=src)
+            else:
+                gpsimd.tensor_scalar(out=dst, in0=src, scalar1=1.0, scalar2=0.0, op0=MULT, op1=ADD)
 
-        def warm_pe(n):
-            for k in range(n):
+        def quantise(code, scale, src):
+            vector.quantize_mx(out=code.bitcast(E4M3), scales=scale, in_=src.rearrange("p c k -> p (c k)"))
+
+        def product(dst, passes):
+            for n, (lhs, lhs_scale, rhs, rhs_scale) in enumerate(passes):
+                nc.tensor.matmul_mx(
+                    out=dst, lhsT=lhs, lhsT_scale=lhs_scale, rhs=rhs, rhs_scale=rhs_scale, start=n == 0, stop=n == 1
+                )
+
+        def load_rows(rows, name, src, g, j0, j1):
+            t = kept("%s%d%d" % (name, g, j0), [128, j1 - j0, 1024], BF16)
+            group = src[512 * g : 512 * (g + 1), :].rearrange("(p j) d -> p j d", j=4)
+            nc.sync.dma_start(out=t[:], in_=group[:, j0:j1, :])
+            for j in range(j0, j1):
+                rows[g, j] = t[:, j - j0, :]
+
+        def load_z(g, j0, j1):
+            load_rows(z_rows, "z", z, g, j0, j1)
+
+        def load_r(g, j0, j1):
+            load_rows(r_rows, "r", r, g, j0, j1)
+
+        def load_scales(queue, name, src):
+            for c in range(4):
+                queue.dma_start(
+                    out=w_scale[name][32 * c : 32 * c + 4, :, :].bitcast(I32),
+                    in_=src[:, 4 * c : 4 * c + 4, :].rearrange("g q n -> q g n").bitcast(I32),
+                )
+
+        def load_wg(qh):
+            half = wg_words.rearrange("g p n -> p g n")[:, :, 1024 * qh : 1024 * (qh + 1)]
+            nc.sync.dma_start(out=wg_sb[qh][:].bitcast(I32), in_=half.bitcast(I32))
+
+        def zero_scales(eng, name):
+            eng.memset(w_scale[name][:].rearrange("p g n -> p (g n)").bitcast(I32), 0)
+
+        def warm_tensor(n):
+            for _ in range(n):
                 t = bank([128, 512])
                 nc.tensor.matmul(t[:], zero[:, 0:128], zero[:], start=True, stop=True)
 
-        def zE(g, j, eng="S"):
-            w = zin[g][j // 2][:].rearrange("p h c k -> p (h c k)").bitcast(F32).rearrange("p (h a c e) -> p h a c e", h=2, a=2, e=2)
-            copy(eng, w[:, :, j % 2, :, :], hold["z", g, j][:].rearrange("p h e c -> p h c e"))
+        def z_sort(g, j):
+            t = work.tile([128, 2, 2, 128], U32, name="zsort", bufs=2)
+            scalar.copy(out=t[:], in_=z_rows[g, j].bitcast(U32).rearrange("p (h c e) -> p h e c", h=2, e=2))
+            held["sorted", g, j] = t
 
-        def zQ(g, h, j0, j1):
-            c = slice(128 * j0, 128 * j1)
-            nc.vector.quantize_mx(
-                out=zc[g][h][:, c].bitcast(E4M3),
-                scales=zs[g][h][:, c],
-                in_=zin[g][j0 // 2][:, h, 128 * (j0 % 2) : 128 * (j0 % 2 + j1 - j0), :].rearrange("p c k -> p (c k)"),
-            )
+        def z_turn(g, j0, j1):
+            for j in range(j0, j1):
+                t = bank([128, 2, 2, 128])
+                words = z_rows[g, j].bitcast(F32)
+                for kg in range(2):
+                    for e in range(2):
+                        if ("sorted", g, j) in held:
+                            src = held["sorted", g, j][:, kg, e, :].bitcast(F32)
+                        else:
+                            src = words[:, 256 * kg + e : 256 * (kg + 1) : 2]
+                        nc.tensor.transpose(t[:, kg, e, :], src, ident[:])
+                dst = z_in[g][j // 2][:].rearrange("p h c k -> p (h c k)").bitcast(F32)
+                dst = dst.rearrange("p (h a c e) -> p h a c e", h=2, a=2, e=2)
+                scalar.copy(out=dst[:, :, j % 2, :, :], in_=t[:].rearrange("p h e c -> p h c e"))
 
-        def bgT():
-            nc.scalar.copy(out=eye[:], in_=ident[:, 0:8])
-            t = bank([128, 8])
-            nc.tensor.matmul(t[:], bg_rows[:], eye[:], start=True, stop=True)
-            nc.scalar.copy(out=bg_t[:], in_=t[:])
+        def z_quantise(g, j0, j1):
+            cols = slice(128 * j0, 128 * j1)
+            for kg in range(2):
+                src = z_in[g][j0 // 2][:, kg, 128 * (j0 % 2) : 128 * (j0 % 2 + j1 - j0), :]
+                quantise(z_code[g][kg][:, cols], z_scale[g][kg][:, cols], src)
 
-        def omM(g, j, nh):
+        def om_product(g, j, ih):
             t = bank([128, 512])
-            for h in range(2):
-                nc.tensor.matmul_mx(
-                    out=t[:],
-                    lhsT=zc[g][h][:, 128 * j : 128 * (j + 1)].bitcast(E4M3),
-                    lhsT_scale=zs[g][h][:, 128 * j : 128 * (j + 1)],
-                    rhs=wo_sb[:, h, 1024 * nh : 1024 * (nh + 1)].bitcast(E2M1),
-                    rhs_scale=ws_sb["o"][:, h, 512 * nh : 512 * (nh + 1)],
-                    start=h == 0,
-                    stop=h == 1,
-                )
-            hold["o", g, j, nh] = t
+            cols = slice(128 * j, 128 * (j + 1))
+            product(
+                t[:],
+                [
+                    (
+                        z_code[g][kg][:, cols].bitcast(E4M3),
+                        z_scale[g][kg][:, cols],
+                        wo_sb[:, kg, 1024 * ih : 1024 * (ih + 1)].bitcast(E2M1),
+                        w_scale["o"][:, kg, 512 * ih : 512 * (ih + 1)],
+                    )
+                    for kg in range(2)
+                ],
+            )
+            held["om", g, j, ih] = t
 
-        def omR(g, j, nh):
-            junk = work.tile([128, 512], F32, name="junk", bufs=2)
-            nc.vector.scalar_tensor_tensor(
-                out=junk[:],
-                in0=hold["o", g, j, nh][:],
+        def om_sum(g, j, ih):
+            prod = work.tile([128, 512], F32, name="junk", bufs=2)
+            vector.scalar_tensor_tensor(
+                out=prod[:],
+                in0=held["om", g, j, ih][:],
                 scalar=1.0,
-                in1=r_sb[g, j][:, 512 * nh : 512 * (nh + 1)],
+                in1=r_rows[g, j][:, 512 * ih : 512 * (ih + 1)],
                 op0=MULT,
                 op1=MULT,
-                accum_out=acc[g][:, j, nh : nh + 1],
+                accum_out=sums[g][:, j, ih : ih + 1],
             )
 
-        def sd(g, j0, j1):
-            t = kt("sm%d%d" % (g, j0), [128, j1 - j0], F32)
-            nc.vector.scalar_tensor_tensor(
-                out=t[:], in0=acc[g][:, j0:j1, 0], scalar=-32.0, in1=acc[g][:, j0:j1, 1], op0=ADD, op1=ADD
+        def om(g, j, ih):
+            om_product(g, j, ih)
+            om_sum(g, j, ih)
+
+        def sdf(g, j0, j1):
+            t = kept("sm%d%d" % (g, j0), [128, j1 - j0], F32)
+            vector.scalar_tensor_tensor(
+                out=t[:], in0=sums[g][:, j0:j1, 0], scalar=-ROOT, in1=sums[g][:, j0:j1, 1], op0=ADD, op1=ADD
             )
             for j in range(j0, j1):
-                sm[g, j] = t[:, j - j0 : j - j0 + 1]
+                neg_sdf[g, j] = t[:, j - j0 : j - j0 + 1]
 
-        def dS(g, j, eng="V"):
-            if eng == "G":
-                t = kt("sm%d%d" % (g, j), [128, 1], F32)
-                nc.gpsimd.tensor_scalar(
-                    out=t[:], in0=acc[g][:, j, 0:1], scalar1=acc[g][:, j, 1:2], scalar2=-32.0, op0=ADD, op1=ADD
-                )
-                sm[g, j] = t[:]
-            (nc.gpsimd if eng == "G" else nc.vector).tensor_scalar(
-                out=dsc[g][:, j, :], in0=r_sb[g, j], scalar1=sm[g, j], scalar2=nv[:, g, j : j + 1], op0=MULT, op1=MULT
+        def d_scale_rows(g, j):
+            vector.tensor_scalar(
+                out=d_rows[g][:, j, :],
+                in0=r_rows[g, j],
+                scalar1=neg_sdf[g, j],
+                scalar2=neg_v[:, g, j : j + 1],
+                op0=MULT,
+                op1=MULT,
             )
 
-        def dI(g, c0, c1, eng="S"):
-            copy(eng, din[g][:, c0:c1, :], dsc[g][:, :, c0:c1].rearrange("p j c -> p c j"))
+        def d_interleave(eng, g, quarter):
+            cols = slice(256 * quarter, 256 * (quarter + 1))
+            copy(eng, d_in[g][:, cols, :], d_rows[g][:, :, cols].rearrange("p j c -> p c j"))
 
-        def dQ(g, c0, c1):
-            nc.vector.quantize_mx(
-                out=dc[g][:, c0:c1].bitcast(E4M3), scales=ds[g][:, c0:c1], in_=din[g][:, c0:c1, :].rearrange("p c k -> p (c k)")
+        def d_quantise(g, ih):
+            cols = slice(512 * ih, 512 * (ih + 1))
+            quantise(d_code[g][:, cols], d_scale[g][:, cols], d_in[g][:, cols, :])
+
+        def bias_columns():
+            scalar.copy(out=eye[:], in_=ident[:, 0:8])
+            t = bank([128, 8])
+            nc.tensor.matmul(t[:], bg_rows[:], eye[:], start=True, stop=True)
+            scalar.copy(out=bg_cols[:], in_=t[:])
+
+        def instrument(g, qt):
+            x = bank([128, 512])
+            product(
+                x[:],
+                [
+                    (
+                        wg_sb[qt // 4][:, kg, 256 * (qt % 4) : 256 * (qt % 4 + 1)].bitcast(E2M1),
+                        w_scale["g"][:, kg, 128 * qt : 128 * (qt + 1)],
+                        z_code[g][kg][:].bitcast(E4M3),
+                        z_scale[g][kg][:],
+                    )
+                    for kg in range(2)
+                ],
             )
+            t = work.tile([128, 512], F32, name="th", bufs=TANH_BUFS)
+            scalar.activation(out=t[:], in_=x[:], func=ACT.Tanh, bias=bg_cols[:, qt : qt + 1])
+            held["tanh", g, qt] = t
 
-        def wgM(g, qt):
-            t = bank([128, 512])
-            for h in range(2):
-                nc.tensor.matmul_mx(
-                    out=t[:],
-                    lhsT=wg_sb[qt // 4][:, h, 256 * (qt % 4) : 256 * (qt % 4 + 1)].bitcast(E2M1),
-                    lhsT_scale=ws_sb["g"][:, h, 128 * qt : 128 * (qt + 1)],
-                    rhs=zc[g][h][:].bitcast(E4M3),
-                    rhs_scale=zs[g][h][:],
-                    start=h == 0,
-                    stop=h == 1,
-                )
-            hold["x", g, qt] = t
-
-        def tanh(g, qt):
-            t = work.tile([128, 512], F32, name="th", bufs=THB)
-            nc.scalar.activation(out=t[:], in_=hold["x", g, qt][:], func=ACT.Tanh, bias=bg_t[:, qt : qt + 1])
-            hold["t", g, qt] = t
-
-        def wg(g, qt):
-            wgM(g, qt)
-            tanh(g, qt)
-
-        def fT(g, qt):
+        def f_turn(g, qt):
             t = bank([128, 4, 128])
             for j in range(4):
-                nc.tensor.transpose(t[:, j, :], hold["t", g, qt][:, 128 * j : 128 * (j + 1)], ident[:])
-            hold["f", g, qt] = t
+                nc.tensor.transpose(t[:, j, :], held["tanh", g, qt][:, 128 * j : 128 * (j + 1)], ident[:])
+            held["f", g, qt] = t
 
-        def fU(g, qt):
-            cols = fin[qt // 4][:, g, :, :]
-            if qt < 4:
-                cols = cols.rearrange("p (m s) j -> p m s j", s=4)
-            else:
-                cols = cols.rearrange("p (s m) j -> p m s j", s=4)
-            nc.vector.tensor_tensor(
+        def f_order(qh):
+            return ("(m s)", "(s m)")[qh]
+
+        def f_weigh(g, qt):
+            cols = f_in[qt // 4][:, g, :, :].rearrange("p %s j -> p m s j" % f_order(qt // 4), s=4)
+            vector.tensor_tensor(
                 out=cols[:, 32 * (qt % 4) : 32 * (qt % 4 + 1), :, :],
-                in0=hold["f", g, qt][:].rearrange("p j (m s) -> p m s j", s=4),
+                in0=held["f", g, qt][:].rearrange("p j (m s) -> p m s j", s=4),
                 in1=u_sb[:, g, :].unsqueeze(1).unsqueeze(1).to_broadcast([128, 32, 4, 4]),
                 op=MULT,
             )
 
-        def fQ(h, g0=0, g1=2):
-            nc.vector.quantize_mx(
-                out=fc[h][:, g0:g1, :].rearrange("p g c -> p (g c)").bitcast(E4M3),
-                scales=fs[h][:, g0:g1, :].rearrange("p g c -> p (g c)"),
-                in_=fin[h][:, g0:g1, :, :].rearrange("p g c k -> p (g c k)"),
-            )
-
-        def outM(h, it):
-            t = bank([128, 512])
-            i = slice(128 * it, 128 * (it + 1))
+        def f_quantise(qh):
             for g in range(2):
-                nc.tensor.matmul_mx(
-                    out=t[:],
-                    lhsT=dc[g][:, i].bitcast(E4M3),
-                    lhsT_scale=ds[g][:, i],
-                    rhs=fc[h][:, g, :].bitcast(E4M3),
-                    rhs_scale=fs[h][:, g, :],
-                    start=g == 0,
-                    stop=g == 1,
-                )
-            hold["out", h, it] = t
+                quantise(f_code[qh][:, g, :], f_scale[qh][:, g, :], f_in[qh][:, g, :, :])
 
-        def outE(h, it, eng="S"):
+        def d_operand(g, it):
+            cols = slice(128 * it, 128 * (it + 1))
+            return d_code[g][:, cols].bitcast(E4M3), d_scale[g][:, cols]
+
+        def out_product(qh, it):
+            t = bank([128, 512])
+            product(t[:], [(*d_operand(g, it), f_code[qh][:, g, :].bitcast(E4M3), f_scale[qh][:, g, :]) for g in range(2)])
+            held["out", qh, it] = t
+
+        def out_store(qh, it):
             if it % 2 == 0:
-                hold["os", h, it // 2] = work.tile([128, 2, 512], F32, name="osb", bufs=OSB)
-            t = hold["os", h, it // 2][:, it % 2, :]
-            scale(eng, t.rearrange("p (m s) -> p m s", s=4), hold["out", h, it][:].rearrange(("p (m s) -> p m s", "p (s m) -> p m s")[h], s=4))
-            nc.sync.dma_start(out=out_0[128 * it : 128 * (it + 1), 512 * h : 512 * (h + 1)], in_=t)
+                held["sb", qh, it // 2] = work.tile([128, 2, 512], F32, name="osb", bufs=OUT_BUFS)
+            t = held["sb", qh, it // 2][:, it % 2, :]
+            src = held["out", qh, it][:].rearrange("p %s -> p m s" % f_order(qh), s=4)
+            scalar.mul(out=t.rearrange("p (m s) -> p m s", s=4), in_=src, mul=1.0 / ROOT)
+            nc.sync.dma_start(out=out_0[128 * it : 128 * (it + 1), 512 * qh : 512 * (qh + 1)], in_=t)
 
-        def out(h, it, eng="S"):
-            outM(h, it)
-            outE(h, it, eng)
+        def out(qh, it):
+            out_product(qh, it)
+            out_store(qh, it)
 
-        def pB(h, it, eng="V"):
-            o = ob[h][it // 2][:, it % 2, :].rearrange("p (e c b) -> p e c b", e=2, b=2)
-            copy(eng, o, hold["os", h, it // 2][:, it % 2, :].rearrange("p (c e b) -> p e c b", e=2, b=2))
+        def round_pair(qh, ip):
+            dst = out_bf[qh][ip][:].rearrange("p k (e c b) -> p k e c b", e=2, b=2)
+            copy(vector, dst, held["sb", qh, ip][:].rearrange("p k (c e b) -> p k e c b", e=2, b=2))
 
-        def pB2(h, ip):
-            o = ob[h][ip][:].rearrange("p k (e c b) -> p k e c b", e=2, b=2)
-            copy("V", o, hold["os", h, ip][:].rearrange("p k (c e b) -> p k e c b", e=2, b=2))
-
-        def pT(h, ip):
+        def plane_turn(qh, ip):
             t = bank([128, 2, 256])
             for k in range(2):
-                w = ob[h][ip][:, k, :].bitcast(F32)
+                words = out_bf[qh][ip][:, k, :].bitcast(F32)
                 for e in range(2):
-                    nc.tensor.transpose(t[:, e, 128 * k : 128 * (k + 1)], w[:, 128 * e : 128 * (e + 1)], ident[:])
-            hold["pt", h, ip] = t
+                    nc.tensor.transpose(t[:, e, 128 * k : 128 * (k + 1)], words[:, 128 * e : 128 * (e + 1)], ident[:])
+            held["turned", qh, ip] = t
 
-        def pE(h, ip, eng="S"):
-            c = slice(256 * ip, 256 * (ip + 1))
-            o = pin[h][:, c, :].rearrange("p c k -> p (c k)").bitcast(F32).rearrange("p (c e) -> p c e", e=2)
-            copy(eng, o, hold["pt", h, ip][:].rearrange("p e c -> p c e"))
+        def plane_copy(eng, qh, ip):
+            dst = p_in[qh][:, 256 * ip : 256 * (ip + 1), :].rearrange("p c k -> p (c k)").bitcast(F32)
+            copy(eng, dst.rearrange("p (c e) -> p c e", e=2), held["turned", qh, ip][:].rearrange("p e c -> p c e"))
 
-        def pM(h, it):
+        def plane_product(it):
             t = bank([128, 4, 128])
-            i = slice(128 * it, 128 * (it + 1))
             for s in range(4):
-                c = slice(128 * s, 128 * (s + 1))
-                for g in range(2):
-                    nc.tensor.matmul_mx(
-                        out=t[:, s, :],
-                        lhsT=fc[h][:, g, c].bitcast(E4M3),
-                        lhsT_scale=fs[h][:, g, c],
-                        rhs=dc[g][:, i].bitcast(E4M3),
-                        rhs_scale=ds[g][:, i],
-                        start=g == 0,
-                        stop=g == 1,
-                    )
-            hold["pm", h, it] = t
+                cols = slice(128 * s, 128 * (s + 1))
+                product(
+                    t[:, s, :],
+                    [(f_code[1][:, g, cols].bitcast(E4M3), f_scale[1][:, g, cols], *d_operand(g, it)) for g in range(2)],
+                )
+            held["direct", it] = t
 
-        def pD(h, it, eng="V"):
-            scale(eng, pin[h][:, 128 * it : 128 * (it + 1), :], hold["pm", h, it][:].rearrange("p s c -> p c s"))
+        def plane_scale(eng, it):
+            dst, src = p_in[1][:, 128 * it : 128 * (it + 1), :], held["direct", it][:].rearrange("p s c -> p c s")
+            if eng is scalar:
+                scalar.mul(out=dst, in_=src, mul=1.0 / ROOT)
+            else:
+                vector.tensor_scalar(out=dst, in0=src, scalar1=1.0 / ROOT, scalar2=None, op0=MULT)
 
-        def pQ(h, c0, c1):
-            nc.vector.quantize_mx(
-                out=pc[h][:, c0:c1].bitcast(E4M3), scales=ps[h][:, c0:c1], in_=pin[h][:, c0:c1, :].rearrange("p c k -> p (c k)")
-            )
-
-        def pW(h, c0, c1):
+        def plane_quantise(qh, c0, c1):
+            quantise(p_code[qh][:, c0:c1], p_scale[qh][:, c0:c1], p_in[qh][:, c0:c1, :])
             nc.sync.dma_start(
-                out=out_1[h].rearrange("p m t -> p (m t)")[:, 4 * c0 : 4 * c1].bitcast(I32), in_=pc[h][:, c0:c1].bitcast(I32)
+                out=out_1[qh].rearrange("p m t -> p (m t)")[:, 4 * c0 : 4 * c1].bitcast(I32),
+                in_=p_code[qh][:, c0:c1].bitcast(I32),
             )
 
-        def pS(h, engs):
-            for b in range(4):
-                engs[b % len(engs)].dma_start(
-                    out=out_2[h, 4 * b : 4 * b + 4, :].bitcast(I32), in_=ps[h][32 * b : 32 * b + 4, :].bitcast(I32)
+        def plane_scales_store(qh):
+            for c in range(4):
+                nc.sync.dma_start(
+                    out=out_2[qh, 4 * c : 4 * c + 4, :].bitcast(I32), in_=p_scale[qh][32 * c : 32 * c + 4, :].bitcast(I32)
                 )
 
-        nc.vector.memset(zero[:], 0.0)
-        nc.vector.memset(ws_sb["o"][:].rearrange("p g n -> p (g n)").bitcast(I32), 0)
-        nc.vector.memset(ident[:], 0.0)
+        vector.memset(zero[:], 0.0)
+        zero_scales(vector, "o")
+        vector.memset(ident[:], 0.0)
         make_identity(nc, ident[:], nomemset=True)
-        nc.vector.memset(bg_rows[:], 0.0)
-        nc.vector.memset(ws_sb["g"][:].rearrange("p g n -> p (g n)").bitcast(I32), 0)
+        vector.memset(bg_rows[:], 0.0)
+        zero_scales(vector, "g")
         load_z(0, 0, 1)
         load_z(0, 1, 2)
         load_z(0, 2, 4)
         nc.sync.dma_start(out=wo_sb[:].bitcast(I32), in_=wo_words.rearrange("g p n -> p g n").bitcast(I32))
-        load_scales(nc.scalar, "o", wo_scales)
+        load_scales(scalar, "o", wo_scales)
         load_r(0, 0, 1)
         load_r(0, 1, 2)
         load_z(1, 0, 2)
@@ -351,151 +338,125 @@ def tile_adversarialsdfconditionalpricingmoments_x2_kernel(
         load_r(1, 2, 4)
         load_wg(1)
         nc.sync.dma_start(out=u_sb[:], in_=u.rearrange("(g p j) -> p g j", p=128, j=4))
-        nc.gpsimd.dma_start(out=bg_rows[0:8, :], in_=bg.rearrange("(a p) -> a p", p=128))
-        nc.gpsimd.dma_start(out=v_sb[:], in_=v.rearrange("(g p j) -> p g j", p=128, j=4))
-        nc.gpsimd.tensor_scalar(out=nv[:], in0=v_sb[:], scalar1=-1.0 / 32, scalar2=0.0, op0=MULT, op1=ADD)
-        nc.scalar.activation(out=warm[:], in_=zero[:, 0:1], func=ACT.Tanh)
-        warm_pe(4)
+        gpsimd.dma_start(out=bg_rows[0:8, :], in_=bg.rearrange("(a p) -> a p", p=128))
+        gpsimd.dma_start(out=v_sb[:], in_=v.rearrange("(g p j) -> p g j", p=128, j=4))
+        gpsimd.tensor_scalar(out=neg_v[:], in0=v_sb[:], scalar1=-1.0 / ROOT, scalar2=0.0, op0=MULT, op1=ADD)
+        scalar.activation(out=warm[:], in_=zero[:, 0:1], func=ACT.Tanh)
+        warm_tensor(4)
 
-        def om(g, j, nh):
-            omM(g, j, nh)
-            omR(g, j, nh)
-
-        def zTE(g, j0, j1):
-            for j in range(j0, j1):
-                zT(g, j)
-                zE(g, j)
-
-        def zQQ(g, j0, j1):
-            for h in range(2):
-                zQ(g, h, j0, j1)
-
-        def fTU(g, qt):
-            fT(g, qt)
-            fU(g, qt)
-
-        def dII(g, a, eng):
-            for k in (2 * a, 2 * a + 1):
-                dI(g, 256 * k, 256 * (k + 1), eng)
-
-        zTE(0, 0, 1)
-        zQQ(0, 0, 1)
-        zTE(0, 1, 2)
-        zQQ(0, 1, 2)
-        warm_pe(2)
-        zTE(0, 2, 4)
+        for j in range(2):
+            z_turn(0, j, j + 1)
+            z_quantise(0, j, j + 1)
+        warm_tensor(2)
+        z_turn(0, 2, 4)
         om(0, 0, 0)
-        zQQ(0, 2, 4)
+        z_quantise(0, 2, 4)
         om(0, 0, 1)
-        bgT()
+        bias_columns()
         om(0, 1, 0)
         om(0, 1, 1)
-        zS(1, 0)
-        zS(1, 1)
+        z_sort(1, 0)
+        z_sort(1, 1)
         om(0, 2, 0)
-        sd(0, 0, 2)
+        sdf(0, 0, 2)
         om(0, 2, 1)
-        omM(0, 3, 0)
-        omM(0, 3, 1)
-        zTE(1, 0, 4)
-        dS(0, 0)
-        omR(0, 3, 0)
-        omR(0, 3, 1)
-        zQQ(1, 0, 2)
-        wg(0, 0)
-        wg(0, 1)
-        omM(1, 0, 0)
-        omM(1, 0, 1)
-        sd(0, 2, 4)
-        dS(0, 1)
-        zQQ(1, 2, 4)
-        dS(0, 2)
-        dS(0, 3)
-        dII(0, 1, "G")
-        omR(1, 0, 0)
-        omR(1, 0, 1)
-        wg(0, 2)
-        wg(0, 3)
-        dII(0, 0, "S")
-        om(1, 1, 0)
-        om(1, 1, 1)
-        for j in (2, 3):
+        om_product(0, 3, 0)
+        om_product(0, 3, 1)
+        z_turn(1, 0, 4)
+        d_scale_rows(0, 0)
+        om_sum(0, 3, 0)
+        om_sum(0, 3, 1)
+        z_quantise(1, 0, 2)
+        instrument(0, 0)
+        instrument(0, 1)
+
+        om_product(1, 0, 0)
+        om_product(1, 0, 1)
+        sdf(0, 2, 4)
+        d_scale_rows(0, 1)
+        z_quantise(1, 2, 4)
+        d_scale_rows(0, 2)
+        d_scale_rows(0, 3)
+        d_interleave(gpsimd, 0, 2)
+        d_interleave(gpsimd, 0, 3)
+        om_sum(1, 0, 0)
+        om_sum(1, 0, 1)
+        instrument(0, 2)
+        instrument(0, 3)
+        d_interleave(scalar, 0, 0)
+        d_interleave(scalar, 0, 1)
+        for j in range(1, 4):
             om(1, j, 0)
             om(1, j, 1)
+
         for qt in range(4):
-            wg(1, qt)
-        for qt in range(4):
-            fT(0, qt)
-        dQ(0, 0, 512)
-        sd(1, 0, 4)
-        dQ(0, 512, 1024)
+            instrument(1, qt)
+        for g in range(2):
+            for qt in range(4):
+                f_turn(g, qt)
+        d_quantise(0, 0)
+        sdf(1, 0, 4)
+        d_quantise(0, 1)
         for j in range(4):
-            dS(1, j)
-        wg(0, 4)
-        wg(0, 5)
-        dI(1, 0, 256, "S")
-        dII(1, 1, "G")
-        for qt in range(4):
-            fU(0, qt)
-        wg(0, 6)
-        wg(0, 7)
-        dI(1, 256, 512, "S")
-        for qt in range(4):
-            fTU(1, qt)
-        for qt in range(4, 8):
-            wg(1, qt)
-        fQ(0, 0, 1)
-        fQ(0, 1, 2)
-        dQ(1, 0, 512)
-        dQ(1, 512, 1024)
-        for qt in range(4, 8):
-            fTU(0, qt)
-        for it in range(4):
+            d_scale_rows(1, j)
+        d_interleave(scalar, 1, 0)
+        d_interleave(scalar, 1, 1)
+        d_interleave(gpsimd, 1, 2)
+        d_interleave(gpsimd, 1, 3)
+        for g in range(2):
+            for qt in range(4):
+                f_weigh(g, qt)
+        for g in range(2):
+            for qt in range(4, 8):
+                instrument(g, qt)
+        f_quantise(0)
+        d_quantise(1, 0)
+        d_quantise(1, 1)
+
+        for g in range(2):
+            for qt in range(4, 8):
+                f_turn(g, qt)
+                f_weigh(g, qt)
+        for it in range(8):
             out(0, it)
-            pB(0, it, "G")
-        for qt in range(4, 8):
-            fTU(1, qt)
-        for it in range(4, 8):
-            out(0, it)
-        pT(0, 0)
-        pT(0, 1)
-        fQ(1, 0, 1)
-        fQ(1, 1, 2)
-        pE(0, 0, "S")
-        pE(0, 1, "V")
-        pB2(0, 2)
-        pB2(0, 3)
-        for it in range(6):
-            out(1, it, "SSSSSS"[it])
-            if it == 0:
-                pQ(0, 0, 512)
-                pW(0, 0, 512)
-            if it in (2, 4):
-                pB2(1, it // 2 - 1)
-        for h, ip in ((0, 2), (0, 3), (1, 0), (1, 1)):
-            pT(h, ip)
-        pE(0, 2, "V")
-        pB2(1, 2)
-        pE(0, 3, "S")
-        pE(1, 0, "S")
-        pE(1, 1, "S")
-        pQ(0, 512, 1024)
-        pW(0, 512, 1024)
-        pS(0, [nc.sync])
-        pM(1, 6)
-        pM(1, 7)
-        pD(1, 6, "V")
-        pT(1, 2)
-        pQ(1, 0, 512)
-        pW(1, 0, 512)
-        pD(1, 7, "S")
-        pE(1, 2, "S")
-        outM(1, 6)
-        outM(1, 7)
-        pQ(1, 768, 1024)
-        pW(1, 768, 1024)
-        outE(1, 6)
-        pQ(1, 512, 768)
-        pW(1, 512, 768)
-        pS(1, [nc.sync])
-        outE(1, 7)
+        f_quantise(1)
+
+        for ip in range(3):
+            round_pair(0, ip)
+        out(1, 0)
+        out(1, 1)
+        plane_turn(0, 0)
+        plane_turn(0, 1)
+        round_pair(0, 3)
+        plane_copy(vector, 0, 0)
+        plane_copy(scalar, 0, 1)
+        round_pair(1, 0)
+        out(1, 2)
+        plane_quantise(0, 0, 512)
+        out(1, 3)
+        out(1, 4)
+        round_pair(1, 1)
+        out(1, 5)
+        for qh, ip in ((0, 2), (0, 3), (1, 0), (1, 1)):
+            plane_turn(qh, ip)
+        plane_copy(vector, 0, 2)
+        round_pair(1, 2)
+        plane_copy(scalar, 0, 3)
+        plane_copy(scalar, 1, 0)
+        plane_copy(scalar, 1, 1)
+        plane_quantise(0, 512, 1024)
+        plane_scales_store(0)
+        plane_product(6)
+        plane_product(7)
+        plane_scale(vector, 6)
+        plane_turn(1, 2)
+        plane_quantise(1, 0, 512)
+        plane_scale(scalar, 7)
+        plane_copy(scalar, 1, 2)
+        out_product(1, 6)
+        out_product(1, 7)
+        plane_quantise(1, 768, 1024)
+        out_store(1, 6)
+        plane_quantise(1, 512, 768)
+        plane_scales_store(1)
+        out_store(1, 7)

@@ -16,8 +16,10 @@ ACT = mybir.ActivationFunctionType
 
 T, D, N, Q = 1024, 1024, 1024, 1024
 ROOT = 32.0
-TANH_BUFS = 12
+TANH_BUFS = 8
+WEIGHED_BUFS = 4
 OUT_BUFS = 5
+WIDE = ((1, 0), (1, 1), (1, 2), (1, 3))
 FLOPS = 3 * 2 * 1024 * 1024 * 1024
 
 
@@ -29,17 +31,21 @@ def tile_adversarialsdfconditionalpricingmoments_x2_kernel(
     with ExitStack() as ctx:
         keep = ctx.enter_context(tc.tile_pool(name="keep", bufs=1))
         work = ctx.enter_context(tc.tile_pool(name="work", bufs=4))
-        psum = ctx.enter_context(tc.psum_pool(name="psum", bufs=8))
+        psum = ctx.enter_context(tc.psum_pool(name="psum", bufs=1))
         ctx.enter_context(tc.manual_schedule())
 
         def kept(name, shape, dtype):
             return keep.tile(shape, dtype, name=name, align_bytes=64)
 
+        ring = list(range(7))
+
         def bank(shape):
-            return psum.tile(shape, F32, name="bank", tag="bank")
+            ring.append(ring.pop(0))
+            return psum.tile(shape, F32, name="bank", tag="bank%d" % ring[-1])
 
         ident = kept("ident", [128, 128], F32)
-        z_rows, r_rows = {}, {}
+        z_rows = {}
+        r_rows = [kept("r%d" % g, [128, 4, N], BF16) for g in range(2)]
         wo_sb = kept("wo", [128, 2, 2048], U8)
         wg_sb = [kept("wg%d" % qh, [128, 2, 1024], U8) for qh in range(2)]
         w_scale = {name: kept("ws" + name, [128, 2, N], U8) for name in "og"}
@@ -48,6 +54,9 @@ def tile_adversarialsdfconditionalpricingmoments_x2_kernel(
         v_sb = kept("v", [128, 2, 4], BF16)
         neg_v = kept("nv", [128, 2, 4], F32)
         u_sb = kept("u", [128, 2, 4], BF16)
+        u_row = kept("u_row", [128, 512], BF16)
+        ones = kept("ones", [128, 128], BF16)
+        u_all = psum.tile([128, 512], F32, name="u_all", tag="bank7")
         zero = kept("zero", [128, 512], BF16)
         warm = kept("warm", [128, 1], F32)
         eye = kept("eye", [128, 8], BF16)
@@ -57,16 +66,15 @@ def tile_adversarialsdfconditionalpricingmoments_x2_kernel(
         f_in = [kept("fin%d" % qh, [128, 2, 512, 4], BF16) for qh in range(2)]
         f_code = [kept("fc%d" % qh, [128, 2, 512], U32) for qh in range(2)]
         f_scale = [kept("fs%d" % qh, [128, 2, 512], U8) for qh in range(2)]
-        d_rows = [kept("dsc%d" % g, [128, 4, N], BF16) for g in range(2)]
         d_in = [kept("din%d" % g, [128, N, 4], BF16) for g in range(2)]
         d_code = [kept("dc%d" % g, [128, N], U32) for g in range(2)]
         d_scale = [kept("ds%d" % g, [128, N], U8) for g in range(2)]
-        sums = [kept("acc%d" % g, [128, 4, 2], F32) for g in range(2)]
+        sums = kept("acc", [128, 2, 4, 4], F32)
         neg_sdf = {}
         out_bf = [[kept("ob%d%d" % (qh, ip), [128, 2, 512], BF16) for ip in range(4 - qh)] for qh in range(2)]
-        p_in = [kept("pin%d" % qh, [128, N, 4], BF16) for qh in range(2)]
+        p_in = d_in
         p_code = [kept("pc%d" % qh, [128, N], U32) for qh in range(2)]
-        p_scale = [kept("ps%d" % qh, [128, N], U8) for qh in range(2)]
+        p_scale = kept("ps", [128, N], U8)
         held = {}
 
         def copy(eng, dst, src):
@@ -86,18 +94,17 @@ def tile_adversarialsdfconditionalpricingmoments_x2_kernel(
                     out=dst, lhsT=lhs, lhsT_scale=lhs_scale, rhs=rhs, rhs_scale=rhs_scale, start=n == 0, stop=n == 1
                 )
 
-        def load_rows(rows, name, src, g, j0, j1):
-            t = kept("%s%d%d" % (name, g, j0), [128, j1 - j0, 1024], BF16)
-            group = src[512 * g : 512 * (g + 1), :].rearrange("(p j) d -> p j d", j=4)
-            nc.sync.dma_start(out=t[:], in_=group[:, j0:j1, :])
-            for j in range(j0, j1):
-                rows[g, j] = t[:, j - j0, :]
+        def by_slot(src, g):
+            return src[512 * g : 512 * (g + 1), :].rearrange("(p j) d -> p j d", j=4)
 
         def load_z(g, j0, j1):
-            load_rows(z_rows, "z", z, g, j0, j1)
+            t = kept("z%d%d" % (g, j0), [128, j1 - j0, 1024], BF16)
+            nc.sync.dma_start(out=t[:], in_=by_slot(z, g)[:, j0:j1, :])
+            for j in range(j0, j1):
+                z_rows[g, j] = t[:, j - j0, :]
 
         def load_r(g, j0, j1):
-            load_rows(r_rows, "r", r, g, j0, j1)
+            nc.sync.dma_start(out=r_rows[g][:, j0:j1, :], in_=by_slot(r, g)[:, j0:j1, :])
 
         def load_scales(queue, name, src):
             for c in range(4):
@@ -118,25 +125,31 @@ def tile_adversarialsdfconditionalpricingmoments_x2_kernel(
                 t = bank([128, 512])
                 nc.tensor.matmul(t[:], zero[:, 0:128], zero[:], start=True, stop=True)
 
+        def spread_u():
+            row = u_row[:].rearrange("r (c e b) -> r e c b", e=2, b=2)
+            nc.tensor.matmul(u_all[:], ones[:], row, start=True, stop=True)
+
         def z_sort(g, j):
-            t = work.tile([128, 2, 2, 128], U32, name="zsort", bufs=2)
+            t = work.tile([128, 2, 2, 128], U32, name="zsort", bufs=4)
             scalar.copy(out=t[:], in_=z_rows[g, j].bitcast(U32).rearrange("p (h c e) -> p h e c", h=2, e=2))
             held["sorted", g, j] = t
 
-        def z_turn(g, j0, j1):
-            for j in range(j0, j1):
-                t = bank([128, 2, 2, 128])
-                words = z_rows[g, j].bitcast(F32)
-                for kg in range(2):
-                    for e in range(2):
-                        if ("sorted", g, j) in held:
-                            src = held["sorted", g, j][:, kg, e, :].bitcast(F32)
-                        else:
-                            src = words[:, 256 * kg + e : 256 * (kg + 1) : 2]
-                        nc.tensor.transpose(t[:, kg, e, :], src, ident[:])
-                dst = z_in[g][j // 2][:].rearrange("p h c k -> p (h c k)").bitcast(F32)
-                dst = dst.rearrange("p (h a c e) -> p h a c e", h=2, a=2, e=2)
-                scalar.copy(out=dst[:, :, j % 2, :, :], in_=t[:].rearrange("p h e c -> p h c e"))
+        def z_turn(g, j):
+            t = bank([128, 2, 2, 128])
+            words = z_rows[g, j].bitcast(F32)
+            for kg in range(2):
+                for e in range(2):
+                    if ("sorted", g, j) in held:
+                        src = held["sorted", g, j][:, kg, e, :].bitcast(F32)
+                    else:
+                        src = words[:, 256 * kg + e : 256 * (kg + 1) : 2]
+                    nc.tensor.transpose(t[:, kg, e, :], src, ident[:])
+            held["z", g, j] = t
+
+        def z_copy(g, j):
+            dst = z_in[g][j // 2][:].rearrange("p h c k -> p (h c k)").bitcast(F32)
+            dst = dst.rearrange("p (h a c e) -> p h a c e", h=2, a=2, e=2)
+            scalar.copy(out=dst[:, :, j % 2, :, :], in_=held["z", g, j][:].rearrange("p h e c -> p h c e"))
 
         def z_quantise(g, j0, j1):
             cols = slice(128 * j0, 128 * j1)
@@ -167,37 +180,54 @@ def tile_adversarialsdfconditionalpricingmoments_x2_kernel(
                 out=prod[:],
                 in0=held["om", g, j, ih][:],
                 scalar=1.0,
-                in1=r_rows[g, j][:, 512 * ih : 512 * (ih + 1)],
+                in1=r_rows[g][:, j, 512 * ih : 512 * (ih + 1)],
                 op0=MULT,
                 op1=MULT,
-                accum_out=sums[g][:, j, ih : ih + 1],
+                accum_out=sums[:, g, j, ih : ih + 1],
             )
 
         def om(g, j, ih):
             om_product(g, j, ih)
             om_sum(g, j, ih)
 
-        def sdf(g, j0, j1):
+        def sdf(g, j0, j1, eng=vector):
             t = kept("sm%d%d" % (g, j0), [128, j1 - j0], F32)
-            vector.scalar_tensor_tensor(
-                out=t[:], in0=sums[g][:, j0:j1, 0], scalar=-ROOT, in1=sums[g][:, j0:j1, 1], op0=ADD, op1=ADD
-            )
+            if eng is vector:
+                vector.tensor_reduce(out=t[:], in_=sums[:, g, j0:j1, 0:3], op=ADD, axis=mybir.AxisListType.X)
+            else:
+                gpsimd.tensor_scalar(
+                    out=t[:], in0=sums[:, g, j0, 0:1], scalar1=sums[:, g, j0, 1:2], scalar2=-ROOT, op0=ADD, op1=ADD
+                )
             for j in range(j0, j1):
                 neg_sdf[g, j] = t[:, j - j0 : j - j0 + 1]
 
-        def d_scale_rows(g, j):
-            vector.tensor_scalar(
-                out=d_rows[g][:, j, :],
-                in0=r_rows[g, j],
+        def d_scale_rows(eng, g, j):
+            if eng is scalar:
+                both = kept("both%d%d" % (g, j), [128, 1], F32)
+                gpsimd.tensor_tensor(out=both[:], in0=neg_sdf[g, j], in1=neg_v[:, g, j : j + 1], op=MULT)
+                scalar.mul(out=r_rows[g][:, j, :], in_=r_rows[g][:, j, :], mul=both[:])
+                return
+            eng.tensor_scalar(
+                out=r_rows[g][:, j, :],
+                in0=r_rows[g][:, j, :],
                 scalar1=neg_sdf[g, j],
                 scalar2=neg_v[:, g, j : j + 1],
                 op0=MULT,
                 op1=MULT,
             )
 
+        def d_place(g, quarter):
+            if (g, quarter) == (1, 3):
+                return f_in[0][:, 1, 0:256, :]
+            return d_in[g][:, 256 * quarter : 256 * (quarter + 1), :]
+
         def d_interleave(eng, g, quarter):
             cols = slice(256 * quarter, 256 * (quarter + 1))
-            copy(eng, d_in[g][:, cols, :], d_rows[g][:, :, cols].rearrange("p j c -> p c j"))
+            copy(eng, d_place(g, quarter), r_rows[g][:, :, cols].rearrange("p j c -> p c j"))
+
+        def d_quantise_quarter(g, quarter):
+            cols = slice(256 * quarter, 256 * (quarter + 1))
+            quantise(d_code[g][:, cols], d_scale[g][:, cols], d_place(g, quarter))
 
         def d_quantise(g, ih):
             cols = slice(512 * ih, 512 * (ih + 1))
@@ -209,7 +239,7 @@ def tile_adversarialsdfconditionalpricingmoments_x2_kernel(
             nc.tensor.matmul(t[:], bg_rows[:], eye[:], start=True, stop=True)
             scalar.copy(out=bg_cols[:], in_=t[:])
 
-        def instrument(g, qt):
+        def x_product(g, qt):
             x = bank([128, 512])
             product(
                 x[:],
@@ -223,56 +253,150 @@ def tile_adversarialsdfconditionalpricingmoments_x2_kernel(
                     for kg in range(2)
                 ],
             )
-            t = work.tile([128, 512], F32, name="th", bufs=TANH_BUFS)
-            scalar.activation(out=t[:], in_=x[:], func=ACT.Tanh, bias=bg_cols[:, qt : qt + 1])
-            held["tanh", g, qt] = t
+            held["x", g, qt] = x
 
-        def f_turn(g, qt):
+        def x_tanh(g, qt):
+            if qt % 2 == 0:
+                held["tanh", g, qt // 2] = work.tile([128, 2, 512], F32, name="th", bufs=TANH_BUFS)
+            order = "p e b c" if (g, qt // 2) in WIDE else "p e c b"
+            scalar.activation(
+                out=held["tanh", g, qt // 2][:, qt % 2, :].rearrange("p (%s) -> %s" % (order[2:], order), e=2, b=2),
+                in_=held["x", g, qt][:].rearrange("p (e b c) -> %s" % order, e=2, b=2),
+                func=ACT.Tanh,
+                bias=bg_cols[:, qt : qt + 1],
+            )
+
+        def instrument(g, qt):
+            x_product(g, qt)
+            x_tanh(g, qt)
+
+        def f_weigh(g, qq):
+            t = work.tile([128, 2, 512], BF16, name="fw", bufs=WEIGHED_BUFS)
+            vector.tensor_tensor(
+                out=t[:],
+                in0=held["tanh", g, qq][:],
+                in1=u_all[:].unsqueeze(1).to_broadcast([128, 2, 512]),
+                op=MULT,
+            )
+            held["weighed", g, qq] = t
+
+        def f_turn(g, qq):
+            t = bank([128, 2, 256])
+            for k in range(2):
+                words = held["weighed", g, qq][:, k, :].bitcast(F32)
+                for e in range(2):
+                    nc.tensor.transpose(t[:, e, 128 * k : 128 * (k + 1)], words[:, 128 * e : 128 * (e + 1)], ident[:])
+            held["f", g, qq] = t
+
+        def f_copy(eng, g, qq):
+            words = f_in[qq // 2][:, g, :, :].rearrange("p c k -> p (c k)").bitcast(F32)
+            src = held["f", g, qq][:]
+            if qq < 2:
+                dst = words.rearrange("p (c e) -> p c e", e=2)[:, 256 * qq : 256 * (qq + 1), :]
+                copy(eng, dst, src.rearrange("p e c -> p c e"))
+            else:
+                dst = words.rearrange("p (s m e) -> p s m e", s=4, e=2)[:, :, 64 * (qq % 2) : 64 * (qq % 2 + 1), :]
+                copy(eng, dst, src.rearrange("p e (m s) -> p s m e", s=4))
+
+        def wide_turn(g, qt):
             t = bank([128, 4, 128])
             for j in range(4):
-                nc.tensor.transpose(t[:, j, :], held["tanh", g, qt][:, 128 * j : 128 * (j + 1)], ident[:])
-            held["f", g, qt] = t
+                nc.tensor.transpose(t[:, j, :], held["tanh", g, qt // 2][:, qt % 2, 128 * j : 128 * (j + 1)], ident[:])
+            held["wide", g, qt] = t
 
-        def f_order(qh):
-            return ("(m s)", "(s m)")[qh]
-
-        def f_weigh(g, qt):
-            cols = f_in[qt // 4][:, g, :, :].rearrange("p %s j -> p m s j" % f_order(qt // 4), s=4)
+        def wide_weigh(g, qt):
+            cols = f_in[qt // 4][:, g, :, :].rearrange("p %s j -> p m s j" % ("(m s)", "(s m)")[qt // 4], s=4)
             vector.tensor_tensor(
                 out=cols[:, 32 * (qt % 4) : 32 * (qt % 4 + 1), :, :],
-                in0=held["f", g, qt][:].rearrange("p j (m s) -> p m s j", s=4),
+                in0=held["wide", g, qt][:].rearrange("p j (m s) -> p m s j", s=4),
                 in1=u_sb[:, g, :].unsqueeze(1).unsqueeze(1).to_broadcast([128, 32, 4, 4]),
                 op=MULT,
             )
 
-        def f_quantise(qh):
-            for g in range(2):
-                quantise(f_code[qh][:, g, :], f_scale[qh][:, g, :], f_in[qh][:, g, :, :])
+        def f_quantise(g, qh, c0, c1):
+            quantise(f_code[qh][:, g, c0:c1], f_scale[qh][:, g, c0:c1], f_in[qh][:, g, c0:c1, :])
 
         def d_operand(g, it):
             cols = slice(128 * it, 128 * (it + 1))
             return d_code[g][:, cols].bitcast(E4M3), d_scale[g][:, cols]
 
+        def f_operand(g, qh, c0, c1):
+            return f_code[qh][:, g, c0:c1].bitcast(E4M3), f_scale[qh][:, g, c0:c1]
+
+        def quarter_product(qq, ip):
+            t = bank([128, 2, 256])
+            for k in range(2):
+                product(
+                    t[:, k, :],
+                    [(*d_operand(g, 2 * ip + k), *f_operand(g, 0, 256 * qq, 256 * (qq + 1))) for g in range(2)],
+                )
+            held["outq", qq, ip] = t
+
+        def quarter_store(qq, ip):
+            t = work.tile([128, 2, 256], F32, name="osq", bufs=1)
+            held["sbq", qq, ip] = t
+            scalar.mul(out=t[:], in_=held["outq", qq, ip][:], mul=1.0 / ROOT)
+            rows = out_0[256 * ip : 256 * (ip + 1), 256 * qq : 256 * (qq + 1)]
+            nc.sync.dma_start(out=rows.rearrange("(k p) c -> p k c", p=128), in_=t[:])
+
+        def quarter(qq, ip):
+            quarter_product(qq, ip)
+            quarter_store(qq, ip)
+
+        def round_quarter(eng, qq, ip):
+            dst = out_bf[0][ip][:].rearrange("p k (e a c b) -> p k e a c b", e=2, a=2, b=2)[:, :, :, qq, :, :]
+            src = held["sbq", qq, ip][:].rearrange("p k (c e b) -> p k e c b", e=2, b=2)
+            if eng is gpsimd:
+                for k in range(2):
+                    copy(eng, dst[:, k], src[:, k])
+            else:
+                copy(eng, dst, src)
+
         def out_product(qh, it):
             t = bank([128, 512])
-            product(t[:], [(*d_operand(g, it), f_code[qh][:, g, :].bitcast(E4M3), f_scale[qh][:, g, :]) for g in range(2)])
+            product(t[:], [(*d_operand(g, it), *f_operand(g, qh, 0, 512)) for g in range(2)])
             held["out", qh, it] = t
 
-        def out_store(qh, it):
+        def out_pass(qh, it, g):
+            if g == 0:
+                held["out", qh, it] = bank([128, 512])
+            lhs, lhs_scale = d_operand(g, it)
+            rhs, rhs_scale = f_operand(g, qh, 0, 512)
+            nc.tensor.matmul_mx(
+                out=held["out", qh, it][:], lhsT=lhs, lhsT_scale=lhs_scale, rhs=rhs, rhs_scale=rhs_scale,
+                start=g == 0, stop=g == 1,
+            )
+
+        def out_store(qh, it, eng=scalar):
             if it % 2 == 0:
                 held["sb", qh, it // 2] = work.tile([128, 2, 512], F32, name="osb", bufs=OUT_BUFS)
             t = held["sb", qh, it // 2][:, it % 2, :]
-            src = held["out", qh, it][:].rearrange("p %s -> p m s" % f_order(qh), s=4)
-            scalar.mul(out=t.rearrange("p (m s) -> p m s", s=4), in_=src, mul=1.0 / ROOT)
+            src = held["out", qh, it][:].rearrange("p %s -> p m s" % ("(m s)", "(s m)")[qh], s=4)
+            scaled(eng, t.rearrange("p (m s) -> p m s", s=4), src)
             nc.sync.dma_start(out=out_0[128 * it : 128 * (it + 1), 512 * qh : 512 * (qh + 1)], in_=t)
 
-        def out(qh, it):
-            out_product(qh, it)
-            out_store(qh, it)
+        def scaled(eng, dst, src):
+            if eng is scalar:
+                scalar.mul(out=dst, in_=src, mul=1.0 / ROOT)
+            else:
+                vector.tensor_scalar(out=dst, in0=src, scalar1=1.0 / ROOT, scalar2=None, op0=MULT)
 
-        def round_pair(qh, ip):
+        def out(qh, it, eng=scalar):
+            out_product(qh, it)
+            out_store(qh, it, eng)
+
+        def round_tile(eng, qh, it):
+            dst = out_bf[qh][it // 2][:, it % 2, :].rearrange("p (e c b) -> p e c b", e=2, b=2)
+            copy(eng, dst, held["sb", qh, it // 2][:, it % 2, :].rearrange("p (c e b) -> p e c b", e=2, b=2))
+
+        def round_pair(eng, qh, ip):
             dst = out_bf[qh][ip][:].rearrange("p k (e c b) -> p k e c b", e=2, b=2)
-            copy(vector, dst, held["sb", qh, ip][:].rearrange("p k (c e b) -> p k e c b", e=2, b=2))
+            src = held["sb", qh, ip][:].rearrange("p k (c e b) -> p k e c b", e=2, b=2)
+            if eng is gpsimd:
+                for k in range(2):
+                    copy(eng, dst[:, k], src[:, k])
+            else:
+                copy(eng, dst, src)
 
         def plane_turn(qh, ip):
             t = bank([128, 2, 256])
@@ -289,37 +413,35 @@ def tile_adversarialsdfconditionalpricingmoments_x2_kernel(
         def plane_product(it):
             t = bank([128, 4, 128])
             for s in range(4):
-                cols = slice(128 * s, 128 * (s + 1))
-                product(
-                    t[:, s, :],
-                    [(f_code[1][:, g, cols].bitcast(E4M3), f_scale[1][:, g, cols], *d_operand(g, it)) for g in range(2)],
-                )
+                product(t[:, s, :], [(*f_operand(g, 1, 128 * s, 128 * (s + 1)), *d_operand(g, it)) for g in range(2)])
             held["direct", it] = t
 
         def plane_scale(eng, it):
-            dst, src = p_in[1][:, 128 * it : 128 * (it + 1), :], held["direct", it][:].rearrange("p s c -> p c s")
-            if eng is scalar:
-                scalar.mul(out=dst, in_=src, mul=1.0 / ROOT)
-            else:
-                vector.tensor_scalar(out=dst, in0=src, scalar1=1.0 / ROOT, scalar2=None, op0=MULT)
+            scaled(eng, p_in[1][:, 128 * it : 128 * (it + 1), :], held["direct", it][:].rearrange("p s c -> p c s"))
 
         def plane_quantise(qh, c0, c1):
-            quantise(p_code[qh][:, c0:c1], p_scale[qh][:, c0:c1], p_in[qh][:, c0:c1, :])
+            quantise(p_code[qh][:, c0:c1], p_scale[4 * qh : 128, c0:c1], p_in[qh][:, c0:c1, :])
+
+        def plane_store(qh, c0, c1):
             nc.sync.dma_start(
                 out=out_1[qh].rearrange("p m t -> p (m t)")[:, 4 * c0 : 4 * c1].bitcast(I32),
                 in_=p_code[qh][:, c0:c1].bitcast(I32),
             )
 
-        def plane_scales_store(qh):
+        def plane_scales_store(queue=nc.sync):
             for c in range(4):
-                nc.sync.dma_start(
-                    out=out_2[qh, 4 * c : 4 * c + 4, :].bitcast(I32), in_=p_scale[qh][32 * c : 32 * c + 4, :].bitcast(I32)
+                queue.dma_start(
+                    out=out_2[:, 4 * c : 4 * c + 4, :].bitcast(I32), in_=p_scale[32 * c : 32 * c + 8, :].bitcast(I32)
                 )
 
         vector.memset(zero[:], 0.0)
         zero_scales(vector, "o")
+        vector.memset(u_row[:], 0.0)
         vector.memset(ident[:], 0.0)
+        gpsimd.dma_start(out=u_row[0:1, :], in_=u[0:512].rearrange("(a t) -> a t", a=1))
         make_identity(nc, ident[:], nomemset=True)
+        vector.memset(ones[:], 1.0)
+        vector.memset(sums[:, :, :, 2:3], -ROOT)
         vector.memset(bg_rows[:], 0.0)
         zero_scales(vector, "g")
         load_z(0, 0, 1)
@@ -343,12 +465,15 @@ def tile_adversarialsdfconditionalpricingmoments_x2_kernel(
         gpsimd.tensor_scalar(out=neg_v[:], in0=v_sb[:], scalar1=-1.0 / ROOT, scalar2=0.0, op0=MULT, op1=ADD)
         scalar.activation(out=warm[:], in_=zero[:, 0:1], func=ACT.Tanh)
         warm_tensor(4)
-
         for j in range(2):
-            z_turn(0, j, j + 1)
+            z_turn(0, j)
+            z_copy(0, j)
             z_quantise(0, j, j + 1)
-        warm_tensor(2)
-        z_turn(0, 2, 4)
+        warm_tensor(1)
+        spread_u()
+        for j in range(2, 4):
+            z_turn(0, j)
+            z_copy(0, j)
         om(0, 0, 0)
         z_quantise(0, 2, 4)
         om(0, 0, 1)
@@ -357,106 +482,132 @@ def tile_adversarialsdfconditionalpricingmoments_x2_kernel(
         om(0, 1, 1)
         z_sort(1, 0)
         z_sort(1, 1)
+        sdf(0, 0, 1, gpsimd)
+        d_scale_rows(gpsimd, 0, 0)
+        sdf(0, 1, 2, gpsimd)
+        d_scale_rows(gpsimd, 0, 1)
         om(0, 2, 0)
-        sdf(0, 0, 2)
         om(0, 2, 1)
         om_product(0, 3, 0)
         om_product(0, 3, 1)
-        z_turn(1, 0, 4)
-        d_scale_rows(0, 0)
+        for j in range(4):
+            z_turn(1, j)
+            z_copy(1, j)
         om_sum(0, 3, 0)
+        sdf(0, 2, 3)
         om_sum(0, 3, 1)
         z_quantise(1, 0, 2)
+        sdf(0, 3, 4)
+        d_scale_rows(vector, 0, 2)
+        z_quantise(1, 2, 4)
+        d_scale_rows(vector, 0, 3)
         instrument(0, 0)
         instrument(0, 1)
-
-        om_product(1, 0, 0)
-        om_product(1, 0, 1)
-        sdf(0, 2, 4)
-        d_scale_rows(0, 1)
-        z_quantise(1, 2, 4)
-        d_scale_rows(0, 2)
-        d_scale_rows(0, 3)
-        d_interleave(gpsimd, 0, 2)
-        d_interleave(gpsimd, 0, 3)
-        om_sum(1, 0, 0)
-        om_sum(1, 0, 1)
-        instrument(0, 2)
-        instrument(0, 3)
         d_interleave(scalar, 0, 0)
-        d_interleave(scalar, 0, 1)
-        for j in range(1, 4):
+        d_interleave(gpsimd, 0, 1)
+        d_interleave(scalar, 0, 2)
+        d_interleave(gpsimd, 0, 3)
+        for j in range(3):
             om(1, j, 0)
             om(1, j, 1)
-
+        om(1, 3, 0)
+        sdf(1, 0, 3)
+        om(1, 3, 1)
+        instrument(0, 2)
+        instrument(0, 3)
         for qt in range(4):
             instrument(1, qt)
-        for g in range(2):
-            for qt in range(4):
-                f_turn(g, qt)
+        d_scale_rows(vector, 1, 0)
+        d_scale_rows(vector, 1, 1)
+        sdf(1, 3, 4)
+        d_scale_rows(vector, 1, 2)
         d_quantise(0, 0)
-        sdf(1, 0, 4)
-        d_quantise(0, 1)
-        for j in range(4):
-            d_scale_rows(1, j)
-        d_interleave(scalar, 1, 0)
-        d_interleave(scalar, 1, 1)
-        d_interleave(gpsimd, 1, 2)
-        d_interleave(gpsimd, 1, 3)
-        for g in range(2):
-            for qt in range(4):
-                f_weigh(g, qt)
-        for g in range(2):
-            for qt in range(4, 8):
-                instrument(g, qt)
-        f_quantise(0)
+        d_scale_rows(vector, 1, 3)
+        for quarter_i in range(3):
+            d_interleave(gpsimd, 1, quarter_i)
+        f_weigh(0, 0)
+        f_weigh(0, 1)
+        instrument(0, 4)
+        instrument(0, 5)
+        for qt in range(4):
+            wide_turn(1, qt)
+        f_turn(0, 0)
+        f_turn(0, 1)
+        for qt in range(4):
+            wide_weigh(1, qt)
+        f_copy(scalar, 0, 0)
+        f_copy(scalar, 0, 1)
+        instrument(0, 6)
+        instrument(0, 7)
+        for qt in range(4, 8):
+            instrument(1, qt)
         d_quantise(1, 0)
-        d_quantise(1, 1)
-
-        for g in range(2):
-            for qt in range(4, 8):
-                f_turn(g, qt)
-                f_weigh(g, qt)
-        for it in range(8):
+        f_quantise(0, 0, 0, 512)
+        f_quantise(1, 0, 0, 512)
+        d_quantise(0, 1)
+        d_quantise_quarter(1, 2)
+        d_interleave(gpsimd, 1, 3)
+        f_weigh(0, 2)
+        f_weigh(0, 3)
+        for it in range(4):
             out(0, it)
-        f_quantise(1)
-
-        for ip in range(3):
-            round_pair(0, ip)
-        out(1, 0)
-        out(1, 1)
+        for qt in range(4, 8):
+            wide_turn(1, qt)
+        ring.append(7)
+        f_turn(0, 2)
+        f_turn(0, 3)
+        for it in range(4):
+            round_tile(gpsimd, 0, it)
+        for qt in range(4, 8):
+            wide_weigh(1, qt)
+        f_copy(scalar, 0, 2)
+        f_copy(scalar, 0, 3)
+        d_quantise_quarter(1, 3)
+        for it in range(4, 8):
+            out(0, it)
+        f_quantise(0, 1, 0, 512)
+        f_quantise(1, 1, 0, 512)
         plane_turn(0, 0)
         plane_turn(0, 1)
-        round_pair(0, 3)
+        round_pair(vector, 0, 2)
         plane_copy(vector, 0, 0)
-        plane_copy(scalar, 0, 1)
-        round_pair(1, 0)
-        out(1, 2)
+        plane_copy(vector, 0, 1)
+        round_pair(vector, 0, 3)
+        out(1, 0)
+        out(1, 1)
         plane_quantise(0, 0, 512)
+        plane_store(0, 0, 512)
+        out(1, 2)
+        round_pair(vector, 1, 0)
         out(1, 3)
         out(1, 4)
-        round_pair(1, 1)
+        round_pair(vector, 1, 1)
         out(1, 5)
-        for qh, ip in ((0, 2), (0, 3), (1, 0), (1, 1)):
-            plane_turn(qh, ip)
+        plane_turn(0, 2)
+        plane_turn(0, 3)
+        plane_turn(1, 0)
+        plane_turn(1, 1)
         plane_copy(vector, 0, 2)
-        round_pair(1, 2)
         plane_copy(scalar, 0, 3)
+        round_pair(vector, 1, 2)
         plane_copy(scalar, 1, 0)
-        plane_copy(scalar, 1, 1)
         plane_quantise(0, 512, 1024)
-        plane_scales_store(0)
+        plane_store(0, 512, 1024)
+        plane_copy(scalar, 1, 1)
         plane_product(6)
         plane_product(7)
         plane_scale(vector, 6)
+        out_product(1, 6)
         plane_turn(1, 2)
         plane_quantise(1, 0, 512)
+        plane_store(1, 0, 512)
         plane_scale(scalar, 7)
-        plane_copy(scalar, 1, 2)
-        out_product(1, 6)
-        out_product(1, 7)
         plane_quantise(1, 768, 1024)
         out_store(1, 6)
+        plane_store(1, 768, 1024)
+        plane_copy(vector, 1, 2)
+        out_product(1, 7)
         plane_quantise(1, 512, 768)
-        plane_scales_store(1)
+        plane_store(1, 512, 768)
         out_store(1, 7)
+        plane_scales_store()

@@ -484,8 +484,6 @@ def tile_adversarialsdfconditionalpricingmoments_x2_kernel(
         z_sort(1, 1)
         sdf(0, 0, 1, gpsimd)
         d_scale_rows(gpsimd, 0, 0)
-        sdf(0, 1, 2, gpsimd)
-        d_scale_rows(gpsimd, 0, 1)
         om(0, 2, 0)
         om(0, 2, 1)
         om_product(0, 3, 0)
@@ -494,8 +492,9 @@ def tile_adversarialsdfconditionalpricingmoments_x2_kernel(
             z_turn(1, j)
             z_copy(1, j)
         om_sum(0, 3, 0)
-        sdf(0, 2, 3)
+        sdf(0, 1, 3)
         om_sum(0, 3, 1)
+        d_scale_rows(vector, 0, 1)
         z_quantise(1, 0, 2)
         sdf(0, 3, 4)
         d_scale_rows(vector, 0, 2)
@@ -523,12 +522,13 @@ def tile_adversarialsdfconditionalpricingmoments_x2_kernel(
         d_scale_rows(vector, 1, 2)
         d_quantise(0, 0)
         d_scale_rows(vector, 1, 3)
-        for quarter_i in range(3):
-            d_interleave(gpsimd, 1, quarter_i)
+        d_interleave(gpsimd, 1, 0)
+        d_interleave(gpsimd, 1, 2)
         f_weigh(0, 0)
         f_weigh(0, 1)
         instrument(0, 4)
         instrument(0, 5)
+        d_interleave(scalar, 1, 1)
         for qt in range(4):
             wide_turn(1, qt)
         f_turn(0, 0)
@@ -556,17 +556,19 @@ def tile_adversarialsdfconditionalpricingmoments_x2_kernel(
         ring.append(7)
         f_turn(0, 2)
         f_turn(0, 3)
-        for it in range(4):
+        for it in range(2):
             round_tile(gpsimd, 0, it)
         for qt in range(4, 8):
             wide_weigh(1, qt)
+        round_tile(scalar, 0, 2)
+        round_tile(scalar, 0, 3)
         f_copy(scalar, 0, 2)
         f_copy(scalar, 0, 3)
         d_quantise_quarter(1, 3)
         for it in range(4, 8):
             out(0, it)
-        f_quantise(0, 1, 0, 512)
         f_quantise(1, 1, 0, 512)
+        f_quantise(0, 1, 0, 512)
         plane_turn(0, 0)
         plane_turn(0, 1)
         round_pair(vector, 0, 2)

@@ -436,14 +436,13 @@ def tile_adversarialsdfconditionalpricingmoments_x2_kernel(
 
         vector.memset(zero[:], 0.0)
         zero_scales(vector, "o")
-        vector.memset(u_row[:], 0.0)
         vector.memset(ident[:], 0.0)
-        gpsimd.dma_start(out=u_row[0:1, :], in_=u[0:512].rearrange("(a t) -> a t", a=1))
         make_identity(nc, ident[:], nomemset=True)
         vector.memset(ones[:], 1.0)
         vector.memset(sums[:, :, :, 2:3], -ROOT)
         vector.memset(bg_rows[:], 0.0)
         zero_scales(vector, "g")
+        vector.memset(u_row[:], 0.0)
         load_z(0, 0, 1)
         load_z(0, 1, 2)
         load_z(0, 2, 4)
@@ -456,6 +455,7 @@ def tile_adversarialsdfconditionalpricingmoments_x2_kernel(
         load_z(1, 2, 4)
         load_wg(0)
         load_scales(nc.sync, "g", wg_scales)
+        nc.sync.dma_start(out=u_row[0:1, :], in_=u[0:512].rearrange("(a t) -> a t", a=1))
         load_r(1, 0, 2)
         load_r(1, 2, 4)
         load_wg(1)
@@ -469,8 +469,7 @@ def tile_adversarialsdfconditionalpricingmoments_x2_kernel(
             z_turn(0, j)
             z_copy(0, j)
             z_quantise(0, j, j + 1)
-        warm_tensor(1)
-        spread_u()
+        warm_tensor(2)
         for j in range(2, 4):
             z_turn(0, j)
             z_copy(0, j)
@@ -502,6 +501,7 @@ def tile_adversarialsdfconditionalpricingmoments_x2_kernel(
         d_scale_rows(vector, 0, 3)
         instrument(0, 0)
         instrument(0, 1)
+        spread_u()
         d_interleave(scalar, 0, 0)
         d_interleave(gpsimd, 0, 1)
         d_interleave(scalar, 0, 2)

@@ -57,6 +57,7 @@ def tile_adversarialsdfconditionalpricingmoments_x2_kernel(
         u_row = kept("u_row", [128, 512], BF16)
         ones = kept("ones", [128, 128], BF16)
         u_all = psum.tile([128, 512], F32, name="u_all", tag="bank7")
+        u_wide = kept("u_wide", [128, 512], F32)
         zero = kept("zero", [128, 512], BF16)
         warm = kept("warm", [128, 1], F32)
         eye = kept("eye", [128, 8], BF16)
@@ -71,7 +72,7 @@ def tile_adversarialsdfconditionalpricingmoments_x2_kernel(
         d_scale = [kept("ds%d" % g, [128, N], U8) for g in range(2)]
         sums = kept("acc", [128, 2, 4, 4], F32)
         neg_sdf = {}
-        out_bf = [[kept("ob%d%d" % (qh, ip), [128, 2, 512], BF16) for ip in range(4 - qh)] for qh in range(2)]
+        out_bf = [[kept("ob%d%d" % (qh, ip), [128, 2, 512], BF16) for ip in range(4)] for qh in range(2)]
         p_in = d_in
         p_code = [kept("pc%d" % qh, [128, N], U32) for qh in range(2)]
         p_scale = kept("ps", [128, N], U8)
@@ -109,8 +110,8 @@ def tile_adversarialsdfconditionalpricingmoments_x2_kernel(
         def load_scales(queue, name, src):
             for c in range(4):
                 queue.dma_start(
-                    out=w_scale[name][32 * c : 32 * c + 4, :, :].bitcast(I32),
-                    in_=src[:, 4 * c : 4 * c + 4, :].rearrange("g q n -> q g n").bitcast(I32),
+                    out=w_scale[name][c:128:32, :, :].bitcast(I32),
+                    in_=src[:, c:16:4, :].rearrange("g q n -> q g n").bitcast(I32),
                 )
 
         def load_wg(qh):
@@ -217,7 +218,7 @@ def tile_adversarialsdfconditionalpricingmoments_x2_kernel(
             )
 
         def d_place(g, quarter):
-            if (g, quarter) == (1, 3):
+            if g == 1 and quarter >= 2:
                 return f_in[0][:, 1, 0:256, :]
             return d_in[g][:, 256 * quarter : 256 * (quarter + 1), :]
 
@@ -234,7 +235,6 @@ def tile_adversarialsdfconditionalpricingmoments_x2_kernel(
             quantise(d_code[g][:, cols], d_scale[g][:, cols], d_in[g][:, cols, :])
 
         def bias_columns():
-            scalar.copy(out=eye[:], in_=ident[:, 0:8])
             t = bank([128, 8])
             nc.tensor.matmul(t[:], bg_rows[:], eye[:], start=True, stop=True)
             scalar.copy(out=bg_cols[:], in_=t[:])
@@ -280,6 +280,14 @@ def tile_adversarialsdfconditionalpricingmoments_x2_kernel(
             )
             held["weighed", g, qq] = t
 
+        def f_weigh_tile(eng, g, qt):
+            if qt % 2 == 0:
+                held["weighed", g, qt // 2] = work.tile([128, 2, 512], BF16, name="fw", bufs=WEIGHED_BUFS)
+            factor = u_all if eng is vector else u_wide
+            eng.tensor_tensor(
+                out=held["weighed", g, qt // 2][:, qt % 2, :], in0=held["tanh", g, qt // 2][:, qt % 2, :], in1=factor[:], op=MULT
+            )
+
         def f_turn(g, qq):
             t = bank([128, 2, 256])
             for k in range(2):
@@ -291,12 +299,8 @@ def tile_adversarialsdfconditionalpricingmoments_x2_kernel(
         def f_copy(eng, g, qq):
             words = f_in[qq // 2][:, g, :, :].rearrange("p c k -> p (c k)").bitcast(F32)
             src = held["f", g, qq][:]
-            if qq < 2:
-                dst = words.rearrange("p (c e) -> p c e", e=2)[:, 256 * qq : 256 * (qq + 1), :]
-                copy(eng, dst, src.rearrange("p e c -> p c e"))
-            else:
-                dst = words.rearrange("p (s m e) -> p s m e", s=4, e=2)[:, :, 64 * (qq % 2) : 64 * (qq % 2 + 1), :]
-                copy(eng, dst, src.rearrange("p e (m s) -> p s m e", s=4))
+            dst = words.rearrange("p (c e) -> p c e", e=2)[:, 256 * (qq % 2) : 256 * (qq % 2 + 1), :]
+            copy(eng, dst, src.rearrange("p e c -> p c e"))
 
         def wide_turn(g, qt):
             t = bank([128, 4, 128])
@@ -305,7 +309,7 @@ def tile_adversarialsdfconditionalpricingmoments_x2_kernel(
             held["wide", g, qt] = t
 
         def wide_weigh(g, qt):
-            cols = f_in[qt // 4][:, g, :, :].rearrange("p %s j -> p m s j" % ("(m s)", "(s m)")[qt // 4], s=4)
+            cols = f_in[qt // 4][:, g, :, :].rearrange("p %s j -> p m s j" % "(m s)", s=4)
             vector.tensor_tensor(
                 out=cols[:, 32 * (qt % 4) : 32 * (qt % 4 + 1), :, :],
                 in0=held["wide", g, qt][:].rearrange("p j (m s) -> p m s j", s=4),
@@ -354,7 +358,7 @@ def tile_adversarialsdfconditionalpricingmoments_x2_kernel(
 
         def out_product(qh, it):
             t = bank([128, 512])
-            product(t[:], [(*d_operand(g, it), *f_operand(g, qh, 0, 512)) for g in range(2)])
+            product(t[:], [(*d_operand(g, it), *f_operand(g, qh, 0, 512)) for g in ((0, 1), (1, 0))[qh]])
             held["out", qh, it] = t
 
         def out_pass(qh, it, g):
@@ -371,7 +375,7 @@ def tile_adversarialsdfconditionalpricingmoments_x2_kernel(
             if it % 2 == 0:
                 held["sb", qh, it // 2] = work.tile([128, 2, 512], F32, name="osb", bufs=OUT_BUFS)
             t = held["sb", qh, it // 2][:, it % 2, :]
-            src = held["out", qh, it][:].rearrange("p %s -> p m s" % ("(m s)", "(s m)")[qh], s=4)
+            src = held["out", qh, it][:].rearrange("p %s -> p m s" % "(m s)", s=4)
             scaled(eng, t.rearrange("p (m s) -> p m s", s=4), src)
             nc.sync.dma_start(out=out_0[128 * it : 128 * (it + 1), 512 * qh : 512 * (qh + 1)], in_=t)
 
@@ -388,6 +392,10 @@ def tile_adversarialsdfconditionalpricingmoments_x2_kernel(
         def round_tile(eng, qh, it):
             dst = out_bf[qh][it // 2][:, it % 2, :].rearrange("p (e c b) -> p e c b", e=2, b=2)
             copy(eng, dst, held["sb", qh, it // 2][:, it % 2, :].rearrange("p (c e b) -> p e c b", e=2, b=2))
+
+        def round_bank(qh, it):
+            dst = out_bf[qh][it // 2][:, it % 2, :].rearrange("p (e c b) -> p e c b", e=2, b=2)
+            scaled(vector, dst, held["out", qh, it][:].rearrange("p (c e b) -> p e c b", e=2, b=2))
 
         def round_pair(eng, qh, ip):
             dst = out_bf[qh][ip][:].rearrange("p k (e c b) -> p k e c b", e=2, b=2)
@@ -464,6 +472,7 @@ def tile_adversarialsdfconditionalpricingmoments_x2_kernel(
         gpsimd.dma_start(out=v_sb[:], in_=v.rearrange("(g p j) -> p g j", p=128, j=4))
         gpsimd.tensor_scalar(out=neg_v[:], in0=v_sb[:], scalar1=-1.0 / ROOT, scalar2=0.0, op0=MULT, op1=ADD)
         scalar.activation(out=warm[:], in_=zero[:, 0:1], func=ACT.Tanh)
+        scalar.copy(out=eye[:], in_=ident[:, 0:8])
         warm_tensor(4)
         for j in range(2):
             z_turn(0, j)
@@ -473,16 +482,19 @@ def tile_adversarialsdfconditionalpricingmoments_x2_kernel(
         for j in range(2, 4):
             z_turn(0, j)
             z_copy(0, j)
+        z_quantise(0, 2, 3)
         om(0, 0, 0)
-        z_quantise(0, 2, 4)
+        z_quantise(0, 3, 4)
         om(0, 0, 1)
-        bias_columns()
         om(0, 1, 0)
         om(0, 1, 1)
+        bias_columns()
         z_sort(1, 0)
         z_sort(1, 1)
         sdf(0, 0, 1, gpsimd)
         d_scale_rows(gpsimd, 0, 0)
+        sdf(0, 1, 2, gpsimd)
+        d_scale_rows(gpsimd, 0, 1)
         om(0, 2, 0)
         om(0, 2, 1)
         om_product(0, 3, 0)
@@ -491,9 +503,8 @@ def tile_adversarialsdfconditionalpricingmoments_x2_kernel(
             z_turn(1, j)
             z_copy(1, j)
         om_sum(0, 3, 0)
-        sdf(0, 1, 3)
+        sdf(0, 2, 3)
         om_sum(0, 3, 1)
-        d_scale_rows(vector, 0, 1)
         z_quantise(1, 0, 2)
         sdf(0, 3, 4)
         d_scale_rows(vector, 0, 2)
@@ -502,10 +513,12 @@ def tile_adversarialsdfconditionalpricingmoments_x2_kernel(
         instrument(0, 0)
         instrument(0, 1)
         spread_u()
-        d_interleave(scalar, 0, 0)
-        d_interleave(gpsimd, 0, 1)
-        d_interleave(scalar, 0, 2)
+        scalar.copy(out=u_wide[:], in_=u_all[:])
         d_interleave(gpsimd, 0, 3)
+        f_weigh_tile(gpsimd, 0, 0)
+        f_weigh_tile(gpsimd, 0, 1)
+        for quarter_i in range(3):
+            d_interleave(scalar, 0, quarter_i)
         for j in range(3):
             om(1, j, 0)
             om(1, j, 1)
@@ -523,8 +536,6 @@ def tile_adversarialsdfconditionalpricingmoments_x2_kernel(
         d_quantise(0, 0)
         d_scale_rows(vector, 1, 3)
         d_interleave(gpsimd, 1, 0)
-        d_interleave(gpsimd, 1, 2)
-        f_weigh(0, 0)
         f_weigh(0, 1)
         instrument(0, 4)
         instrument(0, 5)
@@ -545,23 +556,21 @@ def tile_adversarialsdfconditionalpricingmoments_x2_kernel(
         f_quantise(0, 0, 0, 512)
         f_quantise(1, 0, 0, 512)
         d_quantise(0, 1)
-        d_quantise_quarter(1, 2)
-        d_interleave(gpsimd, 1, 3)
+        d_interleave(gpsimd, 1, 2)
         f_weigh(0, 2)
         f_weigh(0, 3)
         for it in range(4):
             out(0, it)
+        round_tile(vector, 0, 0)
+        d_quantise_quarter(1, 2)
+        d_interleave(gpsimd, 1, 3)
         for qt in range(4, 8):
             wide_turn(1, qt)
         ring.append(7)
         f_turn(0, 2)
         f_turn(0, 3)
-        for it in range(2):
-            round_tile(gpsimd, 0, it)
         for qt in range(4, 8):
             wide_weigh(1, qt)
-        round_tile(scalar, 0, 2)
-        round_tile(scalar, 0, 3)
         f_copy(scalar, 0, 2)
         f_copy(scalar, 0, 3)
         d_quantise_quarter(1, 3)
@@ -569,47 +578,36 @@ def tile_adversarialsdfconditionalpricingmoments_x2_kernel(
             out(0, it)
         f_quantise(1, 1, 0, 512)
         f_quantise(0, 1, 0, 512)
-        plane_turn(0, 0)
-        plane_turn(0, 1)
-        round_pair(vector, 0, 2)
-        plane_copy(vector, 0, 0)
-        plane_copy(vector, 0, 1)
-        round_pair(vector, 0, 3)
+        round_tile(vector, 0, 1)
+        round_pair(vector, 0, 1)
         out(1, 0)
+        round_pair(vector, 0, 2)
         out(1, 1)
+        round_pair(vector, 0, 3)
+        for ip in range(1, 4):
+            out(1, 2 * ip)
+            round_pair(vector, 1, ip - 1)
+            out(1, 2 * ip + 1)
+        for ip in range(4):
+            plane_turn(0, ip)
+        plane_copy(vector, 0, 0)
+        plane_copy(scalar, 0, 1)
+        round_pair(vector, 1, 3)
+        plane_copy(scalar, 0, 2)
         plane_quantise(0, 0, 512)
         plane_store(0, 0, 512)
-        out(1, 2)
-        round_pair(vector, 1, 0)
-        out(1, 3)
-        out(1, 4)
-        round_pair(vector, 1, 1)
-        out(1, 5)
-        plane_turn(0, 2)
-        plane_turn(0, 3)
-        plane_turn(1, 0)
-        plane_turn(1, 1)
-        plane_copy(vector, 0, 2)
         plane_copy(scalar, 0, 3)
-        round_pair(vector, 1, 2)
-        plane_copy(scalar, 1, 0)
+        for ip in range(4):
+            plane_turn(1, ip)
+        plane_copy(vector, 1, 0)
+        plane_copy(scalar, 1, 1)
         plane_quantise(0, 512, 1024)
         plane_store(0, 512, 1024)
-        plane_copy(scalar, 1, 1)
-        plane_product(6)
-        plane_product(7)
-        plane_scale(vector, 6)
-        out_product(1, 6)
-        plane_turn(1, 2)
+        plane_copy(scalar, 1, 2)
         plane_quantise(1, 0, 512)
         plane_store(1, 0, 512)
-        plane_scale(scalar, 7)
-        plane_quantise(1, 768, 1024)
-        out_store(1, 6)
-        plane_store(1, 768, 1024)
-        plane_copy(vector, 1, 2)
-        out_product(1, 7)
+        plane_copy(scalar, 1, 3)
         plane_quantise(1, 512, 768)
-        plane_store(1, 512, 768)
-        out_store(1, 7)
+        plane_quantise(1, 768, 1024)
+        plane_store(1, 512, 1024)
         plane_scales_store()

@@ -461,8 +461,8 @@ def tile_adversarialsdfconditionalpricingmoments_x2_kernel(
         load_z(1, 0, 2)
         load_r(0, 2, 4)
         load_z(1, 2, 4)
-        load_wg(0)
         load_scales(nc.sync, "g", wg_scales)
+        load_wg(0)
         nc.sync.dma_start(out=u_row[0:1, :], in_=u[0:512].rearrange("(a t) -> a t", a=1))
         load_r(1, 0, 2)
         load_r(1, 2, 4)
@@ -540,6 +540,7 @@ def tile_adversarialsdfconditionalpricingmoments_x2_kernel(
         instrument(0, 4)
         instrument(0, 5)
         d_interleave(scalar, 1, 1)
+        f_weigh_tile(gpsimd, 0, 4)
         for qt in range(4):
             wide_turn(1, qt)
         f_turn(0, 0)
@@ -557,28 +558,29 @@ def tile_adversarialsdfconditionalpricingmoments_x2_kernel(
         f_quantise(1, 0, 0, 512)
         d_quantise(0, 1)
         d_interleave(gpsimd, 1, 2)
-        f_weigh(0, 2)
+        f_weigh_tile(vector, 0, 5)
         f_weigh(0, 3)
-        for it in range(4):
+        for it in range(3):
             out(0, it)
-        round_tile(vector, 0, 0)
         d_quantise_quarter(1, 2)
         d_interleave(gpsimd, 1, 3)
-        for qt in range(4, 8):
-            wide_turn(1, qt)
-        ring.append(7)
+        wide_turn(1, 4)
+        wide_turn(1, 5)
         f_turn(0, 2)
+        wide_turn(1, 6)
+        wide_turn(1, 7)
+        ring.append(7)
         f_turn(0, 3)
         for qt in range(4, 8):
             wide_weigh(1, qt)
         f_copy(scalar, 0, 2)
         f_copy(scalar, 0, 3)
         d_quantise_quarter(1, 3)
-        for it in range(4, 8):
+        for it in range(3, 8):
             out(0, it)
         f_quantise(1, 1, 0, 512)
         f_quantise(0, 1, 0, 512)
-        round_tile(vector, 0, 1)
+        round_pair(vector, 0, 0)
         round_pair(vector, 0, 1)
         out(1, 0)
         round_pair(vector, 0, 2)
@@ -610,4 +612,4 @@ def tile_adversarialsdfconditionalpricingmoments_x2_kernel(
         plane_quantise(1, 512, 768)
         plane_quantise(1, 768, 1024)
         plane_store(1, 512, 1024)
-        plane_scales_store()
+        plane_scales_store(scalar)

@@ -152,9 +152,9 @@ def tile_adversarialsdfconditionalpricingmoments_x2_kernel(
             dst = dst.rearrange("p (h a c e) -> p h a c e", h=2, a=2, e=2)
             scalar.copy(out=dst[:, :, j % 2, :, :], in_=held["z", g, j][:].rearrange("p h e c -> p h c e"))
 
-        def z_quantise(g, j0, j1):
+        def z_quantise(g, j0, j1, groups=(0, 1)):
             cols = slice(128 * j0, 128 * j1)
-            for kg in range(2):
+            for kg in groups:
                 src = z_in[g][j0 // 2][:, kg, 128 * (j0 % 2) : 128 * (j0 % 2 + j1 - j0), :]
                 quantise(z_code[g][kg][:, cols], z_scale[g][kg][:, cols], src)
 
@@ -444,16 +444,16 @@ def tile_adversarialsdfconditionalpricingmoments_x2_kernel(
 
         vector.memset(zero[:], 0.0)
         zero_scales(vector, "o")
+        vector.memset(u_row[:], 0.0)
         vector.memset(ident[:], 0.0)
         make_identity(nc, ident[:], nomemset=True)
         vector.memset(ones[:], 1.0)
         vector.memset(sums[:, :, :, 2:3], -ROOT)
         vector.memset(bg_rows[:], 0.0)
         zero_scales(vector, "g")
-        vector.memset(u_row[:], 0.0)
-        load_z(0, 0, 1)
-        load_z(0, 1, 2)
+        load_z(0, 0, 2)
         load_z(0, 2, 4)
+        nc.sync.dma_start(out=u_row[0:1, :], in_=u[0:512].rearrange("(a t) -> a t", a=1))
         nc.sync.dma_start(out=wo_sb[:].bitcast(I32), in_=wo_words.rearrange("g p n -> p g n").bitcast(I32))
         load_scales(scalar, "o", wo_scales)
         load_r(0, 0, 1)
@@ -463,7 +463,6 @@ def tile_adversarialsdfconditionalpricingmoments_x2_kernel(
         load_z(1, 2, 4)
         load_scales(nc.sync, "g", wg_scales)
         load_wg(0)
-        nc.sync.dma_start(out=u_row[0:1, :], in_=u[0:512].rearrange("(a t) -> a t", a=1))
         load_r(1, 0, 2)
         load_r(1, 2, 4)
         load_wg(1)
@@ -473,21 +472,22 @@ def tile_adversarialsdfconditionalpricingmoments_x2_kernel(
         gpsimd.tensor_scalar(out=neg_v[:], in0=v_sb[:], scalar1=-1.0 / ROOT, scalar2=0.0, op0=MULT, op1=ADD)
         scalar.activation(out=warm[:], in_=zero[:, 0:1], func=ACT.Tanh)
         scalar.copy(out=eye[:], in_=ident[:, 0:8])
-        warm_tensor(4)
+        warm_tensor(5)
         for j in range(2):
             z_turn(0, j)
             z_copy(0, j)
             z_quantise(0, j, j + 1)
-        warm_tensor(2)
         for j in range(2, 4):
             z_turn(0, j)
             z_copy(0, j)
+        spread_u()
         z_quantise(0, 2, 3)
         om(0, 0, 0)
         z_quantise(0, 3, 4)
         om(0, 0, 1)
         om(0, 1, 0)
         om(0, 1, 1)
+        scalar.copy(out=u_wide[:], in_=u_all[:])
         bias_columns()
         z_sort(1, 0)
         z_sort(1, 1)
@@ -503,38 +503,32 @@ def tile_adversarialsdfconditionalpricingmoments_x2_kernel(
             z_turn(1, j)
             z_copy(1, j)
         om_sum(0, 3, 0)
-        sdf(0, 2, 3)
         om_sum(0, 3, 1)
-        z_quantise(1, 0, 2)
-        sdf(0, 3, 4)
+        z_quantise(1, 0, 2, (0,))
+        sdf(0, 2, 4)
+        z_quantise(1, 0, 2, (1,))
         d_scale_rows(vector, 0, 2)
         z_quantise(1, 2, 4)
         d_scale_rows(vector, 0, 3)
         instrument(0, 0)
         instrument(0, 1)
-        spread_u()
-        scalar.copy(out=u_wide[:], in_=u_all[:])
+        instrument(0, 2)
         d_interleave(gpsimd, 0, 3)
         f_weigh_tile(gpsimd, 0, 0)
         f_weigh_tile(gpsimd, 0, 1)
         for quarter_i in range(3):
             d_interleave(scalar, 0, quarter_i)
-        for j in range(3):
+        for j in range(4):
             om(1, j, 0)
             om(1, j, 1)
-        om(1, 3, 0)
-        sdf(1, 0, 3)
-        om(1, 3, 1)
-        instrument(0, 2)
         instrument(0, 3)
         for qt in range(4):
             instrument(1, qt)
-        d_scale_rows(vector, 1, 0)
-        d_scale_rows(vector, 1, 1)
-        sdf(1, 3, 4)
-        d_scale_rows(vector, 1, 2)
+        sdf(1, 0, 3)
         d_quantise(0, 0)
-        d_scale_rows(vector, 1, 3)
+        sdf(1, 3, 4)
+        for j in range(4):
+            d_scale_rows(vector, 1, j)
         d_interleave(gpsimd, 1, 0)
         f_weigh(0, 1)
         instrument(0, 4)

@@ -377,7 +377,11 @@ def tile_adversarialsdfconditionalpricingmoments_x2_kernel(
             t = held["sb", qh, it // 2][:, it % 2, :]
             src = held["out", qh, it][:].rearrange("p %s -> p m s" % "(m s)", s=4)
             scaled(eng, t.rearrange("p (m s) -> p m s", s=4), src)
-            nc.sync.dma_start(out=out_0[128 * it : 128 * (it + 1), 512 * qh : 512 * (qh + 1)], in_=t)
+            if qh == 0:
+                nc.sync.dma_start(out=out_0[128 * it : 128 * (it + 1), 0:512], in_=t)
+            elif it % 2 == 1:
+                rows = out_0[128 * (it - 1) : 128 * (it + 1), 512:1024].rearrange("(k p) c -> p k c", p=128)
+                nc.sync.dma_start(out=rows, in_=held["sb", qh, it // 2][:])
 
         def scaled(eng, dst, src):
             if eng is scalar:

@@ -53,7 +53,7 @@ def tile_adversarialsdfconditionalpricingmoments_x2_kernel(
         bg_cols = kept("bg_t", [128, 8], F32)
         v_sb = kept("v", [128, 2, 4], BF16)
         neg_v = kept("nv", [128, 2, 4], F32)
-        u_sb = kept("u", [128, 2, 4], BF16)
+        u_sb = kept("u", [128, 4], BF16)
         u_row = kept("u_row", [128, 512], BF16)
         ones = kept("ones", [128, 128], BF16)
         u_all = psum.tile([128, 512], F32, name="u_all", tag="bank7")
@@ -313,7 +313,7 @@ def tile_adversarialsdfconditionalpricingmoments_x2_kernel(
             vector.tensor_tensor(
                 out=cols[:, 32 * (qt % 4) : 32 * (qt % 4 + 1), :, :],
                 in0=held["wide", g, qt][:].rearrange("p j (m s) -> p m s j", s=4),
-                in1=u_sb[:, g, :].unsqueeze(1).unsqueeze(1).to_broadcast([128, 32, 4, 4]),
+                in1=u_sb[:].unsqueeze(1).unsqueeze(1).to_broadcast([128, 32, 4, 4]),
                 op=MULT,
             )
 
@@ -460,8 +460,7 @@ def tile_adversarialsdfconditionalpricingmoments_x2_kernel(
         nc.sync.dma_start(out=u_row[0:1, :], in_=u[0:512].rearrange("(a t) -> a t", a=1))
         nc.sync.dma_start(out=wo_sb[:].bitcast(I32), in_=wo_words.rearrange("g p n -> p g n").bitcast(I32))
         load_scales(scalar, "o", wo_scales)
-        load_r(0, 0, 1)
-        load_r(0, 1, 2)
+        load_r(0, 0, 2)
         load_z(1, 0, 2)
         load_r(0, 2, 4)
         load_z(1, 2, 4)
@@ -470,7 +469,7 @@ def tile_adversarialsdfconditionalpricingmoments_x2_kernel(
         load_r(1, 0, 2)
         load_r(1, 2, 4)
         load_wg(1)
-        nc.sync.dma_start(out=u_sb[:], in_=u.rearrange("(g p j) -> p g j", p=128, j=4))
+        nc.sync.dma_start(out=u_sb[:], in_=u[512:1024].rearrange("(p j) -> p j", j=4))
         gpsimd.dma_start(out=bg_rows[0:8, :], in_=bg.rearrange("(a p) -> a p", p=128))
         gpsimd.dma_start(out=v_sb[:], in_=v.rearrange("(g p j) -> p g j", p=128, j=4))
         gpsimd.tensor_scalar(out=neg_v[:], in0=v_sb[:], scalar1=-1.0 / ROOT, scalar2=0.0, op0=MULT, op1=ADD)
@@ -486,8 +485,8 @@ def tile_adversarialsdfconditionalpricingmoments_x2_kernel(
             z_copy(0, j)
         spread_u()
         z_quantise(0, 2, 3)
-        om(0, 0, 0)
         z_quantise(0, 3, 4)
+        om(0, 0, 0)
         om(0, 0, 1)
         om(0, 1, 0)
         om(0, 1, 1)

@@ -475,15 +475,17 @@ def tile_adversarialsdfconditionalpricingmoments_x2_kernel(
         gpsimd.tensor_scalar(out=neg_v[:], in0=v_sb[:], scalar1=-1.0 / ROOT, scalar2=0.0, op0=MULT, op1=ADD)
         scalar.activation(out=warm[:], in_=zero[:, 0:1], func=ACT.Tanh)
         scalar.copy(out=eye[:], in_=ident[:, 0:8])
-        warm_tensor(5)
+        warm_tensor(4)
         for j in range(2):
             z_turn(0, j)
             z_copy(0, j)
             z_quantise(0, j, j + 1)
+        warm_tensor(1)
         for j in range(2, 4):
             z_turn(0, j)
             z_copy(0, j)
         spread_u()
+        warm_tensor(1)
         z_quantise(0, 2, 3)
         z_quantise(0, 3, 4)
         om(0, 0, 0)

@@ -48,7 +48,7 @@ def tile_adversarialsdfconditionalpricingmoments_x2_kernel(
         r_rows = [kept("r%d" % g, [128, 4, N], BF16) for g in range(2)]
         wo_sb = kept("wo", [128, 2, 2048], U8)
         wg_sb = [kept("wg%d" % qh, [128, 2, 1024], U8) for qh in range(2)]
-        w_scale = {name: kept("ws" + name, [128, 2, N], U8) for name in "og"}
+        w_scale = {"o": kept("wso", [128, 2, N], U8), 0: kept("wsg0", [128, 2, 512], U8), 1: kept("wsg1", [128, 2, 512], U8)}
         bg_rows = kept("bg_rows", [128, 128], BF16)
         bg_cols = kept("bg_t", [128, 8], F32)
         v_sb = kept("v", [128, 2, 4], BF16)
@@ -246,7 +246,7 @@ def tile_adversarialsdfconditionalpricingmoments_x2_kernel(
                 [
                     (
                         wg_sb[qt // 4][:, kg, 256 * (qt % 4) : 256 * (qt % 4 + 1)].bitcast(E2M1),
-                        w_scale["g"][:, kg, 128 * qt : 128 * (qt + 1)],
+                        w_scale[qt // 4][:, kg, 128 * (qt % 4) : 128 * (qt % 4 + 1)],
                         z_code[g][kg][:].bitcast(E4M3),
                         z_scale[g][kg][:],
                     )
@@ -270,12 +270,13 @@ def tile_adversarialsdfconditionalpricingmoments_x2_kernel(
             x_product(g, qt)
             x_tanh(g, qt)
 
-        def f_weigh(g, qq):
+        def f_weigh(g, qq, eng=vector):
             t = work.tile([128, 2, 512], BF16, name="fw", bufs=WEIGHED_BUFS)
-            vector.tensor_tensor(
+            factor = u_all if eng is vector else u_wide
+            eng.tensor_tensor(
                 out=t[:],
                 in0=held["tanh", g, qq][:],
-                in1=u_all[:].unsqueeze(1).to_broadcast([128, 2, 512]),
+                in1=factor[:].unsqueeze(1).to_broadcast([128, 2, 512]),
                 op=MULT,
             )
             held["weighed", g, qq] = t
@@ -315,6 +316,13 @@ def tile_adversarialsdfconditionalpricingmoments_x2_kernel(
                 in0=held["wide", g, qt][:].rearrange("p j (m s) -> p m s j", s=4),
                 in1=u_sb[:].unsqueeze(1).unsqueeze(1).to_broadcast([128, 32, 4, 4]),
                 op=MULT,
+            )
+
+        def f_quantise_both(qh):
+            quantise(
+                f_code[qh][:].rearrange("p g c -> p (g c)"),
+                f_scale[qh][:].rearrange("p g c -> p (g c)"),
+                f_in[qh][:].rearrange("p g c k -> p (g c) k"),
             )
 
         def f_quantise(g, qh, c0, c1):
@@ -446,15 +454,16 @@ def tile_adversarialsdfconditionalpricingmoments_x2_kernel(
                     out=out_2[:, 4 * c : 4 * c + 4, :].bitcast(I32), in_=p_scale[32 * c : 32 * c + 8, :].bitcast(I32)
                 )
 
-        vector.memset(zero[:], 0.0)
+        vector.memset(zero[:].bitcast(U32), 0)
         zero_scales(vector, "o")
-        vector.memset(u_row[:], 0.0)
+        vector.memset(u_row[:].bitcast(U32), 0)
         vector.memset(ident[:], 0.0)
         make_identity(nc, ident[:], nomemset=True)
         vector.memset(ones[:], 1.0)
         vector.memset(sums[:, :, :, 2:3], -ROOT)
-        vector.memset(bg_rows[:], 0.0)
-        zero_scales(vector, "g")
+        vector.memset(bg_rows[:].bitcast(U32), 0)
+        zero_scales(vector, 0)
+        zero_scales(vector, 1)
         load_z(0, 0, 2)
         load_z(0, 2, 4)
         nc.sync.dma_start(out=u_row[0:1, :], in_=u[0:512].rearrange("(a t) -> a t", a=1))
@@ -464,10 +473,11 @@ def tile_adversarialsdfconditionalpricingmoments_x2_kernel(
         load_z(1, 0, 2)
         load_r(0, 2, 4)
         load_z(1, 2, 4)
-        load_scales(nc.sync, "g", wg_scales)
+        load_scales(nc.sync, 0, wg_scales[:, :, 0:512])
         load_wg(0)
         load_r(1, 0, 2)
         load_r(1, 2, 4)
+        load_scales(nc.sync, 1, wg_scales[:, :, 512:1024])
         load_wg(1)
         nc.sync.dma_start(out=u_sb[:], in_=u[512:1024].rearrange("(p j) -> p j", j=4))
         gpsimd.dma_start(out=bg_rows[0:8, :], in_=bg.rearrange("(a p) -> a p", p=128))
@@ -519,10 +529,10 @@ def tile_adversarialsdfconditionalpricingmoments_x2_kernel(
         instrument(0, 1)
         instrument(0, 2)
         d_interleave(gpsimd, 0, 3)
-        f_weigh_tile(gpsimd, 0, 0)
-        f_weigh_tile(gpsimd, 0, 1)
-        for quarter_i in range(3):
-            d_interleave(scalar, 0, quarter_i)
+        f_weigh(0, 0, gpsimd)
+        f_weigh_tile(gpsimd, 0, 2)
+        copy(scalar, d_in[0][:, 0:512, :], r_rows[0][:, :, 0:512].rearrange("p j c -> p c j"))
+        d_interleave(scalar, 0, 2)
         for j in range(4):
             om(1, j, 0)
             om(1, j, 1)
@@ -534,12 +544,10 @@ def tile_adversarialsdfconditionalpricingmoments_x2_kernel(
         sdf(1, 3, 4)
         for j in range(4):
             d_scale_rows(vector, 1, j)
-        d_interleave(gpsimd, 1, 0)
-        f_weigh(0, 1)
+        copy(gpsimd, d_in[1][:, 0:512, :], r_rows[1][:, :, 0:512].rearrange("p j c -> p c j"))
+        f_weigh_tile(vector, 0, 3)
         instrument(0, 4)
         instrument(0, 5)
-        d_interleave(scalar, 1, 1)
-        f_weigh_tile(gpsimd, 0, 4)
         for qt in range(4):
             wide_turn(1, qt)
         f_turn(0, 0)
@@ -553,11 +561,10 @@ def tile_adversarialsdfconditionalpricingmoments_x2_kernel(
         for qt in range(4, 8):
             instrument(1, qt)
         d_quantise(1, 0)
-        f_quantise(0, 0, 0, 512)
-        f_quantise(1, 0, 0, 512)
+        f_quantise_both(0)
         d_quantise(0, 1)
         d_interleave(gpsimd, 1, 2)
-        f_weigh_tile(vector, 0, 5)
+        f_weigh(0, 2)
         f_weigh(0, 3)
         for it in range(3):
             out(0, it)
@@ -585,15 +592,21 @@ def tile_adversarialsdfconditionalpricingmoments_x2_kernel(
         round_pair(vector, 0, 2)
         out(1, 1)
         round_pair(vector, 0, 3)
-        for ip in range(1, 4):
-            out(1, 2 * ip)
-            round_pair(vector, 1, ip - 1)
-            out(1, 2 * ip + 1)
+        out(1, 2)
+        round_pair(vector, 1, 0)
+        out(1, 3)
+        out(1, 4, vector)
+        round_pair(vector, 1, 1)
+        out(1, 5)
+        out(1, 6)
+        round_pair(vector, 1, 2)
+        out(1, 7)
+        round_tile(vector, 1, 6)
         for ip in range(4):
             plane_turn(0, ip)
-        plane_copy(vector, 0, 0)
-        plane_copy(scalar, 0, 1)
-        round_pair(vector, 1, 3)
+        plane_copy(scalar, 0, 0)
+        plane_copy(vector, 0, 1)
+        round_tile(vector, 1, 7)
         plane_copy(scalar, 0, 2)
         plane_quantise(0, 0, 512)
         plane_store(0, 0, 512)

@@ -528,11 +528,11 @@ def tile_adversarialsdfconditionalpricingmoments_x2_kernel(
         instrument(0, 0)
         instrument(0, 1)
         instrument(0, 2)
-        d_interleave(gpsimd, 0, 3)
+        copy(gpsimd, d_in[0][:, 896:1024, :], r_rows[0][:, :, 896:1024].rearrange("p j c -> p c j"))
         f_weigh(0, 0, gpsimd)
         f_weigh_tile(gpsimd, 0, 2)
         copy(scalar, d_in[0][:, 0:512, :], r_rows[0][:, :, 0:512].rearrange("p j c -> p c j"))
-        d_interleave(scalar, 0, 2)
+        copy(scalar, d_in[0][:, 512:896, :], r_rows[0][:, :, 512:896].rearrange("p j c -> p c j"))
         for j in range(4):
             om(1, j, 0)
             om(1, j, 1)
@@ -544,10 +544,11 @@ def tile_adversarialsdfconditionalpricingmoments_x2_kernel(
         sdf(1, 3, 4)
         for j in range(4):
             d_scale_rows(vector, 1, j)
-        copy(gpsimd, d_in[1][:, 0:512, :], r_rows[1][:, :, 0:512].rearrange("p j c -> p c j"))
+        copy(gpsimd, d_in[1][:, 0:448, :], r_rows[1][:, :, 0:448].rearrange("p j c -> p c j"))
         f_weigh_tile(vector, 0, 3)
         instrument(0, 4)
         instrument(0, 5)
+        copy(scalar, d_in[1][:, 448:512, :], r_rows[1][:, :, 448:512].rearrange("p j c -> p c j"))
         for qt in range(4):
             wide_turn(1, qt)
         f_turn(0, 0)

@@ -18,7 +18,7 @@ T, D, N, Q = 1024, 1024, 1024, 1024
 ROOT = 32.0
 TANH_BUFS = 8
 WEIGHED_BUFS = 4
-OUT_BUFS = 5
+OUT_BUFS = 8
 WIDE = ((1, 0), (1, 1), (1, 2), (1, 3))
 FLOPS = 3 * 2 * 1024 * 1024 * 1024
 
@@ -46,8 +46,8 @@ def tile_adversarialsdfconditionalpricingmoments_x2_kernel(
         ident = kept("ident", [128, 128], F32)
         z_rows = {}
         r_rows = [kept("r%d" % g, [128, 4, N], BF16) for g in range(2)]
-        wo_sb = kept("wo", [128, 2, 2048], U8)
-        wg_sb = [kept("wg%d" % qh, [128, 2, 1024], U8) for qh in range(2)]
+        wo_sb = [kept("wo%d" % kg, [128, 2048], U8) for kg in range(2)]
+        wg_sb = [kept("wg%d" % kg, [128, 2048], U8) for kg in range(2)]
         w_scale = {"o": kept("wso", [128, 2, N], U8), 0: kept("wsg0", [128, 2, 512], U8), 1: kept("wsg1", [128, 2, 512], U8)}
         bg_rows = kept("bg_rows", [128, 128], BF16)
         bg_cols = kept("bg_t", [128, 8], F32)
@@ -114,9 +114,8 @@ def tile_adversarialsdfconditionalpricingmoments_x2_kernel(
                     in_=src[:, c:16:4, :].rearrange("g q n -> q g n").bitcast(I32),
                 )
 
-        def load_wg(qh):
-            half = wg_words.rearrange("g p n -> p g n")[:, :, 1024 * qh : 1024 * (qh + 1)]
-            nc.sync.dma_start(out=wg_sb[qh][:].bitcast(I32), in_=half.bitcast(I32))
+        def load_words(tiles, src, kg):
+            nc.sync.dma_start(out=tiles[kg][:].bitcast(I32), in_=src[kg].bitcast(I32))
 
         def zero_scales(eng, name):
             eng.memset(w_scale[name][:].rearrange("p g n -> p (g n)").bitcast(I32), 0)
@@ -131,7 +130,7 @@ def tile_adversarialsdfconditionalpricingmoments_x2_kernel(
             nc.tensor.matmul(u_all[:], ones[:], row, start=True, stop=True)
 
         def z_sort(g, j):
-            t = work.tile([128, 2, 2, 128], U32, name="zsort", bufs=4)
+            t = work.tile([128, 2, 2, 128], U32, name="zsort", bufs=2)
             scalar.copy(out=t[:], in_=z_rows[g, j].bitcast(U32).rearrange("p (h c e) -> p h e c", h=2, e=2))
             held["sorted", g, j] = t
 
@@ -158,25 +157,26 @@ def tile_adversarialsdfconditionalpricingmoments_x2_kernel(
                 src = z_in[g][j0 // 2][:, kg, 128 * (j0 % 2) : 128 * (j0 % 2 + j1 - j0), :]
                 quantise(z_code[g][kg][:, cols], z_scale[g][kg][:, cols], src)
 
-        def om_product(g, j, ih):
-            t = bank([128, 512])
+        def om_pass(g, j, ih, kg):
+            if kg == 0:
+                held["om", g, j, ih] = bank([128, 512])
             cols = slice(128 * j, 128 * (j + 1))
-            product(
-                t[:],
-                [
-                    (
-                        z_code[g][kg][:, cols].bitcast(E4M3),
-                        z_scale[g][kg][:, cols],
-                        wo_sb[:, kg, 1024 * ih : 1024 * (ih + 1)].bitcast(E2M1),
-                        w_scale["o"][:, kg, 512 * ih : 512 * (ih + 1)],
-                    )
-                    for kg in range(2)
-                ],
+            nc.tensor.matmul_mx(
+                out=held["om", g, j, ih][:],
+                lhsT=z_code[g][kg][:, cols].bitcast(E4M3),
+                lhsT_scale=z_scale[g][kg][:, cols],
+                rhs=wo_sb[kg][:, 1024 * ih : 1024 * (ih + 1)].bitcast(E2M1),
+                rhs_scale=w_scale["o"][:, kg, 512 * ih : 512 * (ih + 1)],
+                start=kg == 0,
+                stop=kg == 1,
             )
-            held["om", g, j, ih] = t
+
+        def om_product(g, j, ih):
+            om_pass(g, j, ih, 0)
+            om_pass(g, j, ih, 1)
 
         def om_sum(g, j, ih):
-            prod = work.tile([128, 512], F32, name="junk", bufs=2)
+            prod = work.tile([128, 512], BF16, name="junk", bufs=8)
             vector.scalar_tensor_tensor(
                 out=prod[:],
                 in0=held["om", g, j, ih][:],
@@ -239,21 +239,22 @@ def tile_adversarialsdfconditionalpricingmoments_x2_kernel(
             nc.tensor.matmul(t[:], bg_rows[:], eye[:], start=True, stop=True)
             scalar.copy(out=bg_cols[:], in_=t[:])
 
-        def x_product(g, qt):
-            x = bank([128, 512])
-            product(
-                x[:],
-                [
-                    (
-                        wg_sb[qt // 4][:, kg, 256 * (qt % 4) : 256 * (qt % 4 + 1)].bitcast(E2M1),
-                        w_scale[qt // 4][:, kg, 128 * (qt % 4) : 128 * (qt % 4 + 1)],
-                        z_code[g][kg][:].bitcast(E4M3),
-                        z_scale[g][kg][:],
-                    )
-                    for kg in range(2)
-                ],
+        def x_pass(g, qt, kg):
+            if kg == 0:
+                held["x", g, qt] = bank([128, 512])
+            nc.tensor.matmul_mx(
+                out=held["x", g, qt][:],
+                lhsT=wg_sb[kg][:, 256 * qt : 256 * (qt + 1)].bitcast(E2M1),
+                lhsT_scale=w_scale[qt // 4][:, kg, 128 * (qt % 4) : 128 * (qt % 4 + 1)],
+                rhs=z_code[g][kg][:].bitcast(E4M3),
+                rhs_scale=z_scale[g][kg][:],
+                start=kg == 0,
+                stop=kg == 1,
             )
-            held["x", g, qt] = x
+
+        def x_product(g, qt):
+            x_pass(g, qt, 0)
+            x_pass(g, qt, 1)
 
         def x_tanh(g, qt):
             if qt % 2 == 0:
@@ -467,18 +468,19 @@ def tile_adversarialsdfconditionalpricingmoments_x2_kernel(
         load_z(0, 0, 2)
         load_z(0, 2, 4)
         nc.sync.dma_start(out=u_row[0:1, :], in_=u[0:512].rearrange("(a t) -> a t", a=1))
-        nc.sync.dma_start(out=wo_sb[:].bitcast(I32), in_=wo_words.rearrange("g p n -> p g n").bitcast(I32))
+        load_words(wo_sb, wo_words, 0)
         load_scales(scalar, "o", wo_scales)
+        load_words(wo_sb, wo_words, 1)
         load_r(0, 0, 2)
         load_z(1, 0, 2)
         load_r(0, 2, 4)
         load_z(1, 2, 4)
         load_scales(nc.sync, 0, wg_scales[:, :, 0:512])
-        load_wg(0)
+        load_words(wg_sb, wg_words, 0)
+        load_words(wg_sb, wg_words, 1)
         load_r(1, 0, 2)
         load_r(1, 2, 4)
         load_scales(nc.sync, 1, wg_scales[:, :, 512:1024])
-        load_wg(1)
         nc.sync.dma_start(out=u_sb[:], in_=u[512:1024].rearrange("(p j) -> p j", j=4))
         gpsimd.dma_start(out=bg_rows[0:8, :], in_=bg.rearrange("(a p) -> a p", p=128))
         gpsimd.dma_start(out=v_sb[:], in_=v.rearrange("(g p j) -> p g j", p=128, j=4))
@@ -495,11 +497,13 @@ def tile_adversarialsdfconditionalpricingmoments_x2_kernel(
             z_turn(0, j)
             z_copy(0, j)
         spread_u()
-        warm_tensor(1)
         z_quantise(0, 2, 3)
         z_quantise(0, 3, 4)
-        om(0, 0, 0)
-        om(0, 0, 1)
+        for kg in range(2):
+            om_pass(0, 0, 0, kg)
+            om_pass(0, 0, 1, kg)
+        om_sum(0, 0, 0)
+        om_sum(0, 0, 1)
         om(0, 1, 0)
         om(0, 1, 1)
         scalar.copy(out=u_wide[:], in_=u_all[:])
@@ -525,8 +529,11 @@ def tile_adversarialsdfconditionalpricingmoments_x2_kernel(
         d_scale_rows(vector, 0, 2)
         z_quantise(1, 2, 4)
         d_scale_rows(vector, 0, 3)
-        instrument(0, 0)
-        instrument(0, 1)
+        for kg in range(2):
+            for qt in range(2):
+                x_pass(0, qt, kg)
+        x_tanh(0, 0)
+        x_tanh(0, 1)
         instrument(0, 2)
         copy(gpsimd, d_in[0][:, 896:1024, :], r_rows[0][:, :, 896:1024].rearrange("p j c -> p c j"))
         f_weigh(0, 0, gpsimd)

@@ -538,8 +538,8 @@ def tile_adversarialsdfconditionalpricingmoments_x2_kernel(
         copy(gpsimd, d_in[0][:, 896:1024, :], r_rows[0][:, :, 896:1024].rearrange("p j c -> p c j"))
         f_weigh(0, 0, gpsimd)
         f_weigh_tile(gpsimd, 0, 2)
-        copy(scalar, d_in[0][:, 0:512, :], r_rows[0][:, :, 0:512].rearrange("p j c -> p c j"))
-        copy(scalar, d_in[0][:, 512:896, :], r_rows[0][:, :, 512:896].rearrange("p j c -> p c j"))
+        copy(scalar, d_in[0][:, 0:512, :].rearrange("p (c i) j -> p c j i", i=4), r_rows[0][:, :, 0:512].rearrange("p j (c i) -> p c j i", i=4))
+        copy(scalar, d_in[0][:, 512:896, :].rearrange("p (c i) j -> p c j i", i=4), r_rows[0][:, :, 512:896].rearrange("p j (c i) -> p c j i", i=4))
         for j in range(4):
             om(1, j, 0)
             om(1, j, 1)
@@ -551,11 +551,12 @@ def tile_adversarialsdfconditionalpricingmoments_x2_kernel(
         sdf(1, 3, 4)
         for j in range(4):
             d_scale_rows(vector, 1, j)
-        copy(gpsimd, d_in[1][:, 0:448, :], r_rows[1][:, :, 0:448].rearrange("p j c -> p c j"))
+        copy(gpsimd, d_in[1][:, 0:256, :], r_rows[1][:, :, 0:256].rearrange("p j c -> p c j"))
         f_weigh_tile(vector, 0, 3)
         instrument(0, 4)
         instrument(0, 5)
-        copy(scalar, d_in[1][:, 448:512, :], r_rows[1][:, :, 448:512].rearrange("p j c -> p c j"))
+        copy(scalar, d_in[1][:, 256:512, :].rearrange("p (c i) j -> p c j i", i=4), r_rows[1][:, :, 256:512].rearrange("p j (c i) -> p c j i", i=4))
+        f_weigh_tile(gpsimd, 0, 4)
         for qt in range(4):
             wide_turn(1, qt)
         f_turn(0, 0)
@@ -572,7 +573,7 @@ def tile_adversarialsdfconditionalpricingmoments_x2_kernel(
         f_quantise_both(0)
         d_quantise(0, 1)
         d_interleave(gpsimd, 1, 2)
-        f_weigh(0, 2)
+        f_weigh_tile(vector, 0, 5)
         f_weigh(0, 3)
         for it in range(3):
             out(0, it)

@@ -58,8 +58,6 @@ def tile_adversarialsdfconditionalpricingmoments_x2_kernel(
         ones = kept("ones", [128, 128], BF16)
         u_all = psum.tile([128, 512], F32, name="u_all", tag="bank7")
         u_wide = kept("u_wide", [128, 512], F32)
-        zero = kept("zero", [128, 512], BF16)
-        warm = kept("warm", [128, 1], F32)
         eye = kept("eye", [128, 8], BF16)
         z_in = [[kept("zin%d%d" % (g, jp), [128, 2, 256, 4], BF16) for jp in range(2)] for g in range(2)]
         z_code = [[kept("zc%d%d" % (g, kg), [128, 512], U32) for kg in range(2)] for g in range(2)]
@@ -119,11 +117,6 @@ def tile_adversarialsdfconditionalpricingmoments_x2_kernel(
 
         def zero_scales(eng, name):
             eng.memset(w_scale[name][:].rearrange("p g n -> p (g n)").bitcast(I32), 0)
-
-        def warm_tensor(n):
-            for _ in range(n):
-                t = bank([128, 512])
-                nc.tensor.matmul(t[:], zero[:, 0:128], zero[:], start=True, stop=True)
 
         def spread_u():
             row = u_row[:].rearrange("r (c e b) -> r e c b", e=2, b=2)
@@ -455,7 +448,6 @@ def tile_adversarialsdfconditionalpricingmoments_x2_kernel(
                     out=out_2[:, 4 * c : 4 * c + 4, :].bitcast(I32), in_=p_scale[32 * c : 32 * c + 8, :].bitcast(I32)
                 )
 
-        vector.memset(zero[:].bitcast(U32), 0)
         zero_scales(vector, "o")
         vector.memset(u_row[:].bitcast(U32), 0)
         vector.memset(ident[:], 0.0)
@@ -485,14 +477,11 @@ def tile_adversarialsdfconditionalpricingmoments_x2_kernel(
         gpsimd.dma_start(out=bg_rows[0:8, :], in_=bg.rearrange("(a p) -> a p", p=128))
         gpsimd.dma_start(out=v_sb[:], in_=v.rearrange("(g p j) -> p g j", p=128, j=4))
         gpsimd.tensor_scalar(out=neg_v[:], in0=v_sb[:], scalar1=-1.0 / ROOT, scalar2=0.0, op0=MULT, op1=ADD)
-        scalar.activation(out=warm[:], in_=zero[:, 0:1], func=ACT.Tanh)
         scalar.copy(out=eye[:], in_=ident[:, 0:8])
-        warm_tensor(4)
         for j in range(2):
             z_turn(0, j)
             z_copy(0, j)
             z_quantise(0, j, j + 1)
-        warm_tensor(1)
         for j in range(2, 4):
             z_turn(0, j)
             z_copy(0, j)

from contextlib import ExitStack

import concourse.mybir as mybir
from concourse.masks import make_identity

F32 = mybir.dt.float32
BF16 = mybir.dt.bfloat16
U8 = mybir.dt.uint8
U32 = mybir.dt.uint32
I32 = mybir.dt.int32
E4M3 = mybir.dt.float8_e4m3fn_x4
E2M1 = mybir.dt.float4_e2m1fn_x4
ADD = mybir.AluOpType.add
MULT = mybir.AluOpType.mult
ACT = mybir.ActivationFunctionType

T, D, N, Q = 1024, 1024, 1024, 1024
ROOT = 32.0
TANH_BUFS = 8
WEIGHED_BUFS = 4
OUT_BUFS = 8
WIDE = ((1, 0), (1, 1), (1, 2), (1, 3))
FLOPS = 3 * 2 * 1024 * 1024 * 1024


def tile_adversarialsdfconditionalpricingmoments_x2_kernel(
    tc, z, wo_words, wo_scales, wg_words, wg_scales, bg, r, v, u, out_0, out_1, out_2
):
    nc = tc.nc
    scalar, vector, gpsimd = nc.scalar, nc.vector, nc.gpsimd
    with ExitStack() as ctx:
        keep = ctx.enter_context(tc.tile_pool(name="keep", bufs=1))
        work = ctx.enter_context(tc.tile_pool(name="work", bufs=4))
        psum = ctx.enter_context(tc.psum_pool(name="psum", bufs=1))
        ctx.enter_context(tc.manual_schedule())

        def kept(name, shape, dtype):
            return keep.tile(shape, dtype, name=name, align_bytes=64)

        ring = list(range(7))

        def bank(shape):
            ring.append(ring.pop(0))
            return psum.tile(shape, F32, name="bank", tag="bank%d" % ring[-1])

        ident = kept("ident", [128, 128], F32)
        z_rows = {}
        r_rows = [kept("r%d" % g, [128, 4, N], BF16) for g in range(2)]
        wo_sb = [kept("wo%d" % kg, [128, 2048], U8) for kg in range(2)]
        wg_sb = [kept("wg%d" % kg, [128, 2048], U8) for kg in range(2)]
        w_scale = {"o": kept("wso", [128, 2, N], U8), 0: kept("wsg0", [128, 2, 512], U8), 1: kept("wsg1", [128, 2, 512], U8)}
        bg_rows = kept("bg_rows", [128, 128], BF16)
        bg_cols = kept("bg_t", [128, 8], F32)
        v_sb = kept("v", [128, 2, 4], BF16)
        neg_v = kept("nv", [128, 2, 4], F32)
        u_sb = kept("u", [128, 4], BF16)
        u_row = kept("u_row", [128, 512], BF16)
        ones = kept("ones", [128, 128], BF16)
        u_all = psum.tile([128, 512], F32, name="u_all", tag="bank7")
        u_wide = kept("u_wide", [128, 512], F32)
        eye = kept("eye", [128, 8], BF16)
        z_in = [[kept("zin%d%d" % (g, jp), [128, 2, 256, 4], BF16) for jp in range(2)] for g in range(2)]
        z_code = [[kept("zc%d%d" % (g, kg), [128, 512], U32) for kg in range(2)] for g in range(2)]
        z_scale = [[kept("zs%d%d" % (g, kg), [128, 512], U8) for kg in range(2)] for g in range(2)]
        f_in = [kept("fin%d" % qh, [128, 2, 512, 4], BF16) for qh in range(2)]
        f_code = [kept("fc%d" % qh, [128, 2, 512], U32) for qh in range(2)]
        f_scale = [kept("fs%d" % qh, [128, 2, 512], U8) for qh in range(2)]
        d_in = [kept("din%d" % g, [128, N, 4], BF16) for g in range(2)]
        d_code = [kept("dc%d" % g, [128, N], U32) for g in range(2)]
        d_scale = [kept("ds%d" % g, [128, N], U8) for g in range(2)]
        sums = kept("acc", [128, 2, 4, 4], F32)
        neg_sdf = {}
        out_bf = [[kept("ob%d%d" % (qh, ip), [128, 2, 512], BF16) for ip in range(4)] for qh in range(2)]
        p_in = d_in
        p_code = [kept("pc%d" % qh, [128, N], U32) for qh in range(2)]
        p_scale = kept("ps", [128, N], U8)
        held = {}

        def copy(eng, dst, src):
            if eng is scalar:
                scalar.copy(out=dst, in_=src)
            elif eng is vector:
                vector.tensor_copy(out=dst, in_=src)
            else:
                gpsimd.tensor_scalar(out=dst, in0=src, scalar1=1.0, scalar2=0.0, op0=MULT, op1=ADD)

        def quantise(code, scale, src):
            vector.quantize_mx(out=code.bitcast(E4M3), scales=scale, in_=src.rearrange("p c k -> p (c k)"))

        def product(dst, passes):
            for n, (lhs, lhs_scale, rhs, rhs_scale) in enumerate(passes):
                nc.tensor.matmul_mx(
                    out=dst, lhsT=lhs, lhsT_scale=lhs_scale, rhs=rhs, rhs_scale=rhs_scale, start=n == 0, stop=n == 1
                )

        def by_slot(src, g):
            return src[512 * g : 512 * (g + 1), :].rearrange("(p j) d -> p j d", j=4)

        def load_z(g, j0, j1):
            t = kept("z%d%d" % (g, j0), [128, j1 - j0, 1024], BF16)
            nc.sync.dma_start(out=t[:], in_=by_slot(z, g)[:, j0:j1, :])
            for j in range(j0, j1):
                z_rows[g, j] = t[:, j - j0, :]

        def load_r(g, j0, j1):
            nc.sync.dma_start(out=r_rows[g][:, j0:j1, :], in_=by_slot(r, g)[:, j0:j1, :])

        def load_scales(queue, name, src):
            for c in range(4):
                queue.dma_start(
                    out=w_scale[name][c:128:32, :, :].bitcast(I32),
                    in_=src[:, c:16:4, :].rearrange("g q n -> q g n").bitcast(I32),
                )

        def load_words(tiles, src, kg):
            nc.sync.dma_start(out=tiles[kg][:].bitcast(I32), in_=src[kg].bitcast(I32))

        def zero_scales(eng, name):
            eng.memset(w_scale[name][:].rearrange("p g n -> p (g n)").bitcast(I32), 0)

        def spread_u():
            row = u_row[:].rearrange("r (c e b) -> r e c b", e=2, b=2)
            nc.tensor.matmul(u_all[:], ones[:], row, start=True, stop=True)

        def z_sort(g, j):
            t = work.tile([128, 2, 2, 128], U32, name="zsort", bufs=2)
            scalar.copy(out=t[:], in_=z_rows[g, j].bitcast(U32).rearrange("p (h c e) -> p h e c", h=2, e=2))
            held["sorted", g, j] = t

        def z_turn(g, j):
            t = bank([128, 2, 2, 128])
            words = z_rows[g, j].bitcast(F32)
            for kg in range(2):
                for e in range(2):
                    if ("sorted", g, j) in held:
                        src = held["sorted", g, j][:, kg, e, :].bitcast(F32)
                    else:
                        src = words[:, 256 * kg + e : 256 * (kg + 1) : 2]
                    nc.tensor.transpose(t[:, kg, e, :], src, ident[:])
            held["z", g, j] = t

        def z_copy(g, j):
            dst = z_in[g][j // 2][:].rearrange("p h c k -> p (h c k)").bitcast(F32)
            dst = dst.rearrange("p (h a c e) -> p h a c e", h=2, a=2, e=2)
            scalar.copy(out=dst[:, :, j % 2, :, :], in_=held["z", g, j][:].rearrange("p h e c -> p h c e"))

        def z_quantise(g, j0, j1, groups=(0, 1)):
            cols = slice(128 * j0, 128 * j1)
            for kg in groups:
                src = z_in[g][j0 // 2][:, kg, 128 * (j0 % 2) : 128 * (j0 % 2 + j1 - j0), :]
                quantise(z_code[g][kg][:, cols], z_scale[g][kg][:, cols], src)

        def om_pass(g, j, ih, kg):
            if kg == 0:
                held["om", g, j, ih] = bank([128, 512])
            cols = slice(128 * j, 128 * (j + 1))
            nc.tensor.matmul_mx(
                out=held["om", g, j, ih][:],
                lhsT=z_code[g][kg][:, cols].bitcast(E4M3),
                lhsT_scale=z_scale[g][kg][:, cols],
                rhs=wo_sb[kg][:, 1024 * ih : 1024 * (ih + 1)].bitcast(E2M1),
                rhs_scale=w_scale["o"][:, kg, 512 * ih : 512 * (ih + 1)],
                start=kg == 0,
                stop=kg == 1,
            )

        def om_product(g, j, ih):
            om_pass(g, j, ih, 0)
            om_pass(g, j, ih, 1)

        def om_sum(g, j, ih):
            prod = work.tile([128, 512], BF16, name="junk", bufs=8)
            vector.scalar_tensor_tensor(
                out=prod[:],
                in0=held["om", g, j, ih][:],
                scalar=1.0,
                in1=r_rows[g][:, j, 512 * ih : 512 * (ih + 1)],
                op0=MULT,
                op1=MULT,
                accum_out=sums[:, g, j, ih : ih + 1],
            )

        def om(g, j, ih):
            om_product(g, j, ih)
            om_sum(g, j, ih)

        def sdf(g, j0, j1, eng=vector):
            t = kept("sm%d%d" % (g, j0), [128, j1 - j0], F32)
            if eng is vector:
                vector.tensor_reduce(out=t[:], in_=sums[:, g, j0:j1, 0:3], op=ADD, axis=mybir.AxisListType.X)
            else:
                gpsimd.tensor_scalar(
                    out=t[:], in0=sums[:, g, j0, 0:1], scalar1=sums[:, g, j0, 1:2], scalar2=-ROOT, op0=ADD, op1=ADD
                )
            for j in range(j0, j1):
                neg_sdf[g, j] = t[:, j - j0 : j - j0 + 1]

        def d_scale_rows(eng, g, j):
            if eng is scalar:
                both = kept("both%d%d" % (g, j), [128, 1], F32)
                gpsimd.tensor_tensor(out=both[:], in0=neg_sdf[g, j], in1=neg_v[:, g, j : j + 1], op=MULT)
                scalar.mul(out=r_rows[g][:, j, :], in_=r_rows[g][:, j, :], mul=both[:])
                return
            eng.tensor_scalar(
                out=r_rows[g][:, j, :],
                in0=r_rows[g][:, j, :],
                scalar1=neg_sdf[g, j],
                scalar2=neg_v[:, g, j : j + 1],
                op0=MULT,
                op1=MULT,
            )

        def d_place(g, quarter):
            if g == 1 and quarter >= 2:
                return f_in[0][:, 1, 0:256, :]
            return d_in[g][:, 256 * quarter : 256 * (quarter + 1), :]

        def d_interleave(eng, g, quarter):
            cols = slice(256 * quarter, 256 * (quarter + 1))
            copy(eng, d_place(g, quarter), r_rows[g][:, :, cols].rearrange("p j c -> p c j"))

        def d_quantise_quarter(g, quarter):
            cols = slice(256 * quarter, 256 * (quarter + 1))
            quantise(d_code[g][:, cols], d_scale[g][:, cols], d_place(g, quarter))

        def d_quantise(g, ih):
            cols = slice(512 * ih, 512 * (ih + 1))
            quantise(d_code[g][:, cols], d_scale[g][:, cols], d_in[g][:, cols, :])

        def bias_columns():
            t = bank([128, 8])
            nc.tensor.matmul(t[:], bg_rows[:], eye[:], start=True, stop=True)
            scalar.copy(out=bg_cols[:], in_=t[:])

        def x_pass(g, qt, kg):
            if kg == 0:
                held["x", g, qt] = bank([128, 512])
            nc.tensor.matmul_mx(
                out=held["x", g, qt][:],
                lhsT=wg_sb[kg][:, 256 * qt : 256 * (qt + 1)].bitcast(E2M1),
                lhsT_scale=w_scale[qt // 4][:, kg, 128 * (qt % 4) : 128 * (qt % 4 + 1)],
                rhs=z_code[g][kg][:].bitcast(E4M3),
                rhs_scale=z_scale[g][kg][:],
                start=kg == 0,
                stop=kg == 1,
            )

        def x_product(g, qt):
            x_pass(g, qt, 0)
            x_pass(g, qt, 1)

        def x_tanh(g, qt):
            if qt % 2 == 0:
                held["tanh", g, qt // 2] = work.tile([128, 2, 512], F32, name="th", bufs=TANH_BUFS)
            order = "p e b c" if (g, qt // 2) in WIDE else "p e c b"
            scalar.activation(
                out=held["tanh", g, qt // 2][:, qt % 2, :].rearrange("p (%s) -> %s" % (order[2:], order), e=2, b=2),
                in_=held["x", g, qt][:].rearrange("p (e b c) -> %s" % order, e=2, b=2),
                func=ACT.Tanh,
                bias=bg_cols[:, qt : qt + 1],
            )

        def instrument(g, qt):
            x_product(g, qt)
            x_tanh(g, qt)

        def f_weigh(g, qq, eng=vector):
            t = work.tile([128, 2, 512], BF16, name="fw", bufs=WEIGHED_BUFS)
            factor = u_all if eng is vector else u_wide
            eng.tensor_tensor(
                out=t[:],
                in0=held["tanh", g, qq][:],
                in1=factor[:].unsqueeze(1).to_broadcast([128, 2, 512]),
                op=MULT,
            )
            held["weighed", g, qq] = t

        def f_weigh_tile(eng, g, qt):
            if qt % 2 == 0:
                held["weighed", g, qt // 2] = work.tile([128, 2, 512], BF16, name="fw", bufs=WEIGHED_BUFS)
            factor = u_all if eng is vector else u_wide
            eng.tensor_tensor(
                out=held["weighed", g, qt // 2][:, qt % 2, :], in0=held["tanh", g, qt // 2][:, qt % 2, :], in1=factor[:], op=MULT
            )

        def f_turn(g, qq):
            t = bank([128, 2, 256])
            for k in range(2):
                words = held["weighed", g, qq][:, k, :].bitcast(F32)
                for e in range(2):
                    nc.tensor.transpose(t[:, e, 128 * k : 128 * (k + 1)], words[:, 128 * e : 128 * (e + 1)], ident[:])
            held["f", g, qq] = t

        def f_copy(eng, g, qq):
            words = f_in[qq // 2][:, g, :, :].rearrange("p c k -> p (c k)").bitcast(F32)
            src = held["f", g, qq][:]
            dst = words.rearrange("p (c e) -> p c e", e=2)[:, 256 * (qq % 2) : 256 * (qq % 2 + 1), :]
            copy(eng, dst, src.rearrange("p e c -> p c e"))

        def wide_turn(g, qt):
            t = bank([128, 4, 128])
            for j in range(4):
                nc.tensor.transpose(t[:, j, :], held["tanh", g, qt // 2][:, qt % 2, 128 * j : 128 * (j + 1)], ident[:])
            held["wide", g, qt] = t

        def wide_weigh(g, qt):
            cols = f_in[qt // 4][:, g, :, :].rearrange("p %s j -> p m s j" % "(m s)", s=4)
            vector.tensor_tensor(
                out=cols[:, 32 * (qt % 4) : 32 * (qt % 4 + 1), :, :],
                in0=held["wide", g, qt][:].rearrange("p j (m s) -> p m s j", s=4),
                in1=u_sb[:].unsqueeze(1).unsqueeze(1).to_broadcast([128, 32, 4, 4]),
                op=MULT,
            )

        def f_quantise_both(qh):
            quantise(
                f_code[qh][:].rearrange("p g c -> p (g c)"),
                f_scale[qh][:].rearrange("p g c -> p (g c)"),
                f_in[qh][:].rearrange("p g c k -> p (g c) k"),
            )

        def f_quantise(g, qh, c0, c1):
            quantise(f_code[qh][:, g, c0:c1], f_scale[qh][:, g, c0:c1], f_in[qh][:, g, c0:c1, :])

        def d_operand(g, it):
            cols = slice(128 * it, 128 * (it + 1))
            return d_code[g][:, cols].bitcast(E4M3), d_scale[g][:, cols]

        def f_operand(g, qh, c0, c1):
            return f_code[qh][:, g, c0:c1].bitcast(E4M3), f_scale[qh][:, g, c0:c1]

        def quarter_product(qq, ip):
            t = bank([128, 2, 256])
            for k in range(2):
                product(
                    t[:, k, :],
                    [(*d_operand(g, 2 * ip + k), *f_operand(g, 0, 256 * qq, 256 * (qq + 1))) for g in range(2)],
                )
            held["outq", qq, ip] = t

        def quarter_store(qq, ip):
            t = work.tile([128, 2, 256], F32, name="osq", bufs=1)
            held["sbq", qq, ip] = t
            scalar.mul(out=t[:], in_=held["outq", qq, ip][:], mul=1.0 / ROOT)
            rows = out_0[256 * ip : 256 * (ip + 1), 256 * qq : 256 * (qq + 1)]
            nc.sync.dma_start(out=rows.rearrange("(k p) c -> p k c", p=128), in_=t[:])

        def quarter(qq, ip):
            quarter_product(qq, ip)
            quarter_store(qq, ip)

        def round_quarter(eng, qq, ip):
            dst = out_bf[0][ip][:].rearrange("p k (e a c b) -> p k e a c b", e=2, a=2, b=2)[:, :, :, qq, :, :]
            src = held["sbq", qq, ip][:].rearrange("p k (c e b) -> p k e c b", e=2, b=2)
            if eng is gpsimd:
                for k in range(2):
                    copy(eng, dst[:, k], src[:, k])
            else:
                copy(eng, dst, src)

        def out_product(qh, it):
            t = bank([128, 512])
            product(t[:], [(*d_operand(g, it), *f_operand(g, qh, 0, 512)) for g in ((0, 1), (1, 0))[qh]])
            held["out", qh, it] = t

        def out_pass(qh, it, g):
            if g == 0:
                held["out", qh, it] = bank([128, 512])
            lhs, lhs_scale = d_operand(g, it)
            rhs, rhs_scale = f_operand(g, qh, 0, 512)
            nc.tensor.matmul_mx(
                out=held["out", qh, it][:], lhsT=lhs, lhsT_scale=lhs_scale, rhs=rhs, rhs_scale=rhs_scale,
                start=g == 0, stop=g == 1,
            )

        def out_store(qh, it, eng=scalar):
            if it % 2 == 0:
                held["sb", qh, it // 2] = work.tile([128, 2, 512], F32, name="osb", bufs=OUT_BUFS)
            t = held["sb", qh, it // 2][:, it % 2, :]
            src = held["out", qh, it][:].rearrange("p %s -> p m s" % "(m s)", s=4)
            scaled(eng, t.rearrange("p (m s) -> p m s", s=4), src)
            if qh == 0:
                nc.sync.dma_start(out=out_0[128 * it : 128 * (it + 1), 0:512], in_=t)
            elif it % 2 == 1:
                rows = out_0[128 * (it - 1) : 128 * (it + 1), 512:1024].rearrange("(k p) c -> p k c", p=128)
                nc.sync.dma_start(out=rows, in_=held["sb", qh, it // 2][:])

        def scaled(eng, dst, src):
            if eng is scalar:
                scalar.mul(out=dst, in_=src, mul=1.0 / ROOT)
            else:
                vector.tensor_scalar(out=dst, in0=src, scalar1=1.0 / ROOT, scalar2=None, op0=MULT)

        def out(qh, it, eng=scalar):
            out_product(qh, it)
            out_store(qh, it, eng)

        def round_tile(eng, qh, it):
            dst = out_bf[qh][it // 2][:, it % 2, :].rearrange("p (e c b) -> p e c b", e=2, b=2)
            copy(eng, dst, held["sb", qh, it // 2][:, it % 2, :].rearrange("p (c e b) -> p e c b", e=2, b=2))

        def round_bank(qh, it):
            dst = out_bf[qh][it // 2][:, it % 2, :].rearrange("p (e c b) -> p e c b", e=2, b=2)
            scaled(vector, dst, held["out", qh, it][:].rearrange("p (c e b) -> p e c b", e=2, b=2))

        def round_pair(eng, qh, ip):
            dst = out_bf[qh][ip][:].rearrange("p k (e c b) -> p k e c b", e=2, b=2)
            src = held["sb", qh, ip][:].rearrange("p k (c e b) -> p k e c b", e=2, b=2)
            if eng is gpsimd:
                for k in range(2):
                    copy(eng, dst[:, k], src[:, k])
            else:
                copy(eng, dst, src)

        def plane_turn(qh, ip):
            t = bank([128, 2, 256])
            for k in range(2):
                words = out_bf[qh][ip][:, k, :].bitcast(F32)
                for e in range(2):
                    nc.tensor.transpose(t[:, e, 128 * k : 128 * (k + 1)], words[:, 128 * e : 128 * (e + 1)], ident[:])
            held["turned", qh, ip] = t

        def plane_copy(eng, qh, ip):
            dst = p_in[qh][:, 256 * ip : 256 * (ip + 1), :].rearrange("p c k -> p (c k)").bitcast(F32)
            copy(eng, dst.rearrange("p (c e) -> p c e", e=2), held["turned", qh, ip][:].rearrange("p e c -> p c e"))

        def plane_product(it):
            t = bank([128, 4, 128])
            for s in range(4):
                product(t[:, s, :], [(*f_operand(g, 1, 128 * s, 128 * (s + 1)), *d_operand(g, it)) for g in range(2)])
            held["direct", it] = t

        def plane_scale(eng, it):
            scaled(eng, p_in[1][:, 128 * it : 128 * (it + 1), :], held["direct", it][:].rearrange("p s c -> p c s"))

        def plane_quantise(qh, c0, c1):
            quantise(p_code[qh][:, c0:c1], p_scale[4 * qh : 128, c0:c1], p_in[qh][:, c0:c1, :])

        def plane_store(qh, c0, c1):
            nc.sync.dma_start(
                out=out_1[qh].rearrange("p m t -> p (m t)")[:, 4 * c0 : 4 * c1].bitcast(I32),
                in_=p_code[qh][:, c0:c1].bitcast(I32),
            )

        def plane_scales_store(queue=nc.sync):
            for c in range(4):
                queue.dma_start(
                    out=out_2[:, 4 * c : 4 * c + 4, :].bitcast(I32), in_=p_scale[32 * c : 32 * c + 8, :].bitcast(I32)
                )

        zero_scales(vector, "o")
        vector.memset(u_row[:].bitcast(U32), 0)
        vector.memset(ident[:], 0.0)
        make_identity(nc, ident[:], nomemset=True)
        vector.memset(ones[:], 1.0)
        vector.memset(sums[:, :, :, 2:3], -ROOT)
        vector.memset(bg_rows[:].bitcast(U32), 0)
        zero_scales(vector, 0)
        zero_scales(vector, 1)
        load_z(0, 0, 2)
        load_z(0, 2, 4)
        nc.sync.dma_start(out=u_row[0:1, :], in_=u[0:512].rearrange("(a t) -> a t", a=1))
        load_words(wo_sb, wo_words, 0)
        load_scales(scalar, "o", wo_scales)
        load_words(wo_sb, wo_words, 1)
        load_r(0, 0, 2)
        load_z(1, 0, 2)
        load_r(0, 2, 4)
        load_z(1, 2, 4)
        load_scales(nc.sync, 0, wg_scales[:, :, 0:512])
        load_words(wg_sb, wg_words, 0)
        load_words(wg_sb, wg_words, 1)
        load_r(1, 0, 2)
        load_r(1, 2, 4)
        load_scales(nc.sync, 1, wg_scales[:, :, 512:1024])
        nc.sync.dma_start(out=u_sb[:], in_=u[512:1024].rearrange("(p j) -> p j", j=4))
        gpsimd.dma_start(out=bg_rows[0:8, :], in_=bg.rearrange("(a p) -> a p", p=128))
        gpsimd.dma_start(out=v_sb[:], in_=v.rearrange("(g p j) -> p g j", p=128, j=4))
        gpsimd.tensor_scalar(out=neg_v[:], in0=v_sb[:], scalar1=-1.0 / ROOT, scalar2=0.0, op0=MULT, op1=ADD)
        scalar.copy(out=eye[:], in_=ident[:, 0:8])
        for j in range(2):
            z_turn(0, j)
            z_copy(0, j)
            z_quantise(0, j, j + 1)
        for j in range(2, 4):
            z_turn(0, j)
            z_copy(0, j)
        spread_u()
        z_quantise(0, 2, 3)
        z_quantise(0, 3, 4)
        for kg in range(2):
            om_pass(0, 0, 0, kg)
            om_pass(0, 0, 1, kg)
        om_sum(0, 0, 0)
        om_sum(0, 0, 1)
        om(0, 1, 0)
        om(0, 1, 1)
        scalar.copy(out=u_wide[:], in_=u_all[:])
        bias_columns()
        z_sort(1, 0)
        z_sort(1, 1)
        sdf(0, 0, 1, gpsimd)
        d_scale_rows(gpsimd, 0, 0)
        sdf(0, 1, 2, gpsimd)
        d_scale_rows(gpsimd, 0, 1)
        om(0, 2, 0)
        om(0, 2, 1)
        om_product(0, 3, 0)
        om_product(0, 3, 1)
        for j in range(4):
            z_turn(1, j)
            z_copy(1, j)
        om_sum(0, 3, 0)
        om_sum(0, 3, 1)
        z_quantise(1, 0, 2, (0,))
        sdf(0, 2, 4)
        z_quantise(1, 0, 2, (1,))
        d_scale_rows(vector, 0, 2)
        z_quantise(1, 2, 4)
        d_scale_rows(vector, 0, 3)
        for kg in range(2):
            for qt in range(2):
                x_pass(0, qt, kg)
        x_tanh(0, 0)
        x_tanh(0, 1)
        instrument(0, 2)
        copy(gpsimd, d_in[0][:, 896:1024, :], r_rows[0][:, :, 896:1024].rearrange("p j c -> p c j"))
        f_weigh(0, 0, gpsimd)
        f_weigh_tile(gpsimd, 0, 2)
        copy(scalar, d_in[0][:, 0:512, :].rearrange("p (c i) j -> p c j i", i=4), r_rows[0][:, :, 0:512].rearrange("p j (c i) -> p c j i", i=4))
        copy(scalar, d_in[0][:, 512:896, :].rearrange("p (c i) j -> p c j i", i=4), r_rows[0][:, :, 512:896].rearrange("p j (c i) -> p c j i", i=4))
        for j in range(4):
            om(1, j, 0)
            om(1, j, 1)
        instrument(0, 3)
        for qt in range(4):
            instrument(1, qt)
        sdf(1, 0, 3)
        d_quantise(0, 0)
        sdf(1, 3, 4)
        for j in range(4):
            d_scale_rows(vector, 1, j)
        copy(gpsimd, d_in[1][:, 0:256, :], r_rows[1][:, :, 0:256].rearrange("p j c -> p c j"))
        f_weigh_tile(vector, 0, 3)
        instrument(0, 4)
        instrument(0, 5)
        copy(scalar, d_in[1][:, 256:512, :].rearrange("p (c i) j -> p c j i", i=4), r_rows[1][:, :, 256:512].rearrange("p j (c i) -> p c j i", i=4))
        f_weigh_tile(gpsimd, 0, 4)
        for qt in range(4):
            wide_turn(1, qt)
        f_turn(0, 0)
        f_turn(0, 1)
        for qt in range(4):
            wide_weigh(1, qt)
        f_copy(scalar, 0, 0)
        f_copy(scalar, 0, 1)
        instrument(0, 6)
        instrument(0, 7)
        for qt in range(4, 8):
            instrument(1, qt)
        d_quantise(1, 0)
        f_quantise_both(0)
        d_quantise(0, 1)
        d_interleave(gpsimd, 1, 2)
        f_weigh_tile(vector, 0, 5)
        f_weigh(0, 3)
        for it in range(3):
            out(0, it)
        d_quantise_quarter(1, 2)
        d_interleave(gpsimd, 1, 3)
        wide_turn(1, 4)
        wide_turn(1, 5)
        f_turn(0, 2)
        wide_turn(1, 6)
        wide_turn(1, 7)
        ring.append(7)
        f_turn(0, 3)
        for qt in range(4, 8):
            wide_weigh(1, qt)
        f_copy(scalar, 0, 2)
        f_copy(scalar, 0, 3)
        d_quantise_quarter(1, 3)
        for it in range(3, 8):
            out(0, it)
        f_quantise(1, 1, 0, 512)
        f_quantise(0, 1, 0, 512)
        round_pair(vector, 0, 0)
        round_pair(vector, 0, 1)
        out(1, 0)
        round_pair(vector, 0, 2)
        out(1, 1)
        round_pair(vector, 0, 3)
        out(1, 2)
        round_pair(vector, 1, 0)
        out(1, 3)
        out(1, 4, vector)
        round_pair(vector, 1, 1)
        out(1, 5)
        out(1, 6)
        round_pair(vector, 1, 2)
        out(1, 7)
        round_tile(vector, 1, 6)
        for ip in range(4):
            plane_turn(0, ip)
        plane_copy(scalar, 0, 0)
        plane_copy(vector, 0, 1)
        round_tile(vector, 1, 7)
        plane_copy(scalar, 0, 2)
        plane_quantise(0, 0, 512)
        plane_store(0, 0, 512)
        plane_copy(scalar, 0, 3)
        for ip in range(4):
            plane_turn(1, ip)
        plane_copy(vector, 1, 0)
        plane_copy(scalar, 1, 1)
        plane_quantise(0, 512, 1024)
        plane_store(0, 512, 1024)
        plane_copy(scalar, 1, 2)
        plane_quantise(1, 0, 512)
        plane_store(1, 0, 512)
        plane_copy(scalar, 1, 3)
        plane_quantise(1, 512, 768)
        plane_quantise(1, 768, 1024)
        plane_store(1, 512, 1024)
        plane_scales_store(scalar)
